import numpy as np
import ml_dtypes


def mxq(x, axis, fmt="e4m3"):
    dtype, down = {"e4m3": (ml_dtypes.float8_e4m3fn, 7), "e5m2": (ml_dtypes.float8_e5m2, 14)}[fmt]
    v = np.moveaxis(np.asarray(x, np.float32).astype(ml_dtypes.bfloat16).astype(np.float64), axis, -1)
    blocks = v.reshape(v.shape[:-1] + (-1, 32))
    amax = np.abs(blocks).max(-1, keepdims=True)
    byte = np.maximum(np.where(amax > 0, np.frexp(amax)[1] - 1 + 127, 0) - down, 1)
    scale = np.exp2(byte - 127.0)
    codes = (blocks / scale).astype(np.float32).astype(dtype).astype(np.float64)
    return np.moveaxis((codes * scale).reshape(v.shape), -1, axis)


WIDE = False


def mx_kscale(k):
    if not WIDE:
        return np.ones(k)
    levels = np.array([10, -10, 5, -5, 0])
    if k % 512:
        return np.exp2(np.random.permutation(np.resize(levels, k // 32))).repeat(32)
    a = np.empty((k // 512, 16))
    for p in range(k // 512):
        a[p, :8] = np.random.permutation(np.resize(levels, 8))
        for g in range(8):
            far = levels[np.abs(levels - a[p, g]) >= 10]
            a[p, g + 8] = far[np.random.randint(len(far))]
    return np.exp2(a.ravel()).repeat(32)


BF16 = ml_dtypes.bfloat16


def bf(x):
    return np.asarray(x, np.float32).astype(BF16)


def f64(x):
    return np.asarray(x).astype(np.float64)


E2M1 = np.array([0.0, 0.5, 1.0, 1.5, 2.0, 3.0, 4.0, 6.0, -0.0, -0.5, -1.0, -1.5, -2.0, -3.0, -4.0, -6.0])


def pack_weight(w, fmt):
    k, n = w.shape
    w = f64(bf(w)).reshape(k // 32, 32, n)
    amax = np.abs(w).max(1)
    if fmt == "e4m3":
        byte = np.frexp(amax)[1] - 1 + 127 - 7
    else:
        mant, ex = np.frexp(amax / 6.0)
        byte = np.where(mant > 0.5, ex, ex - 1) + 127
    byte = np.clip(np.where(amax > 0, byte, 1), 1, 254)
    scaled = (w * np.exp2(127.0 - byte)[:, None, :]).reshape(k, n).astype(np.float32)
    by_word = np.ascontiguousarray(scaled.reshape(k // 512, 128, 4, n).transpose(0, 1, 3, 2))
    if fmt == "e4m3":
        words = by_word.astype(ml_dtypes.float8_e4m3fn).view(np.uint8)
    else:
        c = by_word.astype(ml_dtypes.float4_e2m1fn).view(np.uint8) & 0xF
        words = c[..., 0::2] | (c[..., 1::2] << 4)
    return np.ascontiguousarray(words), np.ascontiguousarray(byte.astype(np.uint8).reshape(k // 512, 16, n))


def unpack_weight(words, scales, fmt):
    g, p, n, _ = words.shape
    if fmt == "e4m3":
        vals = np.ascontiguousarray(words).view(ml_dtypes.float8_e4m3fn).astype(np.float64)
    else:
        nib = np.empty((g, p, n, 4), np.uint8)
        nib[..., 0::2] = words & 0xF
        nib[..., 1::2] = words >> 4
        vals = E2M1[nib]
    vals = vals * np.repeat(np.exp2(scales.astype(np.float64) - 127.0), 8, axis=1)[..., None]
    return vals.transpose(0, 1, 3, 2).reshape(g * 512, n)
def pack4(w):
    words, scales = pack_weight(w, "e2m1")
    return words.reshape(words.shape[0], 128, -1), scales


def unpack4(words, scales):
    return unpack_weight(words.reshape(words.shape[0], 128, -1, 2), scales, "e2m1")


H, J, D, K, C = 2048, 1024, 512, 1024, 512

USTD = 0.5
LSTD = 0.3


def draw0():
    s1, s2, s3 = mx_kscale(D), mx_kscale(K), mx_kscale(H)
    z = np.random.standard_normal((H, D)) * s1
    w = USTD * np.random.standard_normal((D, J)) / np.sqrt(D) / s1[:, None]
    x = np.random.standard_normal((H, K)) * s2
    v = USTD * np.random.standard_normal((K, J)) / np.sqrt(K) / s2[:, None]
    a = np.exp(LSTD * np.random.standard_normal(H)) * s3
    y = np.random.standard_normal((H, C)) / np.sqrt(H) / s3[:, None]
    size = np.exp(LSTD * np.random.standard_normal(J))
    v_words, v_scales = pack4(v)
    y_words, y_scales = pack4(y)
    return {"z": bf(z), "w": bf(w), "x": bf(x),
            "v_words": v_words, "v_scales": v_scales,
            "a": bf(a), "size": bf(size),
            "y_words": y_words, "y_scales": y_scales}


def core(z, w, x, v_words, v_scales, a, size, y_words, y_scales):
    travel = mxq(f64(z), 1, "e4m3") @ mxq(f64(w), 0, "e4m3")
    taste = mxq(f64(x), 1, "e4m3") @ unpack4(v_words, v_scales)
    patronage = np.exp(travel + taste) * f64(a)[:, None]
    flows = mxq(patronage, 0, "e4m3").T @ unpack4(y_words, y_scales)
    return flows * f64(size)[:, None]


def e4m3fn_bytes(y):
    return np.clip(np.asarray(y, np.float64), -448.0, 448.0).astype(np.float32).astype(ml_dtypes.float8_e4m3fn).view(np.uint8)


def e4m3fn_values(b):
    return np.asarray(b, np.uint8).view(ml_dtypes.float8_e4m3fn).astype(np.float64)


def setup_inputs():
    d = draw0()
    x0 = np.asarray(d['x']).astype(np.float64)
    s = (np.max(np.abs(x0), axis=(0,), keepdims=True) / 448.0).astype(np.float32)
    out = {}
    for k, v in d.items():
        if k == 'x':
            out['x_bytes'] = e4m3fn_bytes(x0 / s.astype(np.float64))
            out['x_scale'] = s
        else:
            out[k] = v
    return out


def reference(z, w, x_bytes, x_scale, v_words, v_scales, a, size, y_words, y_scales):
    return core(z, w, e4m3fn_values(x_bytes) * x_scale.astype(np.float64), v_words, v_scales, a, size, y_words, y_scales)

@@ -1,0 +1,400 @@
+from contextlib import ExitStack
+
+import concourse.mybir as mybir
+from concourse.masks import make_identity
+
+H, J, D, K, C = 2048, 1024, 512, 1024, 512
+FLOPS = 2 * H * J * (D + K) + 2 * J * C * H
+
+F32 = mybir.dt.float32
+BF16 = mybir.dt.bfloat16
+U32 = mybir.dt.uint32
+I32 = mybir.dt.int32
+U8 = mybir.dt.uint8
+FP8 = mybir.dt.float8_e4m3fn
+FP8X4 = mybir.dt.float8_e4m3fn_x4
+FP4X4 = mybir.dt.float4_e2m1fn_x4
+ACT = mybir.ActivationFunctionType
+ALU = mybir.AluOpType
+
+P = 128
+G = H // 512
+NT = 4 * G
+HALF = J // 2
+
+
+def tile_huff_retail_flows_s3_kernel(
+    tc, z, w, x_bytes, x_scale, v_words, v_scales, a, size, y_words, y_scales, out
+):
+    nc = tc.nc
+    with ExitStack() as ctx:
+        keep = ctx.enter_context(tc.tile_pool(name="keep", bufs=1))
+        work = ctx.enter_context(tc.tile_pool(name="work", bufs=2))
+        psum = ctx.enter_context(tc.psum_pool(name="psum", bufs=1))
+        ctx.enter_context(tc.manual_schedule())
+
+        def kept(name, shape, dtype):
+            return keep.tile(shape, dtype, name=name, tag=name, align_bytes=64)
+
+        def bank():
+            return psum.tile([P, 512], F32, name="bank", tag="bank", bufs=8)
+
+        ident = kept("ident", [P, P], F32)
+        warm = kept("warm", [P, 1], F32)
+        ones = kept("ones", [P, 512], BF16)
+        warm_out = kept("warm_out", [P, 1], F32)
+        a_in = kept("a_in", [P, G, 4], BF16)
+        ln_a = kept("ln_a", [P, NT], F32)
+        xs_cols = kept("xs_cols", [P, 8], F32)
+        xs_wide = kept("xs_wide", [P, K], F32)
+        size_rows = kept("size_rows", [P, P], BF16)
+        size_rows32 = kept("size_rows32", [P, P], F32)
+        size_cols = kept("size_cols", [P, 8], F32)
+        v_sb = kept("v_sb", [P, 2, 2 * J], U8)
+        v_sc = kept("v_sc", [P, 2 * J], U8)
+        y_sb = kept("y_sb", [P, G, 2 * C], U8)
+        y_sc = kept("y_sc", [P, G * C], U8)
+        w_raw = kept("w_raw", [P, 4, J], BF16)
+        w_grp = [kept("w_grp%d" % h, [P, HALF, 4], BF16) for h in range(2)]
+        w_q = [kept("w_q%d" % h, [P, HALF], U32) for h in range(2)]
+        w_s = [kept("w_s%d" % h, [P, HALF], U8) for h in range(2)]
+        z_raw = [kept("z_raw%d" % g, [P, 4, D], BF16) for g in range(G)]
+        z_q = [kept("z_q%d" % n, [P, 256], U32) for n in range(2 * G)]
+        z_s = [kept("z_s%d" % n, [P, 256], U8) for n in range(2 * G)]
+        x_raw = [kept("x_raw%d" % g, [P, 4 * K], U8) for g in range(G)]
+        x_q = [kept("x_q%d" % i, [P, 2, P], U32) for i in range(NT)]
+        x_s = [kept("x_s%d" % i, [P, 2, P], U8) for i in range(NT)]
+        p_q = [[kept("p_q%d_%d" % (g, h), [P, HALF], U32) for h in range(2)] for g in range(G)]
+        p_s = [[kept("p_s%d_%d" % (g, h), [P, HALF], U8) for h in range(2)] for g in range(G)]
+        z_grp = {}
+        x_bf = {}
+        x_grp = {}
+        p_raw = {}
+        p_grp = {}
+
+        nc.scalar.dma_start(out=a_in[:], in_=a.rearrange("(g p t) -> p g t", p=P, t=4))
+        nc.sync.dma_start(out=xs_cols[:], in_=x_scale.rearrange("o (p c) -> p (o c)", c=8))
+
+        def load_w():
+            nc.sync.dma_start(out=w_raw[:], in_=w.rearrange("(p t) j -> p t j", t=4))
+
+        def load_z(g, t0, t1):
+            src = z[512 * g : 512 * (g + 1), :].rearrange("(p t) k -> p t k", t=4)
+            nc.sync.dma_start(out=z_raw[g][:, t0:t1, :], in_=src[:, t0:t1, :])
+
+        def load_x(g, t0, t1):
+            src = x_bytes[512 * g : 512 * (g + 1), :].rearrange("(p t) k -> p (t k)", t=4)
+            nc.sync.dma_start(out=x_raw[g][:, t0 * K : t1 * K], in_=src[:, t0 * K : t1 * K])
+
+        def load_v():
+            nc.sync.dma_start(out=v_sb[:], in_=v_words.rearrange("g p n -> p g n"))
+
+        def load_scales(tile, src, groups):
+            for r in range(4):
+                nc.sync.dma_start(
+                    out=tile[r:P:32, :].bitcast(I32).rearrange("q (g n) -> q g n", g=groups),
+                    in_=src.bitcast(I32).rearrange("g (q r) n -> r q g n", r=4)[r],
+                )
+
+        nc.vector.memset(v_sc[:].bitcast(I32), 0)
+        nc.vector.memset(warm[:], 1.0)
+        nc.vector.memset(y_sc[:].bitcast(I32), 0)
+        nc.gpsimd.memset(size_rows[:], 0.0)
+        nc.gpsimd.memset(ones[:], 1.0)
+        make_identity(nc, ident[:])
+        nc.scalar.dma_start(out=size_rows[0:8, :], in_=size.rearrange("(c p) -> c p", p=P))
+
+        load_x(0, 0, 2)
+        load_z(0, 0, 2)
+        load_w()
+        load_x(0, 2, 4)
+        load_z(0, 2, 4)
+        load_z(1, 0, 2)
+        load_z(1, 2, 4)
+        load_scales(v_sc, v_scales, 2)
+        load_v()
+        load_x(1, 0, 2)
+        load_x(1, 2, 4)
+        for g in range(2, G):
+            load_z(g, 0, 4)
+            load_x(g, 0, 4)
+        load_scales(y_sc, y_scales, G)
+        nc.sync.dma_start(out=y_sb[:], in_=y_words.rearrange("g p n -> p g n"))
+
+        def widen(i):
+            x_bf[i] = work.tile([P, K], BF16, name="x_bf", tag="x_bf", bufs=8, align_bytes=64)
+            t = i % 4
+            nc.vector.tensor_tensor(
+                out=x_bf[i][:],
+                in0=x_raw[i // 4][:, t * K : (t + 1) * K].bitcast(FP8),
+                in1=xs_wide[:],
+                op=ALU.mult,
+            )
+
+        def turn_x(i):
+            b = bank()
+            words = x_bf[i][:].bitcast(F32)
+            for kg in range(2):
+                for u in range(2):
+                    c = 2 * kg + u
+                    nc.tensor.transpose(
+                        b[:, c * P : (c + 1) * P], words[:, 256 * kg + u : 256 * (kg + 1) : 2], ident[:]
+                    )
+            return b
+
+        def copy_out(engine, dst, src):
+            if engine == "s":
+                nc.scalar.copy(out=dst, in_=src)
+            else:
+                nc.vector.tensor_copy(out=dst, in_=src)
+
+        def empty_x(i, b, engine):
+            x_grp[i] = work.tile([P, 8 * P], BF16, name="x_grp", tag="x_grp", bufs=6, align_bytes=64)
+            dst = x_grp[i][:].bitcast(F32).rearrange("p (k h u) -> p k h u", k=2, u=2)
+            copy_out(engine, dst, b[:].rearrange("p (k u h) -> p k h u", k=2, u=2))
+
+        def quant_x(i):
+            nc.vector.quantize_mx(
+                out=x_q[i][:].rearrange("p k h -> p (k h)").bitcast(FP8X4),
+                scales=x_s[i][:].rearrange("p k h -> p (k h)"),
+                in_=x_grp[i][:],
+            )
+
+        def turn_z(n):
+            b = bank()
+            g, half = divmod(n, 2)
+            for j in range(2):
+                for u in range(2):
+                    c = 2 * j + u
+                    if n in z_split:
+                        words = z_split[n][:].bitcast(F32)[:, c * P : (c + 1) * P]
+                    else:
+                        words = z_raw[g][:, 2 * half + j, :].bitcast(F32)[:, u:256:2]
+                    nc.tensor.transpose(b[:, c * P : (c + 1) * P], words, ident[:])
+            return b
+
+        z_split = {}
+
+        def split_z(n):
+            g, half = divmod(n, 2)
+            z_split[n] = work.tile([P, 2 * D], BF16, name="z_split", tag="z_split", bufs=2, align_bytes=64)
+            nc.scalar.copy(
+                out=z_split[n][:].bitcast(F32).rearrange("p (t u w) -> p t u w", t=2, u=2),
+                in_=z_raw[g][:, 2 * half : 2 * half + 2, :].bitcast(F32).rearrange("p t (w u) -> p t u w", u=2),
+            )
+
+        def empty_z(n, b, engine):
+            z_grp[n] = work.tile([P, 8 * P], BF16, name="z_grp", tag="z_grp", bufs=4, align_bytes=64)
+            dst = z_grp[n][:].bitcast(F32).rearrange("p (t h u) -> p t h u", t=2, u=2)
+            copy_out(engine, dst, b[:].rearrange("p (t u h) -> p t h u", t=2, u=2))
+
+        def quant_z(n):
+            nc.vector.quantize_mx(out=z_q[n][:].bitcast(FP8X4), scales=z_s[n][:], in_=z_grp[n][:])
+
+        def group4(engine, dst, src):
+            copy_out(
+                engine, dst.rearrange("p (c i) t -> p c t i", i=4), src.rearrange("p t (c i) -> p c t i", i=4)
+            )
+
+        def quant_w(h):
+            nc.vector.quantize_mx(
+                out=w_q[h][:].bitcast(FP8X4), scales=w_s[h][:], in_=w_grp[h][:].rearrange("p n t -> p (n t)")
+            )
+
+        u_bank = {}
+
+        def u_pass(i, h, which):
+            if which == 0:
+                u_bank[i, h] = bank()
+            n, t = divmod(i, 2)
+            cols = slice(t * P, (t + 1) * P)
+            if which == 0:
+                lhs, lsc = z_q[n][:, cols].bitcast(FP8X4), z_s[n][:, cols]
+                rhs, rsc = w_q[h][:].bitcast(FP8X4), w_s[h][:]
+            else:
+                kg = which - 1
+                lhs, lsc = x_q[i][:, kg, :].bitcast(FP8X4), x_s[i][:, kg, :]
+                rhs = v_sb[:, kg, 2 * HALF * h : 2 * HALF * (h + 1)].bitcast(FP4X4)
+                rsc = v_sc[:, J * kg + HALF * h : J * kg + HALF * (h + 1)]
+            nc.tensor.matmul_mx(
+                out=u_bank[i, h][:], lhsT=lhs, lhsT_scale=lsc, rhs=rhs, rhs_scale=rsc,
+                start=(which == 0), stop=(which == 2),
+            )
+
+        def u_group(i, h):
+            for which in range(3):
+                u_pass(i, h, which)
+
+        def attract(i, h):
+            g, t = divmod(i, 4)
+            if t == 0:
+                p_raw[g, h] = work.tile([P, 4, HALF], BF16, name="p_raw", tag="p_raw", bufs=6, align_bytes=64)
+            nc.scalar.activation(
+                out=p_raw[g, h][:, t, :], in_=u_bank[i, h][:], func=ACT.Exp, bias=ln_a[:, i : i + 1], scale=1.0
+            )
+
+        def group_p(g, h):
+            p_grp[g, h] = work.tile([P, HALF, 4], BF16, name="p_grp", tag="p_grp", bufs=2, align_bytes=64)
+            group4("v", p_grp[g, h][:], p_raw[g, h][:])
+
+        def quant_p(g, h):
+            nc.vector.quantize_mx(
+                out=p_q[g][h][:].bitcast(FP8X4), scales=p_s[g][h][:],
+                in_=p_grp[g, h][:].rearrange("p n t -> p (n t)"),
+            )
+
+        f_bank = {}
+
+        def f_pass(jt, g):
+            if g == 0:
+                f_bank[jt] = bank()
+            h, c = divmod(jt, 4)
+            cols = slice(c * P, (c + 1) * P)
+            nc.tensor.matmul_mx(
+                out=f_bank[jt][:],
+                lhsT=p_q[g][h][:, cols].bitcast(FP8X4), lhsT_scale=p_s[g][h][:, cols],
+                rhs=y_sb[:, g, :].bitcast(FP4X4), rhs_scale=y_sc[:, C * g : C * (g + 1)],
+                start=(g == 0), stop=(g == G - 1),
+            )
+
+        def finish(jt, split_store):
+            o = work.tile([P, C], F32, name="o_sb", tag="o_sb", bufs=8, align_bytes=64)
+            f = f_bank[jt]
+            rows = out[jt * P : (jt + 1) * P, :]
+            half = C // 2
+            nc.scalar.activation(out=o[:, 0:half], in_=f[:, 0:half], func=ACT.Copy, scale=size_cols[:, jt : jt + 1])
+            if split_store:
+                nc.sync.dma_start(out=rows[:, 0:half], in_=o[:, 0:half])
+            nc.vector.tensor_scalar(
+                out=o[:, half:C], in0=f[:, half:C], scalar1=size_cols[:, jt : jt + 1], scalar2=None, op0=ALU.mult
+            )
+            if split_store:
+                nc.sync.dma_start(out=rows[:, half:C], in_=o[:, half:C])
+            else:
+                nc.sync.dma_start(out=rows, in_=o[:])
+
+        nc.scalar.activation(out=warm_out[:], in_=warm[:], func=ACT.Ln)
+        def keep_warm(count):
+            b = bank()
+            for k in range(count):
+                nc.tensor.matmul(out=b[:], lhsT=ones[:, 0:P], rhs=ones[:], start=True, stop=True)
+
+        keep_warm(2)
+        sc_banks = [bank(), bank()]
+        for c in range(8):
+            nc.tensor.transpose(
+                sc_banks[c // 4][:, (c % 4) * P : (c % 4 + 1) * P],
+                xs_cols[:, c : c + 1].to_broadcast([P, P]),
+                ident[:],
+            )
+        for i in range(2):
+            copy_out(
+                "vs"[i],
+                xs_wide[:].rearrange("p (n c) -> p n c", c=8)[:, :, 4 * i : 4 * i + 4],
+                sc_banks[i][:].rearrange("p (c n) -> p n c", c=4),
+            )
+
+        nc.scalar.activation(out=ln_a[:], in_=a_in[:].rearrange("p g t -> p (g t)"), func=ACT.Ln)
+        nc.scalar.activation(out=warm_out[:], in_=warm[:], func=ACT.Exp)
+
+        def w_part(engine, h, c0, c1):
+            group4(engine, w_grp[h][:, c0:c1, :], w_raw[:, :, h * HALF + c0 : h * HALF + c1])
+
+        zb = {}
+        xb = {}
+        widen(0)
+        widen(1)
+        widen(2)
+        w_part("v", 0, 0, 256)
+        widen(3)
+        for n in range(4):
+            if n < 2:
+                keep_warm(2 if n == 0 else 4)
+            zb[n] = turn_z(n)
+            if n == 0:
+                keep_warm(2)
+            xb[n] = turn_x(n)
+            if n == 2:
+                w_part("s", 1, 256, 512)
+            empty_z(n, zb[n], "s")
+            if n == 0:
+                w_part("s", 0, 256, 512)
+                w_part("s", 1, 0, 256)
+            empty_x(n, xb[n], "s")
+        quant_w(0)
+        quant_z(0)
+        quant_x(0)
+        quant_x(1)
+        quant_w(1)
+        widen(4)
+        widen(5)
+        quant_z(1)
+        quant_x(2)
+        quant_x(3)
+        keep_warm(1)
+        for h in range(2):
+            u_pass(0, h, 0)
+            u_pass(1, h, 0)
+            for i in range(2):
+                u_pass(i, h, 1)
+                u_pass(i, h, 2)
+                attract(i, h)
+
+        p_work = {2:["I00"],3:["I01","Q00"],4:["I10","Q01"],5:["I11","Q10"],6:["Q11","I20","I21","Q20"],7:["Q21"]}
+
+        def do_p(work_list):
+            for it in work_list:
+                (group_p if it[0] == "I" else quant_p)(int(it[1]), int(it[2]))
+
+        order = {n: [(2 * n, 0), (2 * n, 1), (2 * n + 1, 0), (2 * n + 1, 1)] for n in range(8)}
+        order[0] = []
+        order[6] = [(12, 0), (13, 0), (12, 1)]
+        order[7] = [(14, 0), (15, 0), (13, 1), (14, 1), (15, 1)]
+        for n in range(8):
+            if 1 <= n <= 6:
+                quant_z(n + 1)
+                quant_x(2 * n + 2)
+                quant_x(2 * n + 3)
+            for m, grp in enumerate(order[n]):
+                u_group(*grp)
+                attract(*grp)
+                if m == 0 and n + 4 < 8:
+                    split_z(n + 4)
+                if n == 7 and m == 1:
+                    group_p(3, 0)
+            xx, zz = n + 2, n + 4
+            if xx < 8:
+                bx0 = turn_x(2 * xx)
+                bx1 = turn_x(2 * xx + 1)
+                empty_x(2 * xx, bx0, "s")
+                empty_x(2 * xx + 1, bx1, "s")
+                if zz < 8:
+                    bz = turn_z(zz)
+                    empty_z(zz, bz, "s")
+                if xx == 7:
+                    size_bank = bank()
+                    nc.tensor.transpose(size_bank[:, 0:P], size_rows32[:], ident[:])
+                for i in (2 * xx + 2, 2 * xx + 3):
+                    if i < NT:
+                        widen(i)
+            if n == 3:
+                nc.scalar.copy(out=size_rows32[:], in_=size_rows[:])
+            if n == 6:
+                nc.vector.tensor_copy(out=size_cols[:], in_=size_bank[:, 0:8])
+            do_p(p_work.get(n, []))
+
+        for jt in range(3):
+            for g in range(3):
+                f_pass(jt, g)
+        quant_p(3, 0)
+        group_p(3, 1)
+        for g in range(3):
+            f_pass(3, g)
+        quant_p(3, 1)
+        for jt in range(4):
+            f_pass(jt, 3)
+            finish(jt, False)
+        for jt in range(4, 8):
+            for g in range(4):
+                f_pass(jt, g)
+            finish(jt, jt == 7)

@@ -20,7 +20,9 @@ ALU = mybir.AluOpType
 P = 128
 G = H // 512
 NT = 4 * G
+PAIRS = NT // 2
 HALF = J // 2
+Z_SPLIT_FROM = 3
 
 
 def tile_huff_retail_flows_s3_kernel(
@@ -36,206 +38,200 @@ def tile_huff_retail_flows_s3_kernel(
         def kept(name, shape, dtype):
             return keep.tile(shape, dtype, name=name, tag=name, align_bytes=64)
 
+        def rotating(name, shape, dtype, bufs):
+            return work.tile(shape, dtype, name=name, tag=name, bufs=bufs, align_bytes=64)
+
         def bank():
             return psum.tile([P, 512], F32, name="bank", tag="bank", bufs=8)
 
         ident = kept("ident", [P, P], F32)
-        warm = kept("warm", [P, 1], F32)
-        ones = kept("ones", [P, 512], BF16)
-        warm_out = kept("warm_out", [P, 1], F32)
         a_in = kept("a_in", [P, G, 4], BF16)
         ln_a = kept("ln_a", [P, NT], F32)
-        xs_cols = kept("xs_cols", [P, 8], F32)
-        xs_wide = kept("xs_wide", [P, K], F32)
-        size_rows = kept("size_rows", [P, P], BF16)
-        size_rows32 = kept("size_rows32", [P, P], F32)
+        xs_cols = kept("xs_cols", [P, 2, 4], F32)
+        unit = kept("unit", [P, 1], F32)
+        size_in = kept("size_in", [P, 8, 2], BF16)
         size_cols = kept("size_cols", [P, 8], F32)
-        v_sb = kept("v_sb", [P, 2, 2 * J], U8)
+        v_sb = [kept("v_sb%d" % h, [P, 2, 2 * HALF], U8) for h in range(2)]
         v_sc = kept("v_sc", [P, 2 * J], U8)
         y_sb = kept("y_sb", [P, G, 2 * C], U8)
         y_sc = kept("y_sc", [P, G * C], U8)
-        w_raw = kept("w_raw", [P, 4, J], BF16)
+        w_raw = [kept("w_raw%d" % h, [P, 4, HALF], BF16) for h in range(2)]
         w_grp = [kept("w_grp%d" % h, [P, HALF, 4], BF16) for h in range(2)]
         w_q = [kept("w_q%d" % h, [P, HALF], U32) for h in range(2)]
         w_s = [kept("w_s%d" % h, [P, HALF], U8) for h in range(2)]
-        z_raw = [kept("z_raw%d" % g, [P, 4, D], BF16) for g in range(G)]
-        z_q = [kept("z_q%d" % n, [P, 256], U32) for n in range(2 * G)]
-        z_s = [kept("z_s%d" % n, [P, 256], U8) for n in range(2 * G)]
-        x_raw = [kept("x_raw%d" % g, [P, 4 * K], U8) for g in range(G)]
+        z_raw = [kept("z_raw%d" % n, [P, 2 * D], BF16) for n in range(PAIRS)]
+        z_q = [kept("z_q%d" % n, [P, 256], U32) for n in range(PAIRS)]
+        z_s = [kept("z_s%d" % n, [P, 256], U8) for n in range(PAIRS)]
+        x_raw = [kept("x_raw%d" % n, [P, 2 * K], U8) for n in range(PAIRS)]
         x_q = [kept("x_q%d" % i, [P, 2, P], U32) for i in range(NT)]
         x_s = [kept("x_s%d" % i, [P, 2, P], U8) for i in range(NT)]
         p_q = [[kept("p_q%d_%d" % (g, h), [P, HALF], U32) for h in range(2)] for g in range(G)]
         p_s = [[kept("p_s%d_%d" % (g, h), [P, HALF], U8) for h in range(2)] for g in range(G)]
-        z_grp = {}
-        x_bf = {}
-        x_grp = {}
-        p_raw = {}
-        p_grp = {}
+        x_bf, x_split, x_bank, x_grp = {}, {}, {}, {}
+        z_split, z_bank, z_grp = {}, {}, {}
+        u_bank, p_raw, p_grp, f_bank = {}, {}, {}, {}
 
-        nc.scalar.dma_start(out=a_in[:], in_=a.rearrange("(g p t) -> p g t", p=P, t=4))
-        nc.sync.dma_start(out=xs_cols[:], in_=x_scale.rearrange("o (p c) -> p (o c)", c=8))
+        def load_w(h):
+            nc.sync.dma_start(out=w_raw[h][:], in_=w.rearrange("(p t) j -> p t j", t=4)[:, :, h * HALF : (h + 1) * HALF])
 
-        def load_w():
-            nc.sync.dma_start(out=w_raw[:], in_=w.rearrange("(p t) j -> p t j", t=4))
+        def load_v(h):
+            nc.sync.dma_start(
+                out=v_sb[h][:], in_=v_words.rearrange("g p n -> p g n")[:, :, 2 * HALF * h : 2 * HALF * (h + 1)]
+            )
 
-        def load_z(g, t0, t1):
-            src = z[512 * g : 512 * (g + 1), :].rearrange("(p t) k -> p t k", t=4)
-            nc.sync.dma_start(out=z_raw[g][:, t0:t1, :], in_=src[:, t0:t1, :])
+        def load_z(n):
+            g, half = divmod(n, 2)
+            src = z[512 * g : 512 * (g + 1), :].rearrange("(p t) k -> p (t k)", t=4)
+            nc.sync.dma_start(out=z_raw[n][:], in_=src[:, 2 * half * D : 2 * (half + 1) * D])
 
-        def load_x(g, t0, t1):
+        def load_x(n):
+            g, half = divmod(n, 2)
             src = x_bytes[512 * g : 512 * (g + 1), :].rearrange("(p t) k -> p (t k)", t=4)
-            nc.sync.dma_start(out=x_raw[g][:, t0 * K : t1 * K], in_=src[:, t0 * K : t1 * K])
+            nc.sync.dma_start(out=x_raw[n][:], in_=src[:, 2 * half * K : 2 * (half + 1) * K])
 
-        def load_v():
-            nc.sync.dma_start(out=v_sb[:], in_=v_words.rearrange("g p n -> p g n"))
-
-        def load_scales(tile, src, groups):
+        def load_scales(queue, tile, src, groups):
             for r in range(4):
-                nc.sync.dma_start(
+                queue.dma_start(
                     out=tile[r:P:32, :].bitcast(I32).rearrange("q (g n) -> q g n", g=groups),
                     in_=src.bitcast(I32).rearrange("g (q r) n -> r q g n", r=4)[r],
                 )
 
-        nc.vector.memset(v_sc[:].bitcast(I32), 0)
-        nc.vector.memset(warm[:], 1.0)
-        nc.vector.memset(y_sc[:].bitcast(I32), 0)
-        nc.gpsimd.memset(size_rows[:], 0.0)
-        nc.gpsimd.memset(ones[:], 1.0)
-        make_identity(nc, ident[:])
-        nc.scalar.dma_start(out=size_rows[0:8, :], in_=size.rearrange("(c p) -> c p", p=P))
-
-        load_x(0, 0, 2)
-        load_z(0, 0, 2)
-        load_w()
-        load_x(0, 2, 4)
-        load_z(0, 2, 4)
-        load_z(1, 0, 2)
-        load_z(1, 2, 4)
-        load_scales(v_sc, v_scales, 2)
-        load_v()
-        load_x(1, 0, 2)
-        load_x(1, 2, 4)
-        for g in range(2, G):
-            load_z(g, 0, 4)
-            load_x(g, 0, 4)
-        load_scales(y_sc, y_scales, G)
-        nc.sync.dma_start(out=y_sb[:], in_=y_words.rearrange("g p n -> p g n"))
-
-        def widen(i):
-            x_bf[i] = work.tile([P, K], BF16, name="x_bf", tag="x_bf", bufs=8, align_bytes=64)
-            t = i % 4
-            nc.vector.tensor_tensor(
-                out=x_bf[i][:],
-                in0=x_raw[i // 4][:, t * K : (t + 1) * K].bitcast(FP8),
-                in1=xs_wide[:],
-                op=ALU.mult,
-            )
-
-        def turn_x(i):
-            b = bank()
-            words = x_bf[i][:].bitcast(F32)
-            for kg in range(2):
-                for u in range(2):
-                    c = 2 * kg + u
-                    nc.tensor.transpose(
-                        b[:, c * P : (c + 1) * P], words[:, 256 * kg + u : 256 * (kg + 1) : 2], ident[:]
-                    )
-            return b
-
-        def copy_out(engine, dst, src):
+        def copy(engine, dst, src):
             if engine == "s":
                 nc.scalar.copy(out=dst, in_=src)
             else:
                 nc.vector.tensor_copy(out=dst, in_=src)
 
-        def empty_x(i, b, engine):
-            x_grp[i] = work.tile([P, 8 * P], BF16, name="x_grp", tag="x_grp", bufs=6, align_bytes=64)
-            dst = x_grp[i][:].bitcast(F32).rearrange("p (k h u) -> p k h u", k=2, u=2)
-            copy_out(engine, dst, b[:].rearrange("p (k u h) -> p k h u", k=2, u=2))
-
-        def quant_x(i):
-            nc.vector.quantize_mx(
-                out=x_q[i][:].rearrange("p k h -> p (k h)").bitcast(FP8X4),
-                scales=x_s[i][:].rearrange("p k h -> p (k h)"),
-                in_=x_grp[i][:],
+        def widen(i):
+            x_split[i] = rotating("x_split", [P, K], BF16, 6)
+            nc.vector.tensor_scalar(
+                out=x_split[i][:].rearrange("p (u m e) -> p m u e", u=2, e=2),
+                in0=x_raw[i // 2][:, (i % 2) * K : (i % 2 + 1) * K].bitcast(FP8).rearrange("p (m u e) -> p m u e", u=2, e=2),
+                scalar1=unit[:], scalar2=None, op0=ALU.mult,
             )
 
-        def turn_z(n):
-            b = bank()
-            g, half = divmod(n, 2)
-            for j in range(2):
-                for u in range(2):
-                    c = 2 * j + u
-                    if n in z_split:
-                        words = z_split[n][:].bitcast(F32)[:, c * P : (c + 1) * P]
-                    else:
-                        words = z_raw[g][:, 2 * half + j, :].bitcast(F32)[:, u:256:2]
-                    nc.tensor.transpose(b[:, c * P : (c + 1) * P], words, ident[:])
-            return b
-
-        z_split = {}
+        def split_words(engine, name, src):
+            dst = rotating(name, [P, K], BF16, 4)
+            copy(
+                engine,
+                dst[:].bitcast(F32).rearrange("p (c u m) -> p c u m", c=2, u=2),
+                src[:].bitcast(F32).rearrange("p (c m u) -> p c u m", c=2, u=2),
+            )
+            return dst
 
         def split_z(n):
-            g, half = divmod(n, 2)
-            z_split[n] = work.tile([P, 2 * D], BF16, name="z_split", tag="z_split", bufs=2, align_bytes=64)
-            nc.scalar.copy(
-                out=z_split[n][:].bitcast(F32).rearrange("p (t u w) -> p t u w", t=2, u=2),
-                in_=z_raw[g][:, 2 * half : 2 * half + 2, :].bitcast(F32).rearrange("p t (w u) -> p t u w", u=2),
-            )
+            if n >= Z_SPLIT_FROM:
+                z_split[n] = split_words("s", "z_split", z_raw[n])
 
-        def empty_z(n, b, engine):
-            z_grp[n] = work.tile([P, 8 * P], BF16, name="z_grp", tag="z_grp", bufs=4, align_bytes=64)
-            dst = z_grp[n][:].bitcast(F32).rearrange("p (t h u) -> p t h u", t=2, u=2)
-            copy_out(engine, dst, b[:].rearrange("p (t u h) -> p t h u", t=2, u=2))
+        def turn(plain, split):
+            b = bank()
+            for c in range(2):
+                for u in range(2):
+                    m = 2 * c + u
+                    if split is not None:
+                        words = split[:].bitcast(F32)[:, m * P : (m + 1) * P]
+                    else:
+                        words = plain[:].bitcast(F32)[:, 256 * c + u : 256 * (c + 1) : 2]
+                    nc.tensor.transpose(b[:, m * P : (m + 1) * P], words, ident[:])
+            return b
+
+        def turn_x(i):
+            x_bank[i] = bank()
+            words = x_split[i][:].bitcast(F32)
+            for kg in range(2):
+                for u in range(2):
+                    m = 2 * kg + u
+                    nc.tensor.transpose(
+                        x_bank[i][:, m * P : (m + 1) * P], words[:, (2 * u + kg) * P : (2 * u + kg + 1) * P], ident[:]
+                    )
+
+        def turn_z(n):
+            z_bank[n] = turn(z_raw[n], z_split.get(n))
+
+        def empty(engine, name, b):
+            grp = rotating(name, [P, K], BF16, 4)
+            copy(
+                engine,
+                grp[:].bitcast(F32).rearrange("p (c h u) -> p c h u", c=2, u=2),
+                b[:].rearrange("p (c u h) -> p c h u", c=2, u=2),
+            )
+            return grp
+
+        def empty_x(i):
+            x_grp[i] = rotating("x_grp", [P, K], BF16, 4)
+            for kg in range(2):
+                nc.vector.tensor_tensor(
+                    out=x_grp[i][:, 512 * kg : 512 * (kg + 1)].rearrange("p (h u e) -> p h u e", u=2, e=2),
+                    in0=x_bank[i][:, 256 * kg : 256 * (kg + 1)].bitcast(BF16).rearrange("p (u h e) -> p h u e", u=2, e=2),
+                    in1=xs_cols[:, kg, :].rearrange("p (o u e) -> p o u e", o=1, u=2).to_broadcast([P, P, 2, 2]),
+                    op=ALU.mult,
+                )
+
+        def empty_z(n):
+            z_grp[n] = empty("s", "z_grp", z_bank[n])
+
+        def quant_x(i, groups=slice(0, 2)):
+            nc.vector.quantize_mx(
+                out=x_q[i][:, groups, :].rearrange("p k h -> p (k h)").bitcast(FP8X4),
+                scales=x_s[i][:, groups, :].rearrange("p k h -> p (k h)"),
+                in_=x_grp[i][:, 512 * groups.start : 512 * groups.stop],
+            )
 
         def quant_z(n):
             nc.vector.quantize_mx(out=z_q[n][:].bitcast(FP8X4), scales=z_s[n][:], in_=z_grp[n][:])
 
         def group4(engine, dst, src):
-            copy_out(
-                engine, dst.rearrange("p (c i) t -> p c t i", i=4), src.rearrange("p t (c i) -> p c t i", i=4)
-            )
+            copy(engine, dst.rearrange("p (c i) t -> p c t i", i=4), src.rearrange("p t (c i) -> p c t i", i=4))
+
+        def group_w(engine, h, c0, c1):
+            group4(engine, w_grp[h][:, c0:c1, :], w_raw[h][:, :, c0:c1])
 
         def quant_w(h):
             nc.vector.quantize_mx(
                 out=w_q[h][:].bitcast(FP8X4), scales=w_s[h][:], in_=w_grp[h][:].rearrange("p n t -> p (n t)")
             )
 
-        u_bank = {}
-
-        def u_pass(i, h, which):
-            if which == 0:
+        def taste(i, h, first):
+            if first:
                 u_bank[i, h] = bank()
-            n, t = divmod(i, 2)
-            cols = slice(t * P, (t + 1) * P)
-            if which == 0:
-                lhs, lsc = z_q[n][:, cols].bitcast(FP8X4), z_s[n][:, cols]
-                rhs, rsc = w_q[h][:].bitcast(FP8X4), w_s[h][:]
-            else:
-                kg = which - 1
-                lhs, lsc = x_q[i][:, kg, :].bitcast(FP8X4), x_s[i][:, kg, :]
-                rhs = v_sb[:, kg, 2 * HALF * h : 2 * HALF * (h + 1)].bitcast(FP4X4)
-                rsc = v_sc[:, J * kg + HALF * h : J * kg + HALF * (h + 1)]
-            nc.tensor.matmul_mx(
-                out=u_bank[i, h][:], lhsT=lhs, lhsT_scale=lsc, rhs=rhs, rhs_scale=rsc,
-                start=(which == 0), stop=(which == 2),
-            )
+            for kg in range(2):
+                nc.tensor.matmul_mx(
+                    out=u_bank[i, h][:],
+                    lhsT=x_q[i][:, kg, :].bitcast(FP8X4), lhsT_scale=x_s[i][:, kg, :],
+                    rhs=v_sb[h][:, kg, :].bitcast(FP4X4),
+                    rhs_scale=v_sc[:, J * kg + HALF * h : J * kg + HALF * (h + 1)],
+                    start=(first and kg == 0), stop=(not first and kg == 1),
+                )
 
-        def u_group(i, h):
-            for which in range(3):
-                u_pass(i, h, which)
+        def travel(i, h, first):
+            if first:
+                u_bank[i, h] = bank()
+            cols = slice((i % 2) * P, (i % 2 + 1) * P)
+            nc.tensor.matmul_mx(
+                out=u_bank[i, h][:],
+                lhsT=z_q[i // 2][:, cols].bitcast(FP8X4), lhsT_scale=z_s[i // 2][:, cols],
+                rhs=w_q[h][:].bitcast(FP8X4), rhs_scale=w_s[h][:],
+                start=first, stop=not first,
+            )
 
         def attract(i, h):
             g, t = divmod(i, 4)
             if t == 0:
-                p_raw[g, h] = work.tile([P, 4, HALF], BF16, name="p_raw", tag="p_raw", bufs=6, align_bytes=64)
+                p_raw[g, h] = rotating("p_raw", [P, 4, HALF], BF16, 6)
             nc.scalar.activation(
                 out=p_raw[g, h][:, t, :], in_=u_bank[i, h][:], func=ACT.Exp, bias=ln_a[:, i : i + 1], scale=1.0
             )
 
-        def group_p(g, h):
-            p_grp[g, h] = work.tile([P, HALF, 4], BF16, name="p_grp", tag="p_grp", bufs=2, align_bytes=64)
-            group4("v", p_grp[g, h][:], p_raw[g, h][:])
+        def utility(i, h):
+            taste(i, h, True)
+            travel(i, h, False)
+            attract(i, h)
+
+        def group_p(g, h, engine="v", part=0, parts=1):
+            if part == 0:
+                p_grp[g, h] = rotating("p_grp", [P, HALF, 4], BF16, 5)
+            cols = slice(part * HALF // parts, (part + 1) * HALF // parts)
+            group4(engine, p_grp[g, h][:, cols, :], p_raw[g, h][:, :, cols])
 
         def quant_p(g, h):
             nc.vector.quantize_mx(
@@ -243,158 +239,188 @@ def tile_huff_retail_flows_s3_kernel(
                 in_=p_grp[g, h][:].rearrange("p n t -> p (n t)"),
             )
 
-        f_bank = {}
-
-        def f_pass(jt, g):
-            if g == 0:
-                f_bank[jt] = bank()
+        def flow_passes(jt, groups):
             h, c = divmod(jt, 4)
             cols = slice(c * P, (c + 1) * P)
-            nc.tensor.matmul_mx(
-                out=f_bank[jt][:],
-                lhsT=p_q[g][h][:, cols].bitcast(FP8X4), lhsT_scale=p_s[g][h][:, cols],
-                rhs=y_sb[:, g, :].bitcast(FP4X4), rhs_scale=y_sc[:, C * g : C * (g + 1)],
-                start=(g == 0), stop=(g == G - 1),
-            )
+            for g in groups:
+                if g == 0:
+                    f_bank[jt] = bank()
+                nc.tensor.matmul_mx(
+                    out=f_bank[jt][:],
+                    lhsT=p_q[g][h][:, cols].bitcast(FP8X4), lhsT_scale=p_s[g][h][:, cols],
+                    rhs=y_sb[:, g, :].bitcast(FP4X4), rhs_scale=y_sc[:, C * g : C * (g + 1)],
+                    start=(g == 0), stop=(g == G - 1),
+                )
 
-        def finish(jt, split_store):
-            o = work.tile([P, C], F32, name="o_sb", tag="o_sb", bufs=8, align_bytes=64)
-            f = f_bank[jt]
+        def finish(jt, engine, parts=1):
+            o = rotating("o_sb", [P, C], F32, 6)
             rows = out[jt * P : (jt + 1) * P, :]
-            half = C // 2
-            nc.scalar.activation(out=o[:, 0:half], in_=f[:, 0:half], func=ACT.Copy, scale=size_cols[:, jt : jt + 1])
-            if split_store:
-                nc.sync.dma_start(out=rows[:, 0:half], in_=o[:, 0:half])
-            nc.vector.tensor_scalar(
-                out=o[:, half:C], in0=f[:, half:C], scalar1=size_cols[:, jt : jt + 1], scalar2=None, op0=ALU.mult
-            )
-            if split_store:
-                nc.sync.dma_start(out=rows[:, half:C], in_=o[:, half:C])
-            else:
-                nc.sync.dma_start(out=rows, in_=o[:])
+            factor = size_cols[:, jt : jt + 1]
+            for part in range(parts):
+                cols = slice(part * C // parts, (part + 1) * C // parts)
+                if engine == "s":
+                    nc.scalar.activation(out=o[:, cols], in_=f_bank[jt][:, cols], func=ACT.Copy, scale=factor)
+                else:
+                    nc.vector.tensor_scalar(
+                        out=o[:, cols], in0=f_bank[jt][:, cols], scalar1=factor, scalar2=None, op0=ALU.mult
+                    )
+                nc.sync.dma_start(out=rows[:, cols], in_=o[:, cols])
 
-        nc.scalar.activation(out=warm_out[:], in_=warm[:], func=ACT.Ln)
-        def keep_warm(count):
-            b = bank()
-            for k in range(count):
-                nc.tensor.matmul(out=b[:], lhsT=ones[:, 0:P], rhs=ones[:], start=True, stop=True)
 
-        keep_warm(2)
-        sc_banks = [bank(), bank()]
-        for c in range(8):
-            nc.tensor.transpose(
-                sc_banks[c // 4][:, (c % 4) * P : (c % 4 + 1) * P],
-                xs_cols[:, c : c + 1].to_broadcast([P, P]),
-                ident[:],
-            )
-        for i in range(2):
-            copy_out(
-                "vs"[i],
-                xs_wide[:].rearrange("p (n c) -> p n c", c=8)[:, :, 4 * i : 4 * i + 4],
-                sc_banks[i][:].rearrange("p (c n) -> p n c", c=4),
-            )
+        nc.vector.memset(v_sc[:].bitcast(I32), 0)
+        nc.vector.memset(y_sc[:].bitcast(I32), 0)
+        nc.vector.memset(unit[:], 1.0)
+        make_identity(nc, ident[:])
+        load_x(0)
+        nc.scalar.dma_start(out=a_in[:], in_=a.rearrange("(g p t) -> p g t", p=P, t=4))
+        nc.sync.dma_start(out=xs_cols[:], in_=x_scale.rearrange("o (g p t) -> p (o g) t", g=2, t=4))
+        load_w(0)
+        load_z(0)
+        load_scales(nc.sync, v_sc, v_scales, 2)
+        load_v(0)
+        load_v(1)
+        load_x(1)
+        load_w(1)
+        load_x(2)
+        load_z(1)
+        for n in range(3, PAIRS):
+            load_x(n)
+            load_z(n - 1)
+        load_z(PAIRS - 1)
+        load_scales(nc.sync, y_sc, y_scales, G)
+        nc.sync.dma_start(out=y_sb[:], in_=y_words.rearrange("g p n -> p g n"))
+        with nc.allow_non_contiguous_dma(reason="one factor a partition for each tile of 128 stores"):
+            nc.sync.dma_start(out=size_in[:, :, 0], in_=size.rearrange("(c p) -> p c", p=P))
 
+        lo, hi = slice(0, 1), slice(1, 2)
         nc.scalar.activation(out=ln_a[:], in_=a_in[:].rearrange("p g t -> p (g t)"), func=ACT.Ln)
-        nc.scalar.activation(out=warm_out[:], in_=warm[:], func=ACT.Exp)
-
-        def w_part(engine, h, c0, c1):
-            group4(engine, w_grp[h][:, c0:c1, :], w_raw[:, :, h * HALF + c0 : h * HALF + c1])
-
-        zb = {}
-        xb = {}
         widen(0)
         widen(1)
-        widen(2)
-        w_part("v", 0, 0, 256)
-        widen(3)
-        for n in range(4):
-            if n < 2:
-                keep_warm(2 if n == 0 else 4)
-            zb[n] = turn_z(n)
-            if n == 0:
-                keep_warm(2)
-            xb[n] = turn_x(n)
-            if n == 2:
-                w_part("s", 1, 256, 512)
-            empty_z(n, zb[n], "s")
-            if n == 0:
-                w_part("s", 0, 256, 512)
-                w_part("s", 1, 0, 256)
-            empty_x(n, xb[n], "s")
+        turn_x(0)
+        turn_x(1)
+        turn_z(0)
+        group_w("s", 0, 0, 384)
+        empty_z(0)
+        group_w("s", 1, 0, 256)
+        empty_x(0)
+        quant_x(0, lo)
+        group_w("v", 0, 384, 512)
+        quant_x(0, hi)
+        empty_x(1)
         quant_w(0)
-        quant_z(0)
-        quant_x(0)
         quant_x(1)
+        quant_z(0)
+        widen(2)
+        widen(3)
+        group_w("v", 1, 256, 512)
+        taste(0, 0, True)
+        taste(0, 1, True)
+        taste(1, 0, True)
+        travel(0, 0, False)
+        travel(1, 0, False)
+        attract(0, 0)
+        attract(1, 0)
+        turn_x(2)
+        turn_x(3)
+        taste(1, 1, True)
+        turn_z(1)
+        empty_z(1)
+        empty_x(2)
+        quant_x(2, lo)
+        quant_x(2, hi)
         quant_w(1)
         widen(4)
-        widen(5)
         quant_z(1)
-        quant_x(2)
+        empty_x(3)
+        widen(5)
         quant_x(3)
-        keep_warm(1)
-        for h in range(2):
-            u_pass(0, h, 0)
-            u_pass(1, h, 0)
-            for i in range(2):
-                u_pass(i, h, 1)
-                u_pass(i, h, 2)
-                attract(i, h)
+        taste(2, 0, True)
+        taste(2, 1, True)
+        travel(0, 1, False)
+        travel(1, 1, False)
+        attract(0, 1)
+        attract(1, 1)
+        travel(2, 0, False)
+        travel(2, 1, False)
+        turn_x(4)
+        turn_z(2)
+        turn_x(5)
+        attract(2, 0)
+        empty_z(2)
+        attract(2, 1)
+        empty_x(4)
+        quant_x(4, lo)
+        quant_z(2)
+        quant_x(4, hi)
+        widen(6)
+        empty_x(5)
+        widen(7)
+        quant_x(5)
+        utility(3, 0)
+        split_z(3)
+        utility(3, 1)
+        split_z(4)
 
-        p_work = {2:["I00"],3:["I01","Q00"],4:["I10","Q01"],5:["I11","Q10"],6:["Q11","I20","I21","Q20"],7:["Q21"]}
-
-        def do_p(work_list):
-            for it in work_list:
-                (group_p if it[0] == "I" else quant_p)(int(it[1]), int(it[2]))
-
-        order = {n: [(2 * n, 0), (2 * n, 1), (2 * n + 1, 0), (2 * n + 1, 1)] for n in range(8)}
-        order[0] = []
-        order[6] = [(12, 0), (13, 0), (12, 1)]
-        order[7] = [(14, 0), (15, 0), (13, 1), (14, 1), (15, 1)]
-        for n in range(8):
-            if 1 <= n <= 6:
+        for n in range(2, 7):
+            utility(2 * n, 0)
+            group_p((n - 2) // 2, 0, "s", 2 * (n % 2), 4)
+            utility(2 * n, 1)
+            turn_x(2 * n + 2)
+            if n == 2:
+                turn_z(3)
+                empty_z(3)
+            if n < 6:
+                turn_z(n + 2)
+            turn_x(2 * n + 3)
+            empty_x(2 * n + 2)
+            quant_x(2 * n + 2, lo)
+            if n > 2:
                 quant_z(n + 1)
-                quant_x(2 * n + 2)
-                quant_x(2 * n + 3)
-            for m, grp in enumerate(order[n]):
-                u_group(*grp)
-                attract(*grp)
-                if m == 0 and n + 4 < 8:
-                    split_z(n + 4)
-                if n == 7 and m == 1:
-                    group_p(3, 0)
-            xx, zz = n + 2, n + 4
-            if xx < 8:
-                bx0 = turn_x(2 * xx)
-                bx1 = turn_x(2 * xx + 1)
-                empty_x(2 * xx, bx0, "s")
-                empty_x(2 * xx + 1, bx1, "s")
-                if zz < 8:
-                    bz = turn_z(zz)
-                    empty_z(zz, bz, "s")
-                if xx == 7:
-                    size_bank = bank()
-                    nc.tensor.transpose(size_bank[:, 0:P], size_rows32[:], ident[:])
-                for i in (2 * xx + 2, 2 * xx + 3):
-                    if i < NT:
-                        widen(i)
-            if n == 3:
-                nc.scalar.copy(out=size_rows32[:], in_=size_rows[:])
-            if n == 6:
-                nc.vector.tensor_copy(out=size_cols[:], in_=size_bank[:, 0:8])
-            do_p(p_work.get(n, []))
-
-        for jt in range(3):
-            for g in range(3):
-                f_pass(jt, g)
+            quant_x(2 * n + 2, hi)
+            if n < 6:
+                empty_z(n + 2)
+                widen(2 * n + 4)
+            if n == 2:
+                quant_z(n + 1)
+            empty_x(2 * n + 3)
+            if n < 6:
+                widen(2 * n + 5)
+            else:
+                quant_p(0, 0)
+            quant_x(2 * n + 3)
+            utility(2 * n + 1, 0)
+            if n < 5:
+                split_z(n + 3)
+            group_p((n - 2) // 2, 0, "s", 2 * (n % 2) + 1, 4)
+            utility(2 * n + 1, 1)
+        nc.vector.tensor_copy(out=size_cols[:], in_=size_in[:, :, 0])
+        group_p(0, 1)
+        quant_p(1, 0)
+        utility(14, 0)
+        group_p(2, 0, "s", 2, 4)
+        utility(14, 1)
+        group_p(2, 0, "s", 3, 4)
+        utility(15, 0)
+        utility(15, 1)
+        quant_p(2, 0)
+        group_p(3, 0)
+        group_p(2, 1, "s")
+        quant_p(0, 1)
         quant_p(3, 0)
+        group_p(1, 1)
+        quant_p(2, 1)
         group_p(3, 1)
-        for g in range(3):
-            f_pass(3, g)
+        quant_p(1, 1)
         quant_p(3, 1)
-        for jt in range(4):
-            f_pass(jt, 3)
-            finish(jt, False)
-        for jt in range(4, 8):
-            for g in range(4):
-                f_pass(jt, g)
-            finish(jt, jt == 7)
+        for g in range(G):
+            for jt in range(4):
+                flow_passes(jt, [g])
+                if g == G - 1:
+                    finish(jt, "s")
+        for g in (0, 2, 1, 3):
+            for jt in range(4, 7):
+                flow_passes(jt, [g])
+                if g == G - 1:
+                    finish(jt, "vsv"[jt - 4])
+        flow_passes(7, range(G))
+        finish(7, "s", 2)

@@ -22,7 +22,7 @@ G = H // 512
 NT = 4 * G
 PAIRS = NT // 2
 HALF = J // 2
-Z_SPLIT_FROM = 3
+WARM = 2
 
 
 def tile_huff_retail_flows_s3_kernel(
@@ -48,8 +48,10 @@ def tile_huff_retail_flows_s3_kernel(
         a_in = kept("a_in", [P, G, 4], BF16)
         ln_a = kept("ln_a", [P, NT], F32)
         xs_cols = kept("xs_cols", [P, 2, 4], F32)
-        unit = kept("unit", [P, 1], F32)
+        xs_wide = kept("xs_wide", [P, K], F32)
         size_in = kept("size_in", [P, 8, 2], BF16)
+        warm = kept("warm", [P, 1], F32)
+        ones = kept("ones", [P, 512], BF16)
         size_cols = kept("size_cols", [P, 8], F32)
         v_sb = [kept("v_sb%d" % h, [P, 2, 2 * HALF], U8) for h in range(2)]
         v_sc = kept("v_sc", [P, 2 * J], U8)
@@ -103,11 +105,12 @@ def tile_huff_retail_flows_s3_kernel(
                 nc.vector.tensor_copy(out=dst, in_=src)
 
         def widen(i):
-            x_split[i] = rotating("x_split", [P, K], BF16, 6)
-            nc.vector.tensor_scalar(
-                out=x_split[i][:].rearrange("p (u m e) -> p m u e", u=2, e=2),
-                in0=x_raw[i // 2][:, (i % 2) * K : (i % 2 + 1) * K].bitcast(FP8).rearrange("p (m u e) -> p m u e", u=2, e=2),
-                scalar1=unit[:], scalar2=None, op0=ALU.mult,
+            x_bf[i] = rotating("x_bf", [P, K], BF16, 6)
+            nc.vector.tensor_tensor(
+                out=x_bf[i][:],
+                in0=x_raw[i // 2][:, (i % 2) * K : (i % 2 + 1) * K].bitcast(FP8),
+                in1=xs_wide[:],
+                op=ALU.mult,
             )
 
         def split_words(engine, name, src):
@@ -119,9 +122,11 @@ def tile_huff_retail_flows_s3_kernel(
             )
             return dst
 
+        def split_x(i):
+            x_split[i] = split_words("v", "x_split", x_bf[i])
+
         def split_z(n):
-            if n >= Z_SPLIT_FROM:
-                z_split[n] = split_words("s", "z_split", z_raw[n])
+            z_split[n] = split_words("s", "z_split", z_raw[n])
 
         def turn(plain, split):
             b = bank()
@@ -136,14 +141,7 @@ def tile_huff_retail_flows_s3_kernel(
             return b
 
         def turn_x(i):
-            x_bank[i] = bank()
-            words = x_split[i][:].bitcast(F32)
-            for kg in range(2):
-                for u in range(2):
-                    m = 2 * kg + u
-                    nc.tensor.transpose(
-                        x_bank[i][:, m * P : (m + 1) * P], words[:, (2 * u + kg) * P : (2 * u + kg + 1) * P], ident[:]
-                    )
+            x_bank[i] = turn(x_bf[i], x_split.get(i))
 
         def turn_z(n):
             z_bank[n] = turn(z_raw[n], z_split.get(n))
@@ -158,23 +156,16 @@ def tile_huff_retail_flows_s3_kernel(
             return grp
 
         def empty_x(i):
-            x_grp[i] = rotating("x_grp", [P, K], BF16, 4)
-            for kg in range(2):
-                nc.vector.tensor_tensor(
-                    out=x_grp[i][:, 512 * kg : 512 * (kg + 1)].rearrange("p (h u e) -> p h u e", u=2, e=2),
-                    in0=x_bank[i][:, 256 * kg : 256 * (kg + 1)].bitcast(BF16).rearrange("p (u h e) -> p h u e", u=2, e=2),
-                    in1=xs_cols[:, kg, :].rearrange("p (o u e) -> p o u e", o=1, u=2).to_broadcast([P, P, 2, 2]),
-                    op=ALU.mult,
-                )
+            x_grp[i] = empty("s", "x_grp", x_bank[i])
 
         def empty_z(n):
             z_grp[n] = empty("s", "z_grp", z_bank[n])
 
-        def quant_x(i, groups=slice(0, 2)):
+        def quant_x(i):
             nc.vector.quantize_mx(
-                out=x_q[i][:, groups, :].rearrange("p k h -> p (k h)").bitcast(FP8X4),
-                scales=x_s[i][:, groups, :].rearrange("p k h -> p (k h)"),
-                in_=x_grp[i][:, 512 * groups.start : 512 * groups.stop],
+                out=x_q[i][:].rearrange("p k h -> p (k h)").bitcast(FP8X4),
+                scales=x_s[i][:].rearrange("p k h -> p (k h)"),
+                in_=x_grp[i][:],
             )
 
         def quant_z(n):
@@ -229,7 +220,7 @@ def tile_huff_retail_flows_s3_kernel(
 
         def group_p(g, h, engine="v", part=0, parts=1):
             if part == 0:
-                p_grp[g, h] = rotating("p_grp", [P, HALF, 4], BF16, 5)
+                p_grp[g, h] = rotating("p_grp", [P, HALF, 4], BF16, 4)
             cols = slice(part * HALF // parts, (part + 1) * HALF // parts)
             group4(engine, p_grp[g, h][:, cols, :], p_raw[g, h][:, :, cols])
 
@@ -266,161 +257,174 @@ def tile_huff_retail_flows_s3_kernel(
                     )
                 nc.sync.dma_start(out=rows[:, cols], in_=o[:, cols])
 
+        def keep_warm(count):
+            b = bank()
+            for k in range(count):
+                nc.tensor.matmul(out=b[:], lhsT=ones[:, 0:P], rhs=ones[:], start=True, stop=True)
+
+        def spread_scales(kg, engine):
+            b = bank()
+            for t in range(4):
+                nc.tensor.transpose(
+                    b[:, t * P : (t + 1) * P], xs_cols[:, kg, t : t + 1].to_broadcast([P, P]), ident[:]
+                )
+            copy(
+                engine,
+                xs_wide[:, 512 * kg : 512 * (kg + 1)].rearrange("p (m t) -> p m t", t=4),
+                b[:].rearrange("p (t m) -> p m t", t=4),
+            )
 
         nc.vector.memset(v_sc[:].bitcast(I32), 0)
         nc.vector.memset(y_sc[:].bitcast(I32), 0)
-        nc.vector.memset(unit[:], 1.0)
+        nc.vector.memset(warm[:], 1.0)
         make_identity(nc, ident[:])
-        load_x(0)
-        nc.scalar.dma_start(out=a_in[:], in_=a.rearrange("(g p t) -> p g t", p=P, t=4))
+        nc.gpsimd.memset(ones[:], 1.0)
         nc.sync.dma_start(out=xs_cols[:], in_=x_scale.rearrange("o (g p t) -> p (o g) t", g=2, t=4))
+        nc.scalar.dma_start(out=a_in[:], in_=a.rearrange("(g p t) -> p g t", p=P, t=4))
+        load_x(0)
         load_w(0)
         load_z(0)
+        load_x(1)
+        load_z(1)
         load_scales(nc.sync, v_sc, v_scales, 2)
         load_v(0)
         load_v(1)
-        load_x(1)
         load_w(1)
-        load_x(2)
-        load_z(1)
-        for n in range(3, PAIRS):
+        for n in range(2, PAIRS):
             load_x(n)
-            load_z(n - 1)
-        load_z(PAIRS - 1)
+            load_z(n)
         load_scales(nc.sync, y_sc, y_scales, G)
         nc.sync.dma_start(out=y_sb[:], in_=y_words.rearrange("g p n -> p g n"))
         with nc.allow_non_contiguous_dma(reason="one factor a partition for each tile of 128 stores"):
             nc.sync.dma_start(out=size_in[:, :, 0], in_=size.rearrange("(c p) -> p c", p=P))
 
-        lo, hi = slice(0, 1), slice(1, 2)
         nc.scalar.activation(out=ln_a[:], in_=a_in[:].rearrange("p g t -> p (g t)"), func=ACT.Ln)
+        nc.scalar.activation(out=warm[:], in_=warm[:], func=ACT.Exp)
+        spread_scales(0, "v")
+        spread_scales(1, "v")
+        keep_warm(WARM)
+        keep_warm(WARM)
         widen(0)
         widen(1)
-        turn_x(0)
-        turn_x(1)
         turn_z(0)
-        group_w("s", 0, 0, 384)
+        turn_x(0)
+        turn_z(1)
+        turn_x(1)
+        keep_warm(WARM)
+        group_w("s", 0, 0, 256)
         empty_z(0)
-        group_w("s", 1, 0, 256)
         empty_x(0)
-        quant_x(0, lo)
-        group_w("v", 0, 384, 512)
-        quant_x(0, hi)
+        empty_z(1)
         empty_x(1)
+        group_w("v", 0, 256, 512)
+        quant_z(0)
+        quant_x(0)
         quant_w(0)
         quant_x(1)
-        quant_z(0)
         widen(2)
         widen(3)
-        group_w("v", 1, 256, 512)
         taste(0, 0, True)
-        taste(0, 1, True)
-        taste(1, 0, True)
         travel(0, 0, False)
-        travel(1, 0, False)
         attract(0, 0)
-        attract(1, 0)
+        group_w("s", 1, 0, 256)
+        utility(1, 0)
+        taste(0, 1, True)
+        taste(1, 1, True)
         turn_x(2)
         turn_x(3)
-        taste(1, 1, True)
-        turn_z(1)
-        empty_z(1)
+        turn_z(2)
         empty_x(2)
-        quant_x(2, lo)
-        quant_x(2, hi)
-        quant_w(1)
-        widen(4)
-        quant_z(1)
         empty_x(3)
-        widen(5)
+        empty_z(2)
+        group_w("v", 1, 256, 512)
+        quant_z(1)
+        quant_w(1)
+        quant_x(2)
+        widen(4)
         quant_x(3)
-        taste(2, 0, True)
-        taste(2, 1, True)
+        widen(5)
         travel(0, 1, False)
         travel(1, 1, False)
         attract(0, 1)
         attract(1, 1)
-        travel(2, 0, False)
-        travel(2, 1, False)
+        utility(2, 0)
+        utility(2, 1)
         turn_x(4)
-        turn_z(2)
+        turn_z(3)
         turn_x(5)
-        attract(2, 0)
-        empty_z(2)
-        attract(2, 1)
         empty_x(4)
-        quant_x(4, lo)
+        empty_z(3)
         quant_z(2)
-        quant_x(4, hi)
         widen(6)
-        empty_x(5)
+        quant_x(4)
         widen(7)
-        quant_x(5)
-        utility(3, 0)
-        split_z(3)
-        utility(3, 1)
+        split_x(6)
+        split_x(7)
         split_z(4)
+        utility(3, 0)
+        empty_x(5)
+        utility(3, 1)
+        quant_x(5)
+        quant_z(3)
+        widen(8)
 
         for n in range(2, 7):
             utility(2 * n, 0)
-            group_p((n - 2) // 2, 0, "s", 2 * (n % 2), 4)
             utility(2 * n, 1)
             turn_x(2 * n + 2)
-            if n == 2:
-                turn_z(3)
-                empty_z(3)
             if n < 6:
                 turn_z(n + 2)
             turn_x(2 * n + 3)
             empty_x(2 * n + 2)
-            quant_x(2 * n + 2, lo)
-            if n > 2:
-                quant_z(n + 1)
-            quant_x(2 * n + 2, hi)
             if n < 6:
                 empty_z(n + 2)
-                widen(2 * n + 4)
-            if n == 2:
-                quant_z(n + 1)
-            empty_x(2 * n + 3)
-            if n < 6:
-                widen(2 * n + 5)
-            else:
-                quant_p(0, 0)
-            quant_x(2 * n + 3)
-            utility(2 * n + 1, 0)
             if n < 5:
                 split_z(n + 3)
-            group_p((n - 2) // 2, 0, "s", 2 * (n % 2) + 1, 4)
+            if n == 2:
+                group_p(0, 0)
+            quant_x(2 * n + 2)
+            if n < 6:
+                widen(2 * n + 5)
+                split_x(2 * n + 4)
+                split_x(2 * n + 5)
+                quant_z(n + 2)
+            if n < 6:
+                utility(2 * n + 1, 0)
+            empty_x(2 * n + 3)
+            quant_x(2 * n + 3)
+            if n == 6:
+                utility(2 * n + 1, 0)
             utility(2 * n + 1, 1)
-        nc.vector.tensor_copy(out=size_cols[:], in_=size_in[:, :, 0])
-        group_p(0, 1)
-        quant_p(1, 0)
-        utility(14, 0)
-        group_p(2, 0, "s", 2, 4)
-        utility(14, 1)
-        group_p(2, 0, "s", 3, 4)
-        utility(15, 0)
-        utility(15, 1)
-        quant_p(2, 0)
-        group_p(3, 0)
-        group_p(2, 1, "s")
-        quant_p(0, 1)
-        quant_p(3, 0)
+            if n == 2:
+                quant_p(0, 0)
+            if n == 3:
+                group_p(0, 1)
+            if n == 4:
+                quant_p(0, 1)
+            if n == 5:
+                group_p(1, 0)
+                nc.vector.tensor_copy(out=size_cols[:], in_=size_in[:, :, 0])
+                quant_p(1, 0)
+            if n < 5:
+                widen(2 * n + 6)
+        group_p(2, 0)
         group_p(1, 1)
-        quant_p(2, 1)
-        group_p(3, 1)
+        quant_p(2, 0)
+        for h in range(2):
+            utility(NT - 2, h)
+            utility(NT - 1, h)
+        group_p(2, 1, "s")
+        group_p(3, 0)
         quant_p(1, 1)
+        quant_p(3, 0)
+        group_p(3, 1)
+        quant_p(2, 1)
         quant_p(3, 1)
-        for g in range(G):
-            for jt in range(4):
-                flow_passes(jt, [g])
-                if g == G - 1:
-                    finish(jt, "s")
-        for g in (0, 2, 1, 3):
-            for jt in range(4, 7):
-                flow_passes(jt, [g])
-                if g == G - 1:
-                    finish(jt, "vsv"[jt - 4])
-        flow_passes(7, range(G))
-        finish(7, "s", 2)
+        for jt in range(3):
+            flow_passes(jt, range(G - 1))
+        for jt in range(3):
+            flow_passes(jt, [G - 1])
+            finish(jt, "s")
+        for jt in range(3, 8):
+            flow_passes(jt, range(G))
+            finish(jt, "s", 2 if jt == 7 else 1)

@@ -117,8 +117,8 @@ def tile_huff_retail_flows_s3_kernel(
             dst = rotating(name, [P, K], BF16, 4)
             copy(
                 engine,
-                dst[:].bitcast(F32).rearrange("p (c u m) -> p c u m", c=2, u=2),
-                src[:].bitcast(F32).rearrange("p (c m u) -> p c u m", c=2, u=2),
+                dst[:].bitcast(F32).rearrange("p (c u m) -> p c m u", c=2, u=2),
+                src[:].bitcast(F32).rearrange("p (c m u) -> p c m u", c=2, u=2),
             )
             return dst
 

@@ -65,8 +65,8 @@ def tile_huff_retail_flows_s3_kernel(
         z_q = [kept("z_q%d" % n, [P, 256], U32) for n in range(PAIRS)]
         z_s = [kept("z_s%d" % n, [P, 256], U8) for n in range(PAIRS)]
         x_raw = [kept("x_raw%d" % n, [P, 2 * K], U8) for n in range(PAIRS)]
-        x_q = [kept("x_q%d" % i, [P, 2, P], U32) for i in range(NT)]
-        x_s = [kept("x_s%d" % i, [P, 2, P], U8) for i in range(NT)]
+        x_q = [kept("x_q%d" % n, [P, 4 * P], U32) for n in range(PAIRS)]
+        x_s = [kept("x_s%d" % n, [P, 4 * P], U8) for n in range(PAIRS)]
         p_q = [[kept("p_q%d_%d" % (g, h), [P, HALF], U32) for h in range(2)] for g in range(G)]
         p_s = [[kept("p_s%d_%d" % (g, h), [P, HALF], U8) for h in range(2)] for g in range(G)]
         x_bf, x_split, x_bank, x_grp = {}, {}, {}, {}
@@ -105,28 +105,22 @@ def tile_huff_retail_flows_s3_kernel(
                 nc.vector.tensor_copy(out=dst, in_=src)
 
         def widen(i):
-            x_bf[i] = rotating("x_bf", [P, K], BF16, 6)
-            nc.vector.tensor_tensor(
-                out=x_bf[i][:],
-                in0=x_raw[i // 2][:, (i % 2) * K : (i % 2 + 1) * K].bitcast(FP8),
-                in1=xs_wide[:],
-                op=ALU.mult,
-            )
+            n, j = divmod(i, 2)
+            if j == 0:
+                x_bf[n] = rotating("x_bf", [P, 2 * K], BF16, 3)
+            cols = slice(j * K, (j + 1) * K)
+            nc.vector.tensor_tensor(out=x_bf[n][:, cols], in0=x_raw[n][:, cols].bitcast(FP8), in1=xs_wide[:], op=ALU.mult)
 
-        def split_words(engine, name, src):
-            dst = rotating(name, [P, K], BF16, 4)
+        def split_words(engine, dst, src):
             copy(
                 engine,
-                dst[:].bitcast(F32).rearrange("p (c u m) -> p c m u", c=2, u=2),
-                src[:].bitcast(F32).rearrange("p (c m u) -> p c m u", c=2, u=2),
+                dst.bitcast(F32).rearrange("p (c u m) -> p c m u", u=2, m=P),
+                src.bitcast(F32).rearrange("p (c m u) -> p c m u", u=2, m=P),
             )
-            return dst
-
-        def split_x(i):
-            x_split[i] = split_words("v", "x_split", x_bf[i])
 
         def split_z(n):
-            z_split[n] = split_words("s", "z_split", z_raw[n])
+            z_split[n] = rotating("z_split", [P, K], BF16, 2)
+            split_words("s", z_split[n][:], z_raw[n][:])
 
         def turn(plain, split):
             b = bank()
@@ -136,36 +130,37 @@ def tile_huff_retail_flows_s3_kernel(
                     if split is not None:
                         words = split[:].bitcast(F32)[:, m * P : (m + 1) * P]
                     else:
-                        words = plain[:].bitcast(F32)[:, 256 * c + u : 256 * (c + 1) : 2]
+                        words = plain.bitcast(F32)[:, 256 * c + u : 256 * (c + 1) : 2]
                     nc.tensor.transpose(b[:, m * P : (m + 1) * P], words, ident[:])
             return b
 
         def turn_x(i):
-            x_bank[i] = turn(x_bf[i], x_split.get(i))
+            x_bank[i] = turn(x_bf[i // 2][:, (i % 2) * K : (i % 2 + 1) * K], x_split.get(i))
 
         def turn_z(n):
-            z_bank[n] = turn(z_raw[n], z_split.get(n))
+            z_bank[n] = turn(z_raw[n][:], z_split.get(n))
 
-        def empty(engine, name, b):
-            grp = rotating(name, [P, K], BF16, 4)
-            copy(
-                engine,
-                grp[:].bitcast(F32).rearrange("p (c h u) -> p c h u", c=2, u=2),
-                b[:].rearrange("p (c u h) -> p c h u", c=2, u=2),
+        def empty(dst, b):
+            nc.scalar.copy(
+                out=dst.bitcast(F32).rearrange("p (c h u) -> p c h u", c=2, u=2),
+                in_=b[:].rearrange("p (c u h) -> p c h u", c=2, u=2),
             )
-            return grp
 
         def empty_x(i):
-            x_grp[i] = empty("s", "x_grp", x_bank[i])
+            n, j = divmod(i, 2)
+            if j == 0:
+                x_grp[n] = rotating("x_grp", [P, 2 * K], BF16, 2)
+            empty(x_grp[n][:, j * K : (j + 1) * K], x_bank[i])
 
         def empty_z(n):
-            z_grp[n] = empty("s", "z_grp", z_bank[n])
+            z_grp[n] = rotating("z_grp", [P, K], BF16, 3)
+            empty(z_grp[n][:], z_bank[n])
 
-        def quant_x(i):
+        def quant_x(i, tiles=1):
+            n, j = divmod(i, 2)
+            cols = slice(256 * j, 256 * (j + tiles))
             nc.vector.quantize_mx(
-                out=x_q[i][:].rearrange("p k h -> p (k h)").bitcast(FP8X4),
-                scales=x_s[i][:].rearrange("p k h -> p (k h)"),
-                in_=x_grp[i][:],
+                out=x_q[n][:, cols].bitcast(FP8X4), scales=x_s[n][:, cols], in_=x_grp[n][:, j * K : (j + tiles) * K]
             )
 
         def quant_z(n):
@@ -186,9 +181,10 @@ def tile_huff_retail_flows_s3_kernel(
             if first:
                 u_bank[i, h] = bank()
             for kg in range(2):
+                cols = slice((2 * (i % 2) + kg) * P, (2 * (i % 2) + kg + 1) * P)
                 nc.tensor.matmul_mx(
                     out=u_bank[i, h][:],
-                    lhsT=x_q[i][:, kg, :].bitcast(FP8X4), lhsT_scale=x_s[i][:, kg, :],
+                    lhsT=x_q[i // 2][:, cols].bitcast(FP8X4), lhsT_scale=x_s[i // 2][:, cols],
                     rhs=v_sb[h][:, kg, :].bitcast(FP4X4),
                     rhs_scale=v_sc[:, J * kg + HALF * h : J * kg + HALF * (h + 1)],
                     start=(first and kg == 0), stop=(not first and kg == 1),
@@ -282,17 +278,19 @@ def tile_huff_retail_flows_s3_kernel(
         nc.sync.dma_start(out=xs_cols[:], in_=x_scale.rearrange("o (g p t) -> p (o g) t", g=2, t=4))
         nc.scalar.dma_start(out=a_in[:], in_=a.rearrange("(g p t) -> p g t", p=P, t=4))
         load_x(0)
-        load_w(0)
         load_z(0)
+        load_w(0)
         load_x(1)
         load_z(1)
         load_scales(nc.sync, v_sc, v_scales, 2)
         load_v(0)
+        load_z(2)
         load_v(1)
         load_w(1)
         for n in range(2, PAIRS):
             load_x(n)
-            load_z(n)
+            if n + 1 < PAIRS:
+                load_z(n + 1)
         load_scales(nc.sync, y_sc, y_scales, G)
         nc.sync.dma_start(out=y_sb[:], in_=y_words.rearrange("g p n -> p g n"))
         with nc.allow_non_contiguous_dma(reason="one factor a partition for each tile of 128 stores"):
@@ -303,122 +301,105 @@ def tile_huff_retail_flows_s3_kernel(
         spread_scales(0, "v")
         spread_scales(1, "v")
         keep_warm(WARM)
-        keep_warm(WARM)
         widen(0)
         widen(1)
+        widen(2)
         turn_z(0)
+        keep_warm(WARM)
         turn_x(0)
+        keep_warm(WARM)
         turn_z(1)
         turn_x(1)
         keep_warm(WARM)
-        group_w("s", 0, 0, 256)
+        turn_z(2)
         empty_z(0)
+        group_w("s", 0, 0, 384)
         empty_x(0)
-        empty_z(1)
+        group_w("s", 0, 384, 512)
         empty_x(1)
-        group_w("v", 0, 256, 512)
+        empty_z(1)
+        empty_z(2)
         quant_z(0)
         quant_x(0)
         quant_w(0)
         quant_x(1)
-        widen(2)
         widen(3)
+        turn_x(2)
         taste(0, 0, True)
         travel(0, 0, False)
-        attract(0, 0)
-        group_w("s", 1, 0, 256)
-        utility(1, 0)
         taste(0, 1, True)
-        taste(1, 1, True)
-        turn_x(2)
-        turn_x(3)
-        turn_z(2)
         empty_x(2)
+        group_w("s", 1, 0, 256)
+        attract(0, 0)
+        utility(1, 0)
+        taste(1, 1, True)
+        turn_x(3)
         empty_x(3)
-        empty_z(2)
         group_w("v", 1, 256, 512)
         quant_z(1)
-        quant_w(1)
         quant_x(2)
+        quant_w(1)
         widen(4)
-        quant_x(3)
         widen(5)
+        quant_x(3)
+        utility(2, 0)
         travel(0, 1, False)
         travel(1, 1, False)
         attract(0, 1)
         attract(1, 1)
-        utility(2, 0)
         utility(2, 1)
+        split_z(3)
         turn_x(4)
-        turn_z(3)
         turn_x(5)
         empty_x(4)
-        empty_z(3)
+        empty_x(5)
         quant_z(2)
         widen(6)
-        quant_x(4)
         widen(7)
-        split_x(6)
-        split_x(7)
-        split_z(4)
-        utility(3, 0)
-        empty_x(5)
-        utility(3, 1)
+        quant_x(4)
         quant_x(5)
-        quant_z(3)
-        widen(8)
+        utility(3, 0)
+        utility(3, 1)
+        turn_x(6)
+        turn_x(7)
+        turn_z(3)
 
-        for n in range(2, 7):
+        units = [(0, 0), (0, 1), (1, 0), (1, 1)]
+        for n in range(2, 6):
+            empty_x(2 * n + 2)
+            empty_x(2 * n + 3)
+            empty_z(n + 1)
+            widen(2 * n + 4)
+            widen(2 * n + 5)
+            quant_x(2 * n + 2, 2)
+            quant_z(n + 1)
+            group_p(*units[n - 2])
+            if n > 2:
+                quant_p(*units[n - 3])
             utility(2 * n, 0)
             utility(2 * n, 1)
-            turn_x(2 * n + 2)
-            if n < 6:
-                turn_z(n + 2)
-            turn_x(2 * n + 3)
-            empty_x(2 * n + 2)
-            if n < 6:
-                empty_z(n + 2)
-            if n < 5:
-                split_z(n + 3)
-            if n == 2:
-                group_p(0, 0)
-            quant_x(2 * n + 2)
-            if n < 6:
-                widen(2 * n + 5)
-                split_x(2 * n + 4)
-                split_x(2 * n + 5)
-                quant_z(n + 2)
-            if n < 6:
-                utility(2 * n + 1, 0)
-            empty_x(2 * n + 3)
-            quant_x(2 * n + 3)
-            if n == 6:
-                utility(2 * n + 1, 0)
+            split_z(n + 2)
+            utility(2 * n + 1, 0)
             utility(2 * n + 1, 1)
-            if n == 2:
-                quant_p(0, 0)
-            if n == 3:
-                group_p(0, 1)
-            if n == 4:
-                quant_p(0, 1)
-            if n == 5:
-                group_p(1, 0)
-                nc.vector.tensor_copy(out=size_cols[:], in_=size_in[:, :, 0])
-                quant_p(1, 0)
-            if n < 5:
-                widen(2 * n + 6)
+            turn_x(2 * n + 4)
+            turn_x(2 * n + 5)
+            turn_z(n + 2)
+        empty_x(NT - 2)
+        empty_x(NT - 1)
+        empty_z(PAIRS - 1)
+        nc.vector.tensor_copy(out=size_cols[:], in_=size_in[:, :, 0])
+        quant_p(*units[3])
+        quant_x(NT - 2, 2)
+        quant_z(PAIRS - 1)
         group_p(2, 0)
-        group_p(1, 1)
+        group_p(2, 1)
         quant_p(2, 0)
-        for h in range(2):
-            utility(NT - 2, h)
-            utility(NT - 1, h)
-        group_p(2, 1, "s")
+        for i, h in [(12, 0), (13, 0), (12, 1), (14, 0), (15, 0), (13, 1), (14, 1), (15, 1)]:
+            utility(i, h)
         group_p(3, 0)
-        quant_p(1, 1)
+        quant_p(2, 1)
         quant_p(3, 0)
         group_p(3, 1)
-        quant_p(2, 1)
         quant_p(3, 1)
         for jt in range(3):
             flow_passes(jt, range(G - 1))

@@ -104,12 +104,16 @@ def tile_huff_retail_flows_s3_kernel(
             else:
                 nc.vector.tensor_copy(out=dst, in_=src)
 
-        def widen(i):
+        def widen(i, parts=1):
             n, j = divmod(i, 2)
             if j == 0:
                 x_bf[n] = rotating("x_bf", [P, 2 * K], BF16, 3)
-            cols = slice(j * K, (j + 1) * K)
-            nc.vector.tensor_tensor(out=x_bf[n][:, cols], in0=x_raw[n][:, cols].bitcast(FP8), in1=xs_wide[:], op=ALU.mult)
+            for part in range(parts):
+                k0, k1 = part * K // parts, (part + 1) * K // parts
+                cols = slice(j * K + k0, j * K + k1)
+                nc.vector.tensor_tensor(
+                    out=x_bf[n][:, cols], in0=x_raw[n][:, cols].bitcast(FP8), in1=xs_wide[:, k0:k1], op=ALU.mult
+                )
 
         def split_words(engine, dst, src):
             copy(
@@ -118,9 +122,13 @@ def tile_huff_retail_flows_s3_kernel(
                 src.bitcast(F32).rearrange("p (c m u) -> p c m u", u=2, m=P),
             )
 
-        def split_z(n):
+        def split_x(i):
+            x_split[i] = rotating("x_split", [P, K], BF16, 3)
+            split_words("v", x_split[i][:], x_bf[i // 2][:, (i % 2) * K : (i % 2 + 1) * K])
+
+        def split_z(n, engine="s"):
             z_split[n] = rotating("z_split", [P, K], BF16, 2)
-            split_words("s", z_split[n][:], z_raw[n][:])
+            split_words(engine, z_split[n][:], z_raw[n][:])
 
         def turn(plain, split):
             b = bank()
@@ -204,7 +212,7 @@ def tile_huff_retail_flows_s3_kernel(
         def attract(i, h):
             g, t = divmod(i, 4)
             if t == 0:
-                p_raw[g, h] = rotating("p_raw", [P, 4, HALF], BF16, 6)
+                p_raw[g, h] = rotating("p_raw", [P, 4, HALF], BF16, 8)
             nc.scalar.activation(
                 out=p_raw[g, h][:, t, :], in_=u_bank[i, h][:], func=ACT.Exp, bias=ln_a[:, i : i + 1], scale=1.0
             )
@@ -253,6 +261,32 @@ def tile_huff_retail_flows_s3_kernel(
                     )
                 nc.sync.dma_start(out=rows[:, cols], in_=o[:, cols])
 
+        def last_flows(jt, parts):
+            h, c = divmod(jt, 4)
+            cols = slice(c * P, (c + 1) * P)
+            o = rotating("o_sb", [P, C], F32, 6)
+            width = C // parts
+            for part in range(parts):
+                b = bank()
+                for n0 in range(0, width, P):
+                    c0 = part * width + n0
+                    for g in range(G):
+                        nc.tensor.matmul_mx(
+                            out=b[:, n0 : n0 + P],
+                            lhsT=p_q[g][h][:, cols].bitcast(FP8X4), lhsT_scale=p_s[g][h][:, cols],
+                            rhs=y_sb[:, g, 2 * c0 : 2 * (c0 + P)].bitcast(FP4X4),
+                            rhs_scale=y_sc[:, C * g + c0 : C * g + c0 + P],
+                            start=(g == 0), stop=(g == G - 1),
+                        )
+                span = slice(part * width, (part + 1) * width)
+                if part % 2 == 0:
+                    nc.scalar.activation(out=o[:, span], in_=b[:, 0:width], func=ACT.Copy, scale=size_cols[:, jt : jt + 1])
+                else:
+                    nc.vector.tensor_scalar(
+                        out=o[:, span], in0=b[:, 0:width], scalar1=size_cols[:, jt : jt + 1], scalar2=None, op0=ALU.mult
+                    )
+                nc.sync.dma_start(out=out[jt * P : (jt + 1) * P, span], in_=o[:, span])
+
         def keep_warm(count):
             b = bank()
             for k in range(count):
@@ -284,13 +318,13 @@ def tile_huff_retail_flows_s3_kernel(
         load_z(1)
         load_scales(nc.sync, v_sc, v_scales, 2)
         load_v(0)
-        load_z(2)
         load_v(1)
         load_w(1)
-        for n in range(2, PAIRS):
+        load_z(2)
+        load_x(2)
+        for n in range(3, PAIRS):
+            load_z(n)
             load_x(n)
-            if n + 1 < PAIRS:
-                load_z(n + 1)
         load_scales(nc.sync, y_sc, y_scales, G)
         nc.sync.dma_start(out=y_sb[:], in_=y_words.rearrange("g p n -> p g n"))
         with nc.allow_non_contiguous_dma(reason="one factor a partition for each tile of 128 stores"):
@@ -301,40 +335,41 @@ def tile_huff_retail_flows_s3_kernel(
         spread_scales(0, "v")
         spread_scales(1, "v")
         keep_warm(WARM)
-        widen(0)
+        widen(0, 2)
         widen(1)
         widen(2)
         turn_z(0)
         keep_warm(WARM)
         turn_x(0)
         keep_warm(WARM)
-        turn_z(1)
         turn_x(1)
+        turn_z(1)
+        turn_x(2)
         keep_warm(WARM)
-        turn_z(2)
         empty_z(0)
-        group_w("s", 0, 0, 384)
+        group_w("s", 0, 0, 256)
         empty_x(0)
-        group_w("s", 0, 384, 512)
+        group_w("s", 0, 256, 384)
         empty_x(1)
         empty_z(1)
-        empty_z(2)
+        empty_x(2)
+        group_w("v", 0, 384, 512)
         quant_z(0)
         quant_x(0)
         quant_w(0)
         quant_x(1)
         widen(3)
-        turn_x(2)
         taste(0, 0, True)
-        travel(0, 0, False)
         taste(0, 1, True)
-        empty_x(2)
+        travel(0, 0, False)
         group_w("s", 1, 0, 256)
         attract(0, 0)
         utility(1, 0)
         taste(1, 1, True)
         turn_x(3)
+        turn_z(2)
         empty_x(3)
+        empty_z(2)
         group_w("v", 1, 256, 512)
         quant_z(1)
         quant_x(2)
@@ -363,49 +398,114 @@ def tile_huff_retail_flows_s3_kernel(
         turn_x(6)
         turn_x(7)
         turn_z(3)
-
-        units = [(0, 0), (0, 1), (1, 0), (1, 1)]
-        for n in range(2, 6):
-            empty_x(2 * n + 2)
-            empty_x(2 * n + 3)
-            empty_z(n + 1)
-            widen(2 * n + 4)
-            widen(2 * n + 5)
-            quant_x(2 * n + 2, 2)
-            quant_z(n + 1)
-            group_p(*units[n - 2])
-            if n > 2:
-                quant_p(*units[n - 3])
-            utility(2 * n, 0)
-            utility(2 * n, 1)
-            split_z(n + 2)
-            utility(2 * n + 1, 0)
-            utility(2 * n + 1, 1)
-            turn_x(2 * n + 4)
-            turn_x(2 * n + 5)
-            turn_z(n + 2)
-        empty_x(NT - 2)
-        empty_x(NT - 1)
-        empty_z(PAIRS - 1)
+        widen(8)
+        empty_x(6)
+        empty_x(7)
+        empty_z(3)
+        widen(9)
+        split_x(8)
+        quant_x(6, 2)
+        split_x(9)
+        quant_z(3)
+        widen(10)
+        utility(4, 0)
+        utility(4, 1)
+        split_z(4)
+        utility(5, 0)
+        utility(5, 1)
+        turn_x(8)
+        turn_x(9)
+        turn_z(4)
+        empty_x(8)
+        empty_x(9)
+        empty_z(4)
+        widen(11)
+        split_x(10)
+        quant_x(8, 2)
+        split_x(11)
+        quant_z(4)
+        widen(12)
+        group_p(0, 0)
+        utility(6, 0)
+        utility(6, 1)
+        split_z(5)
+        utility(7, 0)
+        utility(7, 1)
+        turn_x(10)
+        turn_x(11)
+        turn_z(5)
+        empty_x(10)
+        empty_x(11)
+        empty_z(5)
+        widen(13)
+        split_x(12)
+        quant_x(10, 2)
+        split_x(13)
+        quant_z(5)
+        widen(14)
+        quant_p(0, 0)
+        utility(8, 0)
+        utility(8, 1)
+        utility(9, 0)
+        utility(9, 1)
+        turn_x(12)
+        turn_x(13)
+        turn_z(6)
+        empty_x(12)
+        empty_x(13)
+        empty_z(6)
+        widen(15)
+        split_x(14)
+        quant_x(12, 2)
+        split_x(15)
+        quant_z(6)
+        group_p(1, 0)
+        utility(10, 0)
+        utility(10, 1)
+        utility(11, 0)
+        utility(11, 1)
+        turn_x(14)
+        turn_x(15)
+        turn_z(7)
+        empty_x(14)
+        empty_x(15)
+        empty_z(7)
         nc.vector.tensor_copy(out=size_cols[:], in_=size_in[:, :, 0])
-        quant_p(*units[3])
-        quant_x(NT - 2, 2)
-        quant_z(PAIRS - 1)
         group_p(2, 0)
-        group_p(2, 1)
+        quant_x(14, 2)
+        quant_z(7)
+        quant_p(1, 0)
+        group_p(0, 1)
         quant_p(2, 0)
-        for i, h in [(12, 0), (13, 0), (12, 1), (14, 0), (15, 0), (13, 1), (14, 1), (15, 1)]:
-            utility(i, h)
+        group_p(1, 1)
+        utility(12, 0)
+        utility(13, 0)
+        utility(12, 1)
+        utility(14, 0)
+        utility(15, 0)
+        utility(13, 1)
+        utility(14, 1)
+        utility(15, 1)
+        group_p(2, 1, "s")
         group_p(3, 0)
-        quant_p(2, 1)
+        quant_p(0, 1)
         quant_p(3, 0)
+        quant_p(1, 1)
         group_p(3, 1)
+        quant_p(2, 1)
         quant_p(3, 1)
         for jt in range(3):
             flow_passes(jt, range(G - 1))
         for jt in range(3):
             flow_passes(jt, [G - 1])
             finish(jt, "s")
-        for jt in range(3, 8):
-            flow_passes(jt, range(G))
-            finish(jt, "s", 2 if jt == 7 else 1)
+        flow_passes(3, range(G))
+        finish(3, "s")
+        for g in (0, 1, 2, 3):
+            for jt in range(4, 6):
+                flow_passes(jt, [g])
+                if g == G - 1:
+                    finish(jt, "s")
+        flow_passes(6, range(G))
+        finish(6, "s")
+        last_flows(7, 2)

@@ -318,13 +318,15 @@ def tile_huff_retail_flows_s3_kernel(
         load_z(1)
         load_scales(nc.sync, v_sc, v_scales, 2)
         load_v(0)
+        load_z(2)
         load_v(1)
         load_w(1)
-        load_z(2)
+        load_z(3)
         load_x(2)
         for n in range(3, PAIRS):
-            load_z(n)
             load_x(n)
+            if n + 1 < PAIRS:
+                load_z(n + 1)
         load_scales(nc.sync, y_sc, y_scales, G)
         nc.sync.dma_start(out=y_sb[:], in_=y_words.rearrange("g p n -> p g n"))
         with nc.allow_non_contiguous_dma(reason="one factor a partition for each tile of 128 stores"):
@@ -334,7 +336,6 @@ def tile_huff_retail_flows_s3_kernel(
         nc.scalar.activation(out=warm[:], in_=warm[:], func=ACT.Exp)
         spread_scales(0, "v")
         spread_scales(1, "v")
-        keep_warm(WARM)
         widen(0, 2)
         widen(1)
         widen(2)
@@ -344,8 +345,9 @@ def tile_huff_retail_flows_s3_kernel(
         keep_warm(WARM)
         turn_x(1)
         turn_z(1)
-        turn_x(2)
         keep_warm(WARM)
+        turn_x(2)
+        turn_z(2)
         empty_z(0)
         group_w("s", 0, 0, 256)
         empty_x(0)
@@ -353,6 +355,7 @@ def tile_huff_retail_flows_s3_kernel(
         empty_x(1)
         empty_z(1)
         empty_x(2)
+        empty_z(2)
         group_w("v", 0, 384, 512)
         quant_z(0)
         quant_x(0)
@@ -367,9 +370,9 @@ def tile_huff_retail_flows_s3_kernel(
         utility(1, 0)
         taste(1, 1, True)
         turn_x(3)
-        turn_z(2)
+        turn_z(3)
         empty_x(3)
-        empty_z(2)
+        empty_z(3)
         group_w("v", 1, 256, 512)
         quant_z(1)
         quant_x(2)
@@ -383,7 +386,6 @@ def tile_huff_retail_flows_s3_kernel(
         attract(0, 1)
         attract(1, 1)
         utility(2, 1)
-        split_z(3)
         turn_x(4)
         turn_x(5)
         empty_x(4)
@@ -397,11 +399,9 @@ def tile_huff_retail_flows_s3_kernel(
         utility(3, 1)
         turn_x(6)
         turn_x(7)
-        turn_z(3)
         widen(8)
         empty_x(6)
         empty_x(7)
-        empty_z(3)
         widen(9)
         split_x(8)
         quant_x(6, 2)
@@ -494,13 +494,11 @@ def tile_huff_retail_flows_s3_kernel(
         group_p(3, 1)
         quant_p(2, 1)
         quant_p(3, 1)
-        for jt in range(3):
+        for jt in range(4):
             flow_passes(jt, range(G - 1))
-        for jt in range(3):
+        for jt in range(4):
             flow_passes(jt, [G - 1])
             finish(jt, "s")
-        flow_passes(3, range(G))
-        finish(3, "s")
         for g in (0, 1, 2, 3):
             for jt in range(4, 6):
                 flow_passes(jt, [g])

@@ -22,7 +22,6 @@ G = H // 512
 NT = 4 * G
 PAIRS = NT // 2
 HALF = J // 2
-WARM = 2
 
 
 def tile_huff_retail_flows_s3_kernel(
@@ -41,14 +40,14 @@ def tile_huff_retail_flows_s3_kernel(
         def rotating(name, shape, dtype, bufs):
             return work.tile(shape, dtype, name=name, tag=name, bufs=bufs, align_bytes=64)
 
-        def bank():
-            return psum.tile([P, 512], F32, name="bank", tag="bank", bufs=8)
+        def bank(ring):
+            return psum.tile([P, 512], F32, name=ring, tag=ring, bufs={"turned": 3, "sums": 5}[ring])
 
         ident = kept("ident", [P, P], F32)
         a_in = kept("a_in", [P, G, 4], BF16)
         ln_a = kept("ln_a", [P, NT], F32)
         xs_cols = kept("xs_cols", [P, 2, 4], F32)
-        xs_wide = kept("xs_wide", [P, K], F32)
+        one = kept("one", [P, 1], F32)
         size_in = kept("size_in", [P, 8, 2], BF16)
         warm = kept("warm", [P, 1], F32)
         ones = kept("ones", [P, 512], BF16)
@@ -69,7 +68,7 @@ def tile_huff_retail_flows_s3_kernel(
         x_s = [kept("x_s%d" % n, [P, 4 * P], U8) for n in range(PAIRS)]
         p_q = [[kept("p_q%d_%d" % (g, h), [P, HALF], U32) for h in range(2)] for g in range(G)]
         p_s = [[kept("p_s%d_%d" % (g, h), [P, HALF], U8) for h in range(2)] for g in range(G)]
-        x_bf, x_split, x_bank, x_grp = {}, {}, {}, {}
+        x_bf, x_apart, x_bank, x_grp = {}, {}, {}, {}
         z_split, z_bank, z_grp = {}, {}, {}
         u_bank, p_raw, p_grp, f_bank = {}, {}, {}, {}
 
@@ -86,14 +85,16 @@ def tile_huff_retail_flows_s3_kernel(
             src = z[512 * g : 512 * (g + 1), :].rearrange("(p t) k -> p (t k)", t=4)
             nc.sync.dma_start(out=z_raw[n][:], in_=src[:, 2 * half * D : 2 * (half + 1) * D])
 
-        def load_x(n):
+        def load_x(n, j0=0, j1=2):
             g, half = divmod(n, 2)
             src = x_bytes[512 * g : 512 * (g + 1), :].rearrange("(p t) k -> p (t k)", t=4)
-            nc.sync.dma_start(out=x_raw[n][:], in_=src[:, 2 * half * K : 2 * (half + 1) * K])
+            nc.sync.dma_start(
+                out=x_raw[n][:, j0 * K : j1 * K], in_=src[:, (2 * half + j0) * K : (2 * half + j1) * K]
+            )
 
-        def load_scales(queue, tile, src, groups):
+        def load_scales(tile, src, groups):
             for r in range(4):
-                queue.dma_start(
+                nc.sync.dma_start(
                     out=tile[r:P:32, :].bitcast(I32).rearrange("q (g n) -> q g n", g=groups),
                     in_=src.bitcast(I32).rearrange("g (q r) n -> r q g n", r=4)[r],
                 )
@@ -104,65 +105,88 @@ def tile_huff_retail_flows_s3_kernel(
             else:
                 nc.vector.tensor_copy(out=dst, in_=src)
 
-        def widen(i, parts=1):
-            n, j = divmod(i, 2)
-            if j == 0:
-                x_bf[n] = rotating("x_bf", [P, 2 * K], BF16, 3)
-            for part in range(parts):
-                k0, k1 = part * K // parts, (part + 1) * K // parts
-                cols = slice(j * K + k0, j * K + k1)
-                nc.vector.tensor_tensor(
-                    out=x_bf[n][:, cols], in0=x_raw[n][:, cols].bitcast(FP8), in1=xs_wide[:, k0:k1], op=ALU.mult
+        def cast(i, engine):
+            x_bf[i] = rotating("x_bf", [P, K], BF16, 4)
+            src = x_raw[i // 2][:, (i % 2) * K : (i % 2 + 1) * K].bitcast(FP8)
+            x_apart[i] = engine == "v"
+            if engine == "v":
+                nc.vector.tensor_scalar(
+                    out=x_bf[i][:].rearrange("p (u m e) -> p m u e", u=2, e=2),
+                    in0=src.rearrange("p (m u e) -> p m u e", u=2, e=2),
+                    scalar1=one[:], scalar2=None, op0=ALU.mult,
                 )
+            else:
+                nc.scalar.copy(out=x_bf[i][:], in_=src)
 
-        def split_words(engine, dst, src):
-            copy(
-                engine,
-                dst.bitcast(F32).rearrange("p (c u m) -> p c m u", u=2, m=P),
-                src.bitcast(F32).rearrange("p (c m u) -> p c m u", u=2, m=P),
+        def first_tile(c):
+            if c == 0:
+                x_bf[0] = rotating("x_bf", [P, K], BF16, 4)
+                x_grp[0] = kept("x_grp0", [P, 2 * K], BF16)
+            half = x_bf[0][:, 512 * c : 512 * (c + 1)]
+            nc.vector.tensor_scalar(
+                out=half.rearrange("p (u m e) -> p m u e", u=2, e=2),
+                in0=x_raw[0][:, 512 * c : 512 * (c + 1)].bitcast(FP8).rearrange("p (m u e) -> p m u e", u=2, e=2),
+                scalar1=one[:], scalar2=None, op0=ALU.mult,
+            )
+            x_bank[0, c] = bank("turned")
+            for u in range(2):
+                nc.tensor.transpose(x_bank[0, c][:, u * P : (u + 1) * P], half.bitcast(F32)[:, u * P : (u + 1) * P], ident[:])
+
+        def first_scale(c):
+            nc.vector.tensor_tensor(
+                out=x_grp[0][:, 512 * c : 512 * (c + 1)].rearrange("p (h u e) -> p h u e", u=2, e=2),
+                in0=x_bank[0, c][:, 0:256].bitcast(BF16).rearrange("p (u h e) -> p h u e", u=2, e=2),
+                in1=xs_cols[:, c, :].rearrange("p (u e) -> p u e", u=2).unsqueeze(1).to_broadcast([P, P, 2, 2]),
+                op=ALU.mult,
             )
 
-        def split_x(i):
-            x_split[i] = rotating("x_split", [P, K], BF16, 3)
-            split_words("v", x_split[i][:], x_bf[i // 2][:, (i % 2) * K : (i % 2 + 1) * K])
+        def first_quant(c):
+            cols = slice(P * c, P * (c + 1))
+            nc.vector.quantize_mx(
+                out=x_q[0][:, cols].bitcast(FP8X4), scales=x_s[0][:, cols], in_=x_grp[0][:, 512 * c : 512 * (c + 1)]
+            )
 
-        def split_z(n, engine="s"):
+        def split_z(n):
             z_split[n] = rotating("z_split", [P, K], BF16, 2)
-            split_words(engine, z_split[n][:], z_raw[n][:])
+            nc.scalar.copy(
+                out=z_split[n][:].bitcast(F32).rearrange("p (u m) -> p m u", u=2),
+                in_=z_raw[n][:].bitcast(F32).rearrange("p (m u) -> p m u", u=2),
+            )
 
-        def turn(plain, split):
-            b = bank()
+        def turn(src, apart):
+            b = bank("turned")
+            words = src.bitcast(F32)
             for c in range(2):
                 for u in range(2):
-                    m = 2 * c + u
-                    if split is not None:
-                        words = split[:].bitcast(F32)[:, m * P : (m + 1) * P]
-                    else:
-                        words = plain.bitcast(F32)[:, 256 * c + u : 256 * (c + 1) : 2]
-                    nc.tensor.transpose(b[:, m * P : (m + 1) * P], words, ident[:])
+                    m = 2 * u + c
+                    cols = words[:, m * P : (m + 1) * P] if apart else words[:, 256 * c + u : 256 * (c + 1) : 2]
+                    nc.tensor.transpose(b[:, m * P : (m + 1) * P], cols, ident[:])
             return b
 
         def turn_x(i):
-            x_bank[i] = turn(x_bf[i // 2][:, (i % 2) * K : (i % 2 + 1) * K], x_split.get(i))
+            x_bank[i] = turn(x_bf[i][:], x_apart[i])
 
         def turn_z(n):
-            z_bank[n] = turn(z_raw[n][:], z_split.get(n))
+            z_bank[n] = turn(z_split[n][:], True) if n in z_split else turn(z_raw[n][:], False)
 
-        def empty(dst, b):
-            nc.scalar.copy(
-                out=dst.bitcast(F32).rearrange("p (c h u) -> p c h u", c=2, u=2),
-                in_=b[:].rearrange("p (c u h) -> p c h u", c=2, u=2),
+        def scale_x(i):
+            n, j = divmod(i, 2)
+            if n not in x_grp:
+                x_grp[n] = kept("x_grp%d" % n, [P, 2 * K], BF16)
+            nc.vector.tensor_tensor(
+                out=x_grp[n][:, j * K : (j + 1) * K].rearrange("p (c h u e) -> p c h u e", c=2, u=2, e=2),
+                in0=x_bank[i][:].bitcast(BF16).rearrange("p (u c h e) -> p c h u e", c=2, u=2, e=2),
+                in1=xs_cols[:].rearrange("p c (u e) -> p c u e", u=2).unsqueeze(2).to_broadcast([P, 2, P, 2, 2]),
+                op=ALU.mult,
             )
 
-        def empty_x(i):
-            n, j = divmod(i, 2)
-            if j == 0:
-                x_grp[n] = rotating("x_grp", [P, 2 * K], BF16, 2)
-            empty(x_grp[n][:, j * K : (j + 1) * K], x_bank[i])
-
-        def empty_z(n):
+        def empty_z(n, engine="s"):
             z_grp[n] = rotating("z_grp", [P, K], BF16, 3)
-            empty(z_grp[n][:], z_bank[n])
+            copy(
+                engine,
+                z_grp[n][:].bitcast(F32).rearrange("p (m u) -> p m u", u=2),
+                z_bank[n][:].rearrange("p (u m) -> p m u", u=2),
+            )
 
         def quant_x(i, tiles=1):
             n, j = divmod(i, 2)
@@ -175,7 +199,12 @@ def tile_huff_retail_flows_s3_kernel(
             nc.vector.quantize_mx(out=z_q[n][:].bitcast(FP8X4), scales=z_s[n][:], in_=z_grp[n][:])
 
         def group4(engine, dst, src):
-            copy(engine, dst.rearrange("p (c i) t -> p c t i", i=4), src.rearrange("p t (c i) -> p c t i", i=4))
+            if engine == "g":
+                nc.gpsimd.tensor_scalar(
+                    out=dst, in0=src.rearrange("p t n -> p n t"), scalar1=1.0, scalar2=0.0, op0=ALU.mult, op1=ALU.add
+                )
+            else:
+                copy(engine, dst.rearrange("p (c i) t -> p c t i", i=4), src.rearrange("p t (c i) -> p c t i", i=4))
 
         def group_w(engine, h, c0, c1):
             group4(engine, w_grp[h][:, c0:c1, :], w_raw[h][:, :, c0:c1])
@@ -185,9 +214,9 @@ def tile_huff_retail_flows_s3_kernel(
                 out=w_q[h][:].bitcast(FP8X4), scales=w_s[h][:], in_=w_grp[h][:].rearrange("p n t -> p (n t)")
             )
 
-        def taste(i, h, first):
+        def taste(i, h, first=True):
             if first:
-                u_bank[i, h] = bank()
+                u_bank[i, h] = bank("sums")
             for kg in range(2):
                 cols = slice((2 * (i % 2) + kg) * P, (2 * (i % 2) + kg + 1) * P)
                 nc.tensor.matmul_mx(
@@ -198,9 +227,9 @@ def tile_huff_retail_flows_s3_kernel(
                     start=(first and kg == 0), stop=(not first and kg == 1),
                 )
 
-        def travel(i, h, first):
+        def travel(i, h, first=False):
             if first:
-                u_bank[i, h] = bank()
+                u_bank[i, h] = bank("sums")
             cols = slice((i % 2) * P, (i % 2 + 1) * P)
             nc.tensor.matmul_mx(
                 out=u_bank[i, h][:],
@@ -218,20 +247,21 @@ def tile_huff_retail_flows_s3_kernel(
             )
 
         def utility(i, h):
-            taste(i, h, True)
-            travel(i, h, False)
+            taste(i, h)
+            travel(i, h)
             attract(i, h)
 
-        def group_p(g, h, engine="v", part=0, parts=1):
-            if part == 0:
-                p_grp[g, h] = rotating("p_grp", [P, HALF, 4], BF16, 4)
-            cols = slice(part * HALF // parts, (part + 1) * HALF // parts)
-            group4(engine, p_grp[g, h][:, cols, :], p_raw[g, h][:, :, cols])
+        def group_p(g, h, engine, c0, c1, after=None):
+            if after is None:
+                p_grp[g, h, c0] = rotating("p_grp%d" % (c1 - c0), [P, c1 - c0, 4], BF16, {128: 4, 256: 3, 512: 2}[c1 - c0])[:]
+            else:
+                p_grp[g, h, c0] = x_grp[after][:, 0 : 4 * (c1 - c0)].rearrange("p (n t) -> p n t", t=4)
+            group4(engine, p_grp[g, h, c0], p_raw[g, h][:, :, c0:c1])
 
-        def quant_p(g, h):
+        def quant_p(g, h, c0=0, c1=HALF):
             nc.vector.quantize_mx(
-                out=p_q[g][h][:].bitcast(FP8X4), scales=p_s[g][h][:],
-                in_=p_grp[g, h][:].rearrange("p n t -> p (n t)"),
+                out=p_q[g][h][:, c0:c1].bitcast(FP8X4), scales=p_s[g][h][:, c0:c1],
+                in_=p_grp[g, h, c0].rearrange("p n t -> p (n t)"),
             )
 
         def flow_passes(jt, groups):
@@ -239,7 +269,7 @@ def tile_huff_retail_flows_s3_kernel(
             cols = slice(c * P, (c + 1) * P)
             for g in groups:
                 if g == 0:
-                    f_bank[jt] = bank()
+                    f_bank[jt] = bank("turned" if 1 <= jt <= 3 else "sums")
                 nc.tensor.matmul_mx(
                     out=f_bank[jt][:],
                     lhsT=p_q[g][h][:, cols].bitcast(FP8X4), lhsT_scale=p_s[g][h][:, cols],
@@ -247,19 +277,14 @@ def tile_huff_retail_flows_s3_kernel(
                     start=(g == 0), stop=(g == G - 1),
                 )
 
-        def finish(jt, engine, parts=1):
+        def finish(jt, engine):
             o = rotating("o_sb", [P, C], F32, 6)
-            rows = out[jt * P : (jt + 1) * P, :]
             factor = size_cols[:, jt : jt + 1]
-            for part in range(parts):
-                cols = slice(part * C // parts, (part + 1) * C // parts)
-                if engine == "s":
-                    nc.scalar.activation(out=o[:, cols], in_=f_bank[jt][:, cols], func=ACT.Copy, scale=factor)
-                else:
-                    nc.vector.tensor_scalar(
-                        out=o[:, cols], in0=f_bank[jt][:, cols], scalar1=factor, scalar2=None, op0=ALU.mult
-                    )
-                nc.sync.dma_start(out=rows[:, cols], in_=o[:, cols])
+            if engine == "s":
+                nc.scalar.activation(out=o[:], in_=f_bank[jt][:], func=ACT.Copy, scale=factor)
+            else:
+                nc.vector.tensor_scalar(out=o[:], in0=f_bank[jt][:], scalar1=factor, scalar2=None, op0=ALU.mult)
+            nc.sync.dma_start(out=out[jt * P : (jt + 1) * P, :], in_=o[:])
 
         def last_flows(jt, parts):
             h, c = divmod(jt, 4)
@@ -267,7 +292,7 @@ def tile_huff_retail_flows_s3_kernel(
             o = rotating("o_sb", [P, C], F32, 6)
             width = C // parts
             for part in range(parts):
-                b = bank()
+                b = bank("turned")
                 for n0 in range(0, width, P):
                     c0 = part * width + n0
                     for g in range(G):
@@ -288,222 +313,173 @@ def tile_huff_retail_flows_s3_kernel(
                 nc.sync.dma_start(out=out[jt * P : (jt + 1) * P, span], in_=o[:, span])
 
         def keep_warm(count):
-            b = bank()
+            b = bank("sums")
             for k in range(count):
                 nc.tensor.matmul(out=b[:], lhsT=ones[:, 0:P], rhs=ones[:], start=True, stop=True)
 
-        def spread_scales(kg, engine):
-            b = bank()
-            for t in range(4):
-                nc.tensor.transpose(
-                    b[:, t * P : (t + 1) * P], xs_cols[:, kg, t : t + 1].to_broadcast([P, P]), ident[:]
-                )
-            copy(
-                engine,
-                xs_wide[:, 512 * kg : 512 * (kg + 1)].rearrange("p (m t) -> p m t", t=4),
-                b[:].rearrange("p (t m) -> p m t", t=4),
-            )
-
-        nc.vector.memset(v_sc[:].bitcast(I32), 0)
-        nc.vector.memset(y_sc[:].bitcast(I32), 0)
-        nc.vector.memset(warm[:], 1.0)
-        make_identity(nc, ident[:])
-        nc.gpsimd.memset(ones[:], 1.0)
-        nc.sync.dma_start(out=xs_cols[:], in_=x_scale.rearrange("o (g p t) -> p (o g) t", g=2, t=4))
         nc.scalar.dma_start(out=a_in[:], in_=a.rearrange("(g p t) -> p g t", p=P, t=4))
-        load_x(0)
+        nc.vector.memset(ones[:], 1.0)
+        nc.vector.memset(v_sc[:].bitcast(I32), 0)
+        nc.vector.memset(one[:], 1.0)
+        nc.vector.memset(warm[:], 1.0)
+        nc.vector.memset(y_sc[:].bitcast(I32), 0)
+        make_identity(nc, ident[:])
+        load_x(0, 0, 1)
+        nc.sync.dma_start(out=xs_cols[:], in_=x_scale.rearrange("o (g p t) -> p (o g) t", g=2, t=4))
+        load_x(0, 1, 2)
         load_z(0)
-        load_w(0)
-        load_x(1)
-        load_z(1)
-        load_scales(nc.sync, v_sc, v_scales, 2)
+        load_scales(v_sc, v_scales, 2)
         load_v(0)
-        load_z(2)
+        load_x(1)
+        load_w(0)
         load_v(1)
-        load_w(1)
-        load_z(3)
         load_x(2)
-        for n in range(3, PAIRS):
+        load_w(1)
+        load_z(1)
+        load_z(2)
+        load_x(3)
+        load_z(3)
+        for n in range(4, PAIRS):
             load_x(n)
-            if n + 1 < PAIRS:
-                load_z(n + 1)
-        load_scales(nc.sync, y_sc, y_scales, G)
+            load_z(n)
+        load_scales(y_sc, y_scales, G)
         nc.sync.dma_start(out=y_sb[:], in_=y_words.rearrange("g p n -> p g n"))
         with nc.allow_non_contiguous_dma(reason="one factor a partition for each tile of 128 stores"):
             nc.sync.dma_start(out=size_in[:, :, 0], in_=size.rearrange("(c p) -> p c", p=P))
 
         nc.scalar.activation(out=ln_a[:], in_=a_in[:].rearrange("p g t -> p (g t)"), func=ACT.Ln)
         nc.scalar.activation(out=warm[:], in_=warm[:], func=ACT.Exp)
-        spread_scales(0, "v")
-        spread_scales(1, "v")
-        widen(0, 2)
-        widen(1)
-        widen(2)
+        keep_warm(3)
+        first_tile(0)
+        first_tile(1)
+        keep_warm(2)
+        cast(1, "v")
         turn_z(0)
-        keep_warm(WARM)
-        turn_x(0)
-        keep_warm(WARM)
-        turn_x(1)
-        turn_z(1)
-        keep_warm(WARM)
-        turn_x(2)
-        turn_z(2)
         empty_z(0)
-        group_w("s", 0, 0, 256)
-        empty_x(0)
-        group_w("s", 0, 256, 384)
-        empty_x(1)
-        empty_z(1)
-        empty_x(2)
-        empty_z(2)
-        group_w("v", 0, 384, 512)
+        first_scale(0)
+        turn_x(1)
+        keep_warm(1)
+        first_scale(1)
+        first_quant(0)
+        first_quant(1)
+        scale_x(1)
         quant_z(0)
-        quant_x(0)
-        quant_w(0)
         quant_x(1)
-        widen(3)
-        taste(0, 0, True)
-        taste(0, 1, True)
-        travel(0, 0, False)
-        group_w("s", 1, 0, 256)
-        attract(0, 0)
-        utility(1, 0)
-        taste(1, 1, True)
+        cast(2, "s")
+        cast(3, "s")
+        taste(0, 0)
+        turn_x(2)
         turn_x(3)
-        turn_z(3)
-        empty_x(3)
-        empty_z(3)
-        group_w("v", 1, 256, 512)
-        quant_z(1)
+        scale_x(2)
+        group_w("s", 0, 0, 256)
+        group_w("v", 0, 256, 512)
         quant_x(2)
-        quant_w(1)
-        widen(4)
-        widen(5)
-        quant_x(3)
-        utility(2, 0)
-        travel(0, 1, False)
-        travel(1, 1, False)
-        attract(0, 1)
-        attract(1, 1)
-        utility(2, 1)
+        quant_w(0)
+        scale_x(3)
+        cast(4, "s")
+        cast(5, "s")
+        taste(1, 0)
+        taste(0, 1)
+        taste(1, 1)
         turn_x(4)
         turn_x(5)
-        empty_x(4)
-        empty_x(5)
+        group_w("s", 1, 0, 320)
+        group_w("v", 1, 320, 512)
+        quant_x(3)
+        scale_x(4)
+        quant_w(1)
+        travel(0, 0)
+        travel(1, 0)
+        attract(0, 0)
+        attract(1, 0)
+        taste(2, 0)
+        turn_z(1)
+        empty_z(1)
+        quant_z(1)
+        scale_x(5)
+        taste(3, 0)
+        turn_z(2)
+        empty_z(2)
+        travel(0, 1)
+        travel(1, 1)
+        travel(2, 0)
+        travel(3, 0)
+        split_z(3)
+        attract(0, 1)
+        attract(1, 1)
+        attract(2, 0)
+        attract(3, 0)
+        cast(6, "v")
+        cast(7, "v")
+        quant_x(4, 2)
         quant_z(2)
-        widen(6)
-        widen(7)
-        quant_x(4)
-        quant_x(5)
-        utility(3, 0)
+        utility(2, 1)
         utility(3, 1)
         turn_x(6)
         turn_x(7)
-        widen(8)
-        empty_x(6)
-        empty_x(7)
-        widen(9)
-        split_x(8)
-        quant_x(6, 2)
-        split_x(9)
-        quant_z(3)
-        widen(10)
-        utility(4, 0)
-        utility(4, 1)
-        split_z(4)
-        utility(5, 0)
-        utility(5, 1)
-        turn_x(8)
-        turn_x(9)
-        turn_z(4)
-        empty_x(8)
-        empty_x(9)
-        empty_z(4)
-        widen(11)
-        split_x(10)
-        quant_x(8, 2)
-        split_x(11)
-        quant_z(4)
-        widen(12)
-        group_p(0, 0)
-        utility(6, 0)
-        utility(6, 1)
-        split_z(5)
-        utility(7, 0)
-        utility(7, 1)
-        turn_x(10)
-        turn_x(11)
-        turn_z(5)
-        empty_x(10)
-        empty_x(11)
-        empty_z(5)
-        widen(13)
-        split_x(12)
-        quant_x(10, 2)
-        split_x(13)
-        quant_z(5)
-        widen(14)
-        quant_p(0, 0)
-        utility(8, 0)
-        utility(8, 1)
-        utility(9, 0)
-        utility(9, 1)
-        turn_x(12)
-        turn_x(13)
-        turn_z(6)
-        empty_x(12)
-        empty_x(13)
-        empty_z(6)
-        widen(15)
-        split_x(14)
-        quant_x(12, 2)
-        split_x(15)
-        quant_z(6)
-        group_p(1, 0)
-        utility(10, 0)
-        utility(10, 1)
-        utility(11, 0)
-        utility(11, 1)
-        turn_x(14)
-        turn_x(15)
-        turn_z(7)
-        empty_x(14)
-        empty_x(15)
+        turn_z(3)
+        for n in range(2, 6):
+            empty_z(n + 1)
+            scale_x(2 * n + 2)
+            scale_x(2 * n + 3)
+            group_p((n - 2) // 2, 0, "g", 256 * (n % 2), 256 * (n % 2 + 1), after=n)
+            cast(2 * n + 4, "v")
+            cast(2 * n + 5, "v")
+            quant_z(n + 1)
+            quant_x(2 * n + 2, 2)
+            split_z(n + 2)
+            utility(2 * n, 0)
+            utility(2 * n, 1)
+            utility(2 * n + 1, 0)
+            group_p(0, 1, "s", 128 * (n - 2), 128 * (n - 1))
+            utility(2 * n + 1, 1)
+            turn_x(2 * n + 4)
+            turn_x(2 * n + 5)
+            turn_z(n + 2)
         empty_z(7)
+        scale_x(14)
+        scale_x(15)
+        group_p(1, 1, "g", 0, 256, after=6)
         nc.vector.tensor_copy(out=size_cols[:], in_=size_in[:, :, 0])
-        group_p(2, 0)
-        quant_x(14, 2)
         quant_z(7)
-        quant_p(1, 0)
-        group_p(0, 1)
+        quant_x(14, 2)
+        for c in (0, 256):
+            quant_p(0, 0, c, c + 256)
+        for c in (0, 256):
+            quant_p(1, 0, c, c + 256)
+        group_p(2, 0, "v", 0, 512)
+        for c in range(0, 512, 128):
+            quant_p(0, 1, c, c + 128)
         quant_p(2, 0)
-        group_p(1, 1)
         utility(12, 0)
         utility(13, 0)
+        group_p(1, 1, "s", 256, 512)
         utility(12, 1)
+        utility(13, 1)
         utility(14, 0)
         utility(15, 0)
-        utility(13, 1)
+        group_p(2, 1, "s", 0, 256)
         utility(14, 1)
         utility(15, 1)
-        group_p(2, 1, "s")
-        group_p(3, 0)
-        quant_p(0, 1)
+        group_p(2, 1, "s", 256, 512)
+        quant_p(1, 1, 0, 256)
+        group_p(3, 0, "v", 0, 512)
+        quant_p(1, 1, 256, 512)
         quant_p(3, 0)
-        quant_p(1, 1)
-        group_p(3, 1)
-        quant_p(2, 1)
+        group_p(3, 1, "v", 0, 512)
+        quant_p(2, 1, 0, 256)
+        quant_p(2, 1, 256, 512)
         quant_p(3, 1)
-        for jt in range(4):
-            flow_passes(jt, range(G - 1))
-        for jt in range(4):
-            flow_passes(jt, [G - 1])
-            finish(jt, "s")
-        for g in (0, 1, 2, 3):
-            for jt in range(4, 6):
+        for g in range(G):
+            for jt in range(4):
                 flow_passes(jt, [g])
                 if g == G - 1:
                     finish(jt, "s")
+        for jt in (4, 5):
+            flow_passes(jt, range(G - 1))
+        for jt in (4, 5):
+            flow_passes(jt, [G - 1])
+            finish(jt, "s" if jt == 4 else "v")
         flow_passes(6, range(G))
         finish(6, "s")
         last_flows(7, 2)

@@ -40,8 +40,16 @@ def tile_huff_retail_flows_s3_kernel(
         def rotating(name, shape, dtype, bufs):
             return work.tile(shape, dtype, name=name, tag=name, bufs=bufs, align_bytes=64)
 
-        def bank(ring):
-            return psum.tile([P, 512], F32, name=ring, tag=ring, bufs={"turned": 3, "sums": 5}[ring])
+        free_banks = ["bank%d" % k for k in range(8)]
+        bank_name = {}
+
+        def bank(key):
+            name = free_banks.pop(0)
+            bank_name[key] = name
+            return psum.tile([P, 512], F32, name=name, tag=name, bufs=1)
+
+        def release(key):
+            free_banks.append(bank_name[key])
 
         ident = kept("ident", [P, P], F32)
         a_in = kept("a_in", [P, G, 4], BF16)
@@ -52,7 +60,7 @@ def tile_huff_retail_flows_s3_kernel(
         warm = kept("warm", [P, 1], F32)
         ones = kept("ones", [P, 512], BF16)
         size_cols = kept("size_cols", [P, 8], F32)
-        v_sb = [kept("v_sb%d" % h, [P, 2, 2 * HALF], U8) for h in range(2)]
+        v_sb = kept("v_sb", [P, 2, 2 * J], U8)
         v_sc = kept("v_sc", [P, 2 * J], U8)
         y_sb = kept("y_sb", [P, G, 2 * C], U8)
         y_sc = kept("y_sc", [P, G * C], U8)
@@ -74,11 +82,6 @@ def tile_huff_retail_flows_s3_kernel(
 
         def load_w(h):
             nc.sync.dma_start(out=w_raw[h][:], in_=w.rearrange("(p t) j -> p t j", t=4)[:, :, h * HALF : (h + 1) * HALF])
-
-        def load_v(h):
-            nc.sync.dma_start(
-                out=v_sb[h][:], in_=v_words.rearrange("g p n -> p g n")[:, :, 2 * HALF * h : 2 * HALF * (h + 1)]
-            )
 
         def load_z(n):
             g, half = divmod(n, 2)
@@ -105,18 +108,21 @@ def tile_huff_retail_flows_s3_kernel(
             else:
                 nc.vector.tensor_copy(out=dst, in_=src)
 
-        def cast(i, engine):
-            x_bf[i] = rotating("x_bf", [P, K], BF16, 4)
-            src = x_raw[i // 2][:, (i % 2) * K : (i % 2 + 1) * K].bitcast(FP8)
-            x_apart[i] = engine == "v"
+        def cast(i, engine, c0=0, c1=2):
+            if c0 == 0:
+                x_bf[i] = rotating("x_bf", [P, K], BF16, 4)
+            dst = x_bf[i][:, 512 * c0 : 512 * c1]
+            src = x_raw[i // 2][:, (i % 2) * K + 512 * c0 : (i % 2) * K + 512 * c1].bitcast(FP8)
+            for c in range(c0, c1):
+                x_apart[i, c] = (c0, c1) if engine == "v" else None
             if engine == "v":
                 nc.vector.tensor_scalar(
-                    out=x_bf[i][:].rearrange("p (u m e) -> p m u e", u=2, e=2),
+                    out=dst.rearrange("p (u m e) -> p m u e", u=2, e=2),
                     in0=src.rearrange("p (m u e) -> p m u e", u=2, e=2),
                     scalar1=one[:], scalar2=None, op0=ALU.mult,
                 )
             else:
-                nc.scalar.copy(out=x_bf[i][:], in_=src)
+                nc.scalar.copy(out=dst, in_=src)
 
         def first_tile(c):
             if c == 0:
@@ -128,7 +134,7 @@ def tile_huff_retail_flows_s3_kernel(
                 in0=x_raw[0][:, 512 * c : 512 * (c + 1)].bitcast(FP8).rearrange("p (m u e) -> p m u e", u=2, e=2),
                 scalar1=one[:], scalar2=None, op0=ALU.mult,
             )
-            x_bank[0, c] = bank("turned")
+            x_bank[0, c] = bank(("x", 0, c))
             for u in range(2):
                 nc.tensor.transpose(x_bank[0, c][:, u * P : (u + 1) * P], half.bitcast(F32)[:, u * P : (u + 1) * P], ident[:])
 
@@ -139,6 +145,7 @@ def tile_huff_retail_flows_s3_kernel(
                 in1=xs_cols[:, c, :].rearrange("p (u e) -> p u e", u=2).unsqueeze(1).to_broadcast([P, P, 2, 2]),
                 op=ALU.mult,
             )
+            release(("x", 0, c))
 
         def first_quant(c):
             cols = slice(P * c, P * (c + 1))
@@ -153,21 +160,29 @@ def tile_huff_retail_flows_s3_kernel(
                 in_=z_raw[n][:].bitcast(F32).rearrange("p (m u) -> p m u", u=2),
             )
 
-        def turn(src, apart):
-            b = bank("turned")
+        def turn(key, src, apart):
+            b = bank(key)
             words = src.bitcast(F32)
             for c in range(2):
                 for u in range(2):
+                    if apart[c] is None:
+                        cols = words[:, 256 * c + u : 256 * (c + 1) : 2]
+                    else:
+                        c0, c1 = apart[c]
+                        first = 256 * c0 + P * ((c1 - c0) * u + c - c0)
+                        cols = words[:, first : first + P]
                     m = 2 * u + c
-                    cols = words[:, m * P : (m + 1) * P] if apart else words[:, 256 * c + u : 256 * (c + 1) : 2]
                     nc.tensor.transpose(b[:, m * P : (m + 1) * P], cols, ident[:])
             return b
 
         def turn_x(i):
-            x_bank[i] = turn(x_bf[i][:], x_apart[i])
+            x_bank[i] = turn(("x", i), x_bf[i][:], [x_apart[i, 0], x_apart[i, 1]])
 
         def turn_z(n):
-            z_bank[n] = turn(z_split[n][:], True) if n in z_split else turn(z_raw[n][:], False)
+            if n in z_split:
+                z_bank[n] = turn(("z", n), z_split[n][:], [(0, 2), (0, 2)])
+            else:
+                z_bank[n] = turn(("z", n), z_raw[n][:], [None, None])
 
         def scale_x(i):
             n, j = divmod(i, 2)
@@ -179,6 +194,7 @@ def tile_huff_retail_flows_s3_kernel(
                 in1=xs_cols[:].rearrange("p c (u e) -> p c u e", u=2).unsqueeze(2).to_broadcast([P, 2, P, 2, 2]),
                 op=ALU.mult,
             )
+            release(("x", i))
 
         def empty_z(n, engine="s"):
             z_grp[n] = rotating("z_grp", [P, K], BF16, 3)
@@ -187,6 +203,7 @@ def tile_huff_retail_flows_s3_kernel(
                 z_grp[n][:].bitcast(F32).rearrange("p (m u) -> p m u", u=2),
                 z_bank[n][:].rearrange("p (u m) -> p m u", u=2),
             )
+            release(("z", n))
 
         def quant_x(i, tiles=1):
             n, j = divmod(i, 2)
@@ -216,20 +233,20 @@ def tile_huff_retail_flows_s3_kernel(
 
         def taste(i, h, first=True):
             if first:
-                u_bank[i, h] = bank("sums")
+                u_bank[i, h] = bank(("u", i, h))
             for kg in range(2):
                 cols = slice((2 * (i % 2) + kg) * P, (2 * (i % 2) + kg + 1) * P)
                 nc.tensor.matmul_mx(
                     out=u_bank[i, h][:],
                     lhsT=x_q[i // 2][:, cols].bitcast(FP8X4), lhsT_scale=x_s[i // 2][:, cols],
-                    rhs=v_sb[h][:, kg, :].bitcast(FP4X4),
+                    rhs=v_sb[:, kg, 2 * HALF * h : 2 * HALF * (h + 1)].bitcast(FP4X4),
                     rhs_scale=v_sc[:, J * kg + HALF * h : J * kg + HALF * (h + 1)],
                     start=(first and kg == 0), stop=(not first and kg == 1),
                 )
 
         def travel(i, h, first=False):
             if first:
-                u_bank[i, h] = bank("sums")
+                u_bank[i, h] = bank(("u", i, h))
             cols = slice((i % 2) * P, (i % 2 + 1) * P)
             nc.tensor.matmul_mx(
                 out=u_bank[i, h][:],
@@ -245,31 +262,30 @@ def tile_huff_retail_flows_s3_kernel(
             nc.scalar.activation(
                 out=p_raw[g, h][:, t, :], in_=u_bank[i, h][:], func=ACT.Exp, bias=ln_a[:, i : i + 1], scale=1.0
             )
+            release(("u", i, h))
 
         def utility(i, h):
             taste(i, h)
             travel(i, h)
             attract(i, h)
 
-        def group_p(g, h, engine, c0, c1, after=None):
-            if after is None:
-                p_grp[g, h, c0] = rotating("p_grp%d" % (c1 - c0), [P, c1 - c0, 4], BF16, {128: 4, 256: 3, 512: 2}[c1 - c0])[:]
-            else:
-                p_grp[g, h, c0] = x_grp[after][:, 0 : 4 * (c1 - c0)].rearrange("p (n t) -> p n t", t=4)
-            group4(engine, p_grp[g, h, c0], p_raw[g, h][:, :, c0:c1])
+        def group_p(g, h, engine, c0=0, c1=HALF, after=None):
+            if (g, h) not in p_grp:
+                if after is None:
+                    p_grp[g, h] = rotating("p_grp", [P, 4 * HALF], BF16, 3)
+                else:
+                    p_grp[g, h] = x_grp[after]
+            group4(engine, p_grp[g, h][:].rearrange("p (n t) -> p n t", t=4)[:, c0:c1, :], p_raw[g, h][:, :, c0:c1])
 
-        def quant_p(g, h, c0=0, c1=HALF):
-            nc.vector.quantize_mx(
-                out=p_q[g][h][:, c0:c1].bitcast(FP8X4), scales=p_s[g][h][:, c0:c1],
-                in_=p_grp[g, h, c0].rearrange("p n t -> p (n t)"),
-            )
+        def quant_p(g, h):
+            nc.vector.quantize_mx(out=p_q[g][h][:].bitcast(FP8X4), scales=p_s[g][h][:], in_=p_grp[g, h][:])
 
         def flow_passes(jt, groups):
             h, c = divmod(jt, 4)
             cols = slice(c * P, (c + 1) * P)
             for g in groups:
                 if g == 0:
-                    f_bank[jt] = bank("turned" if 1 <= jt <= 3 else "sums")
+                    f_bank[jt] = bank(("f", jt))
                 nc.tensor.matmul_mx(
                     out=f_bank[jt][:],
                     lhsT=p_q[g][h][:, cols].bitcast(FP8X4), lhsT_scale=p_s[g][h][:, cols],
@@ -284,6 +300,7 @@ def tile_huff_retail_flows_s3_kernel(
                 nc.scalar.activation(out=o[:], in_=f_bank[jt][:], func=ACT.Copy, scale=factor)
             else:
                 nc.vector.tensor_scalar(out=o[:], in0=f_bank[jt][:], scalar1=factor, scalar2=None, op0=ALU.mult)
+            release(("f", jt))
             nc.sync.dma_start(out=out[jt * P : (jt + 1) * P, :], in_=o[:])
 
         def last_flows(jt, parts):
@@ -292,7 +309,7 @@ def tile_huff_retail_flows_s3_kernel(
             o = rotating("o_sb", [P, C], F32, 6)
             width = C // parts
             for part in range(parts):
-                b = bank("turned")
+                b = bank(("f", jt, part))
                 for n0 in range(0, width, P):
                     c0 = part * width + n0
                     for g in range(G):
@@ -313,9 +330,10 @@ def tile_huff_retail_flows_s3_kernel(
                 nc.sync.dma_start(out=out[jt * P : (jt + 1) * P, span], in_=o[:, span])
 
         def keep_warm(count):
-            b = bank("sums")
+            b = bank("warm")
             for k in range(count):
                 nc.tensor.matmul(out=b[:], lhsT=ones[:, 0:P], rhs=ones[:], start=True, stop=True)
+            release("warm")
 
         nc.scalar.dma_start(out=a_in[:], in_=a.rearrange("(g p t) -> p g t", p=P, t=4))
         nc.vector.memset(ones[:], 1.0)
@@ -328,16 +346,15 @@ def tile_huff_retail_flows_s3_kernel(
         nc.sync.dma_start(out=xs_cols[:], in_=x_scale.rearrange("o (g p t) -> p (o g) t", g=2, t=4))
         load_x(0, 1, 2)
         load_z(0)
-        load_scales(v_sc, v_scales, 2)
-        load_v(0)
         load_x(1)
-        load_w(0)
-        load_v(1)
+        load_scales(v_sc, v_scales, 2)
+        nc.sync.dma_start(out=v_sb[:], in_=v_words.rearrange("g p n -> p g n"))
         load_x(2)
+        load_w(0)
         load_w(1)
         load_z(1)
-        load_z(2)
         load_x(3)
+        load_z(2)
         load_z(3)
         for n in range(4, PAIRS):
             load_x(n)
@@ -349,137 +366,122 @@ def tile_huff_retail_flows_s3_kernel(
 
         nc.scalar.activation(out=ln_a[:], in_=a_in[:].rearrange("p g t -> p (g t)"), func=ACT.Ln)
         nc.scalar.activation(out=warm[:], in_=warm[:], func=ACT.Exp)
-        keep_warm(3)
+        keep_warm(4)
         first_tile(0)
         first_tile(1)
-        keep_warm(2)
         cast(1, "v")
+        cast(2, "s")
+        cast(3, "s")
         turn_z(0)
+        keep_warm(2)
         empty_z(0)
         first_scale(0)
         turn_x(1)
-        keep_warm(1)
         first_scale(1)
         first_quant(0)
         first_quant(1)
+        turn_x(2)
         scale_x(1)
         quant_z(0)
         quant_x(1)
-        cast(2, "s")
-        cast(3, "s")
         taste(0, 0)
-        turn_x(2)
+        taste(0, 1)
         turn_x(3)
         scale_x(2)
-        group_w("s", 0, 0, 256)
-        group_w("v", 0, 256, 512)
-        quant_x(2)
-        quant_w(0)
         scale_x(3)
         cast(4, "s")
         cast(5, "s")
+        group_w("g", 0, 256, 512)
+        group_w("s", 0, 0, 256)
+        group_w("s", 1, 0, 256)
         taste(1, 0)
-        taste(0, 1)
-        taste(1, 1)
         turn_x(4)
+        taste(1, 1)
         turn_x(5)
-        group_w("s", 1, 0, 320)
-        group_w("v", 1, 320, 512)
-        quant_x(3)
-        scale_x(4)
-        quant_w(1)
+        turn_z(1)
+        empty_z(1)
+        group_w("s", 1, 256, 512)
+        quant_w(0)
+        quant_x(2, 2)
+        quant_z(1)
         travel(0, 0)
         travel(1, 0)
         attract(0, 0)
+        scale_x(4)
         attract(1, 0)
-        taste(2, 0)
-        turn_z(1)
-        empty_z(1)
-        quant_z(1)
-        scale_x(5)
-        taste(3, 0)
+        quant_w(1)
+        utility(2, 0)
+        utility(3, 0)
         turn_z(2)
         empty_z(2)
+        scale_x(5)
+        split_z(3)
         travel(0, 1)
         travel(1, 1)
-        travel(2, 0)
-        travel(3, 0)
-        split_z(3)
         attract(0, 1)
         attract(1, 1)
-        attract(2, 0)
-        attract(3, 0)
         cast(6, "v")
         cast(7, "v")
-        quant_x(4, 2)
         quant_z(2)
+        quant_x(4, 2)
         utility(2, 1)
         utility(3, 1)
         turn_x(6)
         turn_x(7)
         turn_z(3)
-        for n in range(2, 6):
+        for n in range(2, 7):
+            g, h = divmod(n - 2, 2)
             empty_z(n + 1)
             scale_x(2 * n + 2)
             scale_x(2 * n + 3)
-            group_p((n - 2) // 2, 0, "g", 256 * (n % 2), 256 * (n % 2 + 1), after=n)
-            cast(2 * n + 4, "v")
-            cast(2 * n + 5, "v")
+            group_p(g, h, "g", 0, 288, after=n)
+            if n < 6:
+                cast(2 * n + 4, "v")
+                cast(2 * n + 5, "v", 0, 1)
             quant_z(n + 1)
             quant_x(2 * n + 2, 2)
-            split_z(n + 2)
+            if n < 6:
+                cast(2 * n + 5, "s", 1, 2)
+                split_z(n + 2)
             utility(2 * n, 0)
-            utility(2 * n, 1)
             utility(2 * n + 1, 0)
-            group_p(0, 1, "s", 128 * (n - 2), 128 * (n - 1))
+            group_p(g, h, "s", 288, 416 if n < 6 else HALF)
+            utility(2 * n, 1)
             utility(2 * n + 1, 1)
-            turn_x(2 * n + 4)
-            turn_x(2 * n + 5)
-            turn_z(n + 2)
-        empty_z(7)
-        scale_x(14)
-        scale_x(15)
-        group_p(1, 1, "g", 0, 256, after=6)
+            if n < 6:
+                turn_x(2 * n + 4)
+                turn_x(2 * n + 5)
+                turn_z(n + 2)
         nc.vector.tensor_copy(out=size_cols[:], in_=size_in[:, :, 0])
-        quant_z(7)
-        quant_x(14, 2)
-        for c in (0, 256):
-            quant_p(0, 0, c, c + 256)
-        for c in (0, 256):
-            quant_p(1, 0, c, c + 256)
-        group_p(2, 0, "v", 0, 512)
-        for c in range(0, 512, 128):
-            quant_p(0, 1, c, c + 128)
-        quant_p(2, 0)
-        utility(12, 0)
-        utility(13, 0)
-        group_p(1, 1, "s", 256, 512)
-        utility(12, 1)
-        utility(13, 1)
+        for g in range(2):
+            group_p(g, 0, "v", 416, HALF)
+        for g in range(3):
+            quant_p(g, 0)
+        for g in range(2):
+            group_p(g, 1, "v", 416, HALF)
         utility(14, 0)
         utility(15, 0)
         group_p(2, 1, "s", 0, 256)
         utility(14, 1)
         utility(15, 1)
         group_p(2, 1, "s", 256, 512)
-        quant_p(1, 1, 0, 256)
-        group_p(3, 0, "v", 0, 512)
-        quant_p(1, 1, 256, 512)
+        group_p(3, 0, "v")
+        quant_p(0, 1)
         quant_p(3, 0)
-        group_p(3, 1, "v", 0, 512)
-        quant_p(2, 1, 0, 256)
-        quant_p(2, 1, 256, 512)
+        quant_p(1, 1)
+        group_p(3, 1, "v")
+        quant_p(2, 1)
         quant_p(3, 1)
         for g in range(G):
             for jt in range(4):
                 flow_passes(jt, [g])
                 if g == G - 1:
                     finish(jt, "s")
-        for jt in (4, 5):
-            flow_passes(jt, range(G - 1))
-        for jt in (4, 5):
-            flow_passes(jt, [G - 1])
-            finish(jt, "s" if jt == 4 else "v")
+        for g in range(G):
+            for jt in (4, 5):
+                flow_passes(jt, [g])
+                if g == G - 1:
+                    finish(jt, "s" if jt == 4 else "v")
         flow_passes(6, range(G))
         finish(6, "s")
         last_flows(7, 2)

@@ -65,7 +65,7 @@ def tile_huff_retail_flows_s3_kernel(
         y_sb = kept("y_sb", [P, G, 2 * C], U8)
         y_sc = kept("y_sc", [P, G * C], U8)
         w_raw = [kept("w_raw%d" % h, [P, 4, HALF], BF16) for h in range(2)]
-        w_grp = [kept("w_grp%d" % h, [P, HALF, 4], BF16) for h in range(2)]
+        w_grp = kept("w_grp", [P, 4 * 256], BF16)
         w_q = [kept("w_q%d" % h, [P, HALF], U32) for h in range(2)]
         w_s = [kept("w_s%d" % h, [P, HALF], U8) for h in range(2)]
         z_raw = [kept("z_raw%d" % n, [P, 2 * D], BF16) for n in range(PAIRS)]
@@ -220,15 +220,17 @@ def tile_huff_retail_flows_s3_kernel(
                 nc.gpsimd.tensor_scalar(
                     out=dst, in0=src.rearrange("p t n -> p n t"), scalar1=1.0, scalar2=0.0, op0=ALU.mult, op1=ALU.add
                 )
+            elif engine == "s":
+                nc.scalar.copy(out=dst, in_=src.rearrange("p t n -> p n t"))
             else:
                 copy(engine, dst.rearrange("p (c i) t -> p c t i", i=4), src.rearrange("p t (c i) -> p c t i", i=4))
 
-        def group_w(engine, h, c0, c1):
-            group4(engine, w_grp[h][:, c0:c1, :], w_raw[h][:, :, c0:c1])
+        def group_w(engine, h, c0, c1, room):
+            group4(engine, room[:].rearrange("p (n t) -> p n t", t=4)[:, c0:c1, :], w_raw[h][:, :, c0:c1])
 
-        def quant_w(h):
+        def quant_w(h, c0, c1, room):
             nc.vector.quantize_mx(
-                out=w_q[h][:].bitcast(FP8X4), scales=w_s[h][:], in_=w_grp[h][:].rearrange("p n t -> p (n t)")
+                out=w_q[h][:, c0:c1].bitcast(FP8X4), scales=w_s[h][:, c0:c1], in_=room[:, 4 * c0 : 4 * c1]
             )
 
         def taste(i, h, first=True):
@@ -351,8 +353,8 @@ def tile_huff_retail_flows_s3_kernel(
         nc.sync.dma_start(out=v_sb[:], in_=v_words.rearrange("g p n -> p g n"))
         load_x(2)
         load_w(0)
-        load_w(1)
         load_z(1)
+        load_w(1)
         load_x(3)
         load_z(2)
         load_z(3)
@@ -391,41 +393,41 @@ def tile_huff_retail_flows_s3_kernel(
         scale_x(3)
         cast(4, "s")
         cast(5, "s")
-        group_w("g", 0, 256, 512)
-        group_w("s", 0, 0, 256)
-        group_w("s", 1, 0, 256)
+        group_w("g", 0, 192, 512, x_grp[0])
+        group_w("s", 0, 0, 192, x_grp[0])
         taste(1, 0)
         turn_x(4)
-        taste(1, 1)
-        turn_x(5)
         turn_z(1)
         empty_z(1)
-        group_w("s", 1, 256, 512)
-        quant_w(0)
-        quant_x(2, 2)
+        taste(1, 1)
+        turn_x(5)
+        group_w("s", 1, 0, 256, w_grp)
+        quant_w(0, 0, 512, x_grp[0])
         quant_z(1)
+        quant_x(2, 2)
+        group_w("g", 1, 256, 512, x_grp[1])
         travel(0, 0)
         travel(1, 0)
         attract(0, 0)
         scale_x(4)
         attract(1, 0)
-        quant_w(1)
         utility(2, 0)
         utility(3, 0)
+        scale_x(5)
+        quant_w(1, 0, 256, w_grp)
+        quant_w(1, 256, 512, x_grp[1])
         turn_z(2)
         empty_z(2)
-        scale_x(5)
         split_z(3)
-        travel(0, 1)
-        travel(1, 1)
-        attract(0, 1)
-        attract(1, 1)
+        taste(2, 1)
+        taste(3, 1)
+        for i in range(4):
+            travel(i, 1)
+            attract(i, 1)
         cast(6, "v")
         cast(7, "v")
         quant_z(2)
         quant_x(4, 2)
-        utility(2, 1)
-        utility(3, 1)
         turn_x(6)
         turn_x(7)
         turn_z(3)
@@ -434,7 +436,7 @@ def tile_huff_retail_flows_s3_kernel(
             empty_z(n + 1)
             scale_x(2 * n + 2)
             scale_x(2 * n + 3)
-            group_p(g, h, "g", 0, 288, after=n)
+            group_p(g, h, "g", 0, 352, after=n)
             if n < 6:
                 cast(2 * n + 4, "v")
                 cast(2 * n + 5, "v", 0, 1)
@@ -445,7 +447,7 @@ def tile_huff_retail_flows_s3_kernel(
                 split_z(n + 2)
             utility(2 * n, 0)
             utility(2 * n + 1, 0)
-            group_p(g, h, "s", 288, 416 if n < 6 else HALF)
+            group_p(g, h, "s", 352, 384 if n < 6 else HALF)
             utility(2 * n, 1)
             utility(2 * n + 1, 1)
             if n < 6:
@@ -454,22 +456,21 @@ def tile_huff_retail_flows_s3_kernel(
                 turn_z(n + 2)
         nc.vector.tensor_copy(out=size_cols[:], in_=size_in[:, :, 0])
         for g in range(2):
-            group_p(g, 0, "v", 416, HALF)
+            group_p(g, 0, "v", 384, HALF)
         for g in range(3):
             quant_p(g, 0)
         for g in range(2):
-            group_p(g, 1, "v", 416, HALF)
+            group_p(g, 1, "v", 384, HALF)
         utility(14, 0)
         utility(15, 0)
-        group_p(2, 1, "s", 0, 256)
         utility(14, 1)
         utility(15, 1)
-        group_p(2, 1, "s", 256, 512)
+        group_p(2, 1, "s")
         group_p(3, 0, "v")
         quant_p(0, 1)
         quant_p(3, 0)
-        quant_p(1, 1)
         group_p(3, 1, "v")
+        quant_p(1, 1)
         quant_p(2, 1)
         quant_p(3, 1)
         for g in range(G):

@@ -60,7 +60,7 @@ def tile_huff_retail_flows_s3_kernel(
         warm = kept("warm", [P, 1], F32)
         ones = kept("ones", [P, 512], BF16)
         size_cols = kept("size_cols", [P, 8], F32)
-        v_sb = kept("v_sb", [P, 2, 2 * J], U8)
+        v_sb = [kept("v_sb%d" % h, [P, 2, 2 * HALF], U8) for h in range(2)]
         v_sc = kept("v_sc", [P, 2 * J], U8)
         y_sb = kept("y_sb", [P, G, 2 * C], U8)
         y_sc = kept("y_sc", [P, G * C], U8)
@@ -83,6 +83,11 @@ def tile_huff_retail_flows_s3_kernel(
         def load_w(h):
             nc.sync.dma_start(out=w_raw[h][:], in_=w.rearrange("(p t) j -> p t j", t=4)[:, :, h * HALF : (h + 1) * HALF])
 
+        def load_v(h):
+            nc.sync.dma_start(
+                out=v_sb[h][:], in_=v_words.rearrange("g p n -> p g n")[:, :, 2 * HALF * h : 2 * HALF * (h + 1)]
+            )
+
         def load_z(n):
             g, half = divmod(n, 2)
             src = z[512 * g : 512 * (g + 1), :].rearrange("(p t) k -> p (t k)", t=4)
@@ -96,10 +101,10 @@ def tile_huff_retail_flows_s3_kernel(
             )
 
         def load_scales(tile, src, groups):
-            for r in range(4):
+            for q in range(4):
                 nc.sync.dma_start(
-                    out=tile[r:P:32, :].bitcast(I32).rearrange("q (g n) -> q g n", g=groups),
-                    in_=src.bitcast(I32).rearrange("g (q r) n -> r q g n", r=4)[r],
+                    out=tile[32 * q : 32 * q + 4, :].bitcast(I32).rearrange("r (g n) -> r g n", g=groups),
+                    in_=src.bitcast(I32).rearrange("g (q r) n -> q r g n", r=4)[q],
                 )
 
         def copy(engine, dst, src):
@@ -241,7 +246,7 @@ def tile_huff_retail_flows_s3_kernel(
                 nc.tensor.matmul_mx(
                     out=u_bank[i, h][:],
                     lhsT=x_q[i // 2][:, cols].bitcast(FP8X4), lhsT_scale=x_s[i // 2][:, cols],
-                    rhs=v_sb[:, kg, 2 * HALF * h : 2 * HALF * (h + 1)].bitcast(FP4X4),
+                    rhs=v_sb[h][:, kg, :].bitcast(FP4X4),
                     rhs_scale=v_sc[:, J * kg + HALF * h : J * kg + HALF * (h + 1)],
                     start=(first and kg == 0), stop=(not first and kg == 1),
                 )
@@ -350,7 +355,8 @@ def tile_huff_retail_flows_s3_kernel(
         load_z(0)
         load_x(1)
         load_scales(v_sc, v_scales, 2)
-        nc.sync.dma_start(out=v_sb[:], in_=v_words.rearrange("g p n -> p g n"))
+        load_v(0)
+        load_v(1)
         load_x(2)
         load_w(0)
         load_z(1)
@@ -446,9 +452,9 @@ def tile_huff_retail_flows_s3_kernel(
                 cast(2 * n + 5, "s", 1, 2)
                 split_z(n + 2)
             utility(2 * n, 0)
-            utility(2 * n + 1, 0)
-            group_p(g, h, "s", 352, 384 if n < 6 else HALF)
             utility(2 * n, 1)
+            group_p(g, h, "s", 352, 384 if n < 6 else HALF)
+            utility(2 * n + 1, 0)
             utility(2 * n + 1, 1)
             if n < 6:
                 turn_x(2 * n + 4)

@@ -58,14 +58,14 @@ def tile_huff_retail_flows_s3_kernel(
         one = kept("one", [P, 1], F32)
         size_in = kept("size_in", [P, 8, 2], BF16)
         warm = kept("warm", [P, 1], F32)
-        ones = kept("ones", [P, 512], BF16)
+        ones = kept("ones", [P, 256], F32)
         size_cols = kept("size_cols", [P, 8], F32)
         v_sb = [kept("v_sb%d" % h, [P, 2, 2 * HALF], U8) for h in range(2)]
         v_sc = kept("v_sc", [P, 2 * J], U8)
         y_sb = kept("y_sb", [P, G, 2 * C], U8)
         y_sc = kept("y_sc", [P, G * C], U8)
         w_raw = [kept("w_raw%d" % h, [P, 4, HALF], BF16) for h in range(2)]
-        w_grp = kept("w_grp", [P, 4 * 256], BF16)
+        w_all = kept("w_all", [P, 4 * HALF], BF16)
         w_q = [kept("w_q%d" % h, [P, HALF], U32) for h in range(2)]
         w_s = [kept("w_s%d" % h, [P, HALF], U8) for h in range(2)]
         z_raw = [kept("z_raw%d" % n, [P, 2 * D], BF16) for n in range(PAIRS)]
@@ -128,35 +128,6 @@ def tile_huff_retail_flows_s3_kernel(
                 )
             else:
                 nc.scalar.copy(out=dst, in_=src)
-
-        def first_tile(c):
-            if c == 0:
-                x_bf[0] = rotating("x_bf", [P, K], BF16, 4)
-                x_grp[0] = kept("x_grp0", [P, 2 * K], BF16)
-            half = x_bf[0][:, 512 * c : 512 * (c + 1)]
-            nc.vector.tensor_scalar(
-                out=half.rearrange("p (u m e) -> p m u e", u=2, e=2),
-                in0=x_raw[0][:, 512 * c : 512 * (c + 1)].bitcast(FP8).rearrange("p (m u e) -> p m u e", u=2, e=2),
-                scalar1=one[:], scalar2=None, op0=ALU.mult,
-            )
-            x_bank[0, c] = bank(("x", 0, c))
-            for u in range(2):
-                nc.tensor.transpose(x_bank[0, c][:, u * P : (u + 1) * P], half.bitcast(F32)[:, u * P : (u + 1) * P], ident[:])
-
-        def first_scale(c):
-            nc.vector.tensor_tensor(
-                out=x_grp[0][:, 512 * c : 512 * (c + 1)].rearrange("p (h u e) -> p h u e", u=2, e=2),
-                in0=x_bank[0, c][:, 0:256].bitcast(BF16).rearrange("p (u h e) -> p h u e", u=2, e=2),
-                in1=xs_cols[:, c, :].rearrange("p (u e) -> p u e", u=2).unsqueeze(1).to_broadcast([P, P, 2, 2]),
-                op=ALU.mult,
-            )
-            release(("x", 0, c))
-
-        def first_quant(c):
-            cols = slice(P * c, P * (c + 1))
-            nc.vector.quantize_mx(
-                out=x_q[0][:, cols].bitcast(FP8X4), scales=x_s[0][:, cols], in_=x_grp[0][:, 512 * c : 512 * (c + 1)]
-            )
 
         def split_z(n):
             z_split[n] = rotating("z_split", [P, K], BF16, 2)
@@ -339,7 +310,7 @@ def tile_huff_retail_flows_s3_kernel(
         def keep_warm(count):
             b = bank("warm")
             for k in range(count):
-                nc.tensor.matmul(out=b[:], lhsT=ones[:, 0:P], rhs=ones[:], start=True, stop=True)
+                nc.tensor.matmul(out=b[:, 0:256], lhsT=ones[:, 0:P], rhs=ones[:], start=True, stop=True)
             release("warm")
 
         nc.scalar.dma_start(out=a_in[:], in_=a.rearrange("(g p t) -> p g t", p=P, t=4))
@@ -349,17 +320,16 @@ def tile_huff_retail_flows_s3_kernel(
         nc.vector.memset(warm[:], 1.0)
         nc.vector.memset(y_sc[:].bitcast(I32), 0)
         make_identity(nc, ident[:])
-        load_x(0, 0, 1)
+        load_x(0)
         nc.sync.dma_start(out=xs_cols[:], in_=x_scale.rearrange("o (g p t) -> p (o g) t", g=2, t=4))
-        load_x(0, 1, 2)
-        load_z(0)
         load_x(1)
+        load_z(0)
+        load_w(0)
+        load_x(2)
+        load_z(1)
         load_scales(v_sc, v_scales, 2)
         load_v(0)
         load_v(1)
-        load_x(2)
-        load_w(0)
-        load_z(1)
         load_w(1)
         load_x(3)
         load_z(2)
@@ -371,69 +341,65 @@ def tile_huff_retail_flows_s3_kernel(
         nc.sync.dma_start(out=y_sb[:], in_=y_words.rearrange("g p n -> p g n"))
         with nc.allow_non_contiguous_dma(reason="one factor a partition for each tile of 128 stores"):
             nc.sync.dma_start(out=size_in[:, :, 0], in_=size.rearrange("(c p) -> p c", p=P))
-
         nc.scalar.activation(out=ln_a[:], in_=a_in[:].rearrange("p g t -> p (g t)"), func=ACT.Ln)
-        nc.scalar.activation(out=warm[:], in_=warm[:], func=ACT.Exp)
-        keep_warm(4)
-        first_tile(0)
-        first_tile(1)
+        keep_warm(2)
+        cast(0, "v")
         cast(1, "v")
         cast(2, "s")
         cast(3, "s")
-        turn_z(0)
-        keep_warm(2)
-        empty_z(0)
-        first_scale(0)
+        turn_x(0)
         turn_x(1)
-        first_scale(1)
-        first_quant(0)
-        first_quant(1)
-        turn_x(2)
+        keep_warm(1)
+        scale_x(0)
         scale_x(1)
-        quant_z(0)
-        quant_x(1)
-        taste(0, 0)
-        taste(0, 1)
+        group_w("g", 0, 128, 512, w_all)
+        group_w("s", 0, 0, 128, w_all)
+        turn_z(0)
+        empty_z(0)
+        turn_x(2)
         turn_x(3)
+        keep_warm(1)
+        turn_z(1)
         scale_x(2)
-        scale_x(3)
         cast(4, "s")
         cast(5, "s")
-        group_w("g", 0, 192, 512, x_grp[0])
-        group_w("s", 0, 0, 192, x_grp[0])
-        taste(1, 0)
-        turn_x(4)
-        turn_z(1)
         empty_z(1)
-        taste(1, 1)
-        turn_x(5)
-        group_w("s", 1, 0, 256, w_grp)
-        quant_w(0, 0, 512, x_grp[0])
+        nc.scalar.activation(out=warm[:], in_=warm[:], func=ACT.Exp)
+        quant_z(0)
+        quant_w(0, 0, 512, w_all)
         quant_z(1)
+        quant_x(0, 2)
+        turn_x(4)
+        turn_x(5)
+        scale_x(3)
         quant_x(2, 2)
-        group_w("g", 1, 256, 512, x_grp[1])
-        travel(0, 0)
-        travel(1, 0)
+        for i in range(4):
+            travel(i, 0, True)
+        taste(0, 0, False)
         attract(0, 0)
-        scale_x(4)
+        taste(1, 0, False)
         attract(1, 0)
-        utility(2, 0)
-        utility(3, 0)
+        taste(0, 1)
+        scale_x(4)
         scale_x(5)
-        quant_w(1, 0, 256, w_grp)
-        quant_w(1, 256, 512, x_grp[1])
+        group_w("g", 1, 320, 512, x_grp[1])
+        group_w("s", 1, 0, 320, x_grp[1])
+        taste(2, 0, False)
+        taste(3, 0, False)
+        attract(2, 0)
+        attract(3, 0)
+        quant_w(1, 0, 512, x_grp[1])
+        cast(6, "v")
+        cast(7, "v")
+        for i in range(1, 4):
+            taste(i, 1)
         turn_z(2)
-        empty_z(2)
-        split_z(3)
-        taste(2, 1)
-        taste(3, 1)
+        empty_z(2, "v")
         for i in range(4):
             travel(i, 1)
             attract(i, 1)
-        cast(6, "v")
-        cast(7, "v")
-        quant_z(2)
         quant_x(4, 2)
+        quant_z(2)
         turn_x(6)
         turn_x(7)
         turn_z(3)

@@ -196,8 +196,6 @@ def tile_huff_retail_flows_s3_kernel(
                 nc.gpsimd.tensor_scalar(
                     out=dst, in0=src.rearrange("p t n -> p n t"), scalar1=1.0, scalar2=0.0, op0=ALU.mult, op1=ALU.add
                 )
-            elif engine == "s":
-                nc.scalar.copy(out=dst, in_=src.rearrange("p t n -> p n t"))
             else:
                 copy(engine, dst.rearrange("p (c i) t -> p c t i", i=4), src.rearrange("p t (c i) -> p c t i", i=4))
 
@@ -323,8 +321,8 @@ def tile_huff_retail_flows_s3_kernel(
         load_x(0)
         nc.sync.dma_start(out=xs_cols[:], in_=x_scale.rearrange("o (g p t) -> p (o g) t", g=2, t=4))
         load_x(1)
-        load_z(0)
         load_w(0)
+        load_z(0)
         load_x(2)
         load_z(1)
         load_scales(v_sc, v_scales, 2)
@@ -342,57 +340,58 @@ def tile_huff_retail_flows_s3_kernel(
         with nc.allow_non_contiguous_dma(reason="one factor a partition for each tile of 128 stores"):
             nc.sync.dma_start(out=size_in[:, :, 0], in_=size.rearrange("(c p) -> p c", p=P))
         nc.scalar.activation(out=ln_a[:], in_=a_in[:].rearrange("p g t -> p (g t)"), func=ACT.Ln)
-        keep_warm(2)
+        nc.scalar.activation(out=warm[:], in_=warm[:], func=ACT.Exp)
+        keep_warm(3)
         cast(0, "v")
         cast(1, "v")
-        cast(2, "s")
-        cast(3, "s")
         turn_x(0)
         turn_x(1)
+        cast(2, "v")
+        cast(3, "v")
         keep_warm(1)
         scale_x(0)
+        turn_x(2)
+        turn_x(3)
         scale_x(1)
         group_w("g", 0, 128, 512, w_all)
         group_w("s", 0, 0, 128, w_all)
-        turn_z(0)
-        empty_z(0)
-        turn_x(2)
-        turn_x(3)
-        keep_warm(1)
-        turn_z(1)
         scale_x(2)
+        turn_z(0)
+        keep_warm(1)
+        empty_z(0)
         cast(4, "s")
         cast(5, "s")
-        empty_z(1)
-        nc.scalar.activation(out=warm[:], in_=warm[:], func=ACT.Exp)
-        quant_z(0)
         quant_w(0, 0, 512, w_all)
-        quant_z(1)
+        quant_z(0)
         quant_x(0, 2)
+        turn_z(1)
+        keep_warm(1)
         turn_x(4)
         turn_x(5)
+        empty_z(1)
         scale_x(3)
+        travel(0, 0, True)
+        travel(1, 0, True)
+        quant_z(1)
         quant_x(2, 2)
-        for i in range(4):
-            travel(i, 0, True)
         taste(0, 0, False)
         attract(0, 0)
         taste(1, 0, False)
         attract(1, 0)
         taste(0, 1)
+        taste(1, 1)
         scale_x(4)
         scale_x(5)
         group_w("g", 1, 320, 512, x_grp[1])
-        group_w("s", 1, 0, 320, x_grp[1])
-        taste(2, 0, False)
-        taste(3, 0, False)
-        attract(2, 0)
-        attract(3, 0)
-        quant_w(1, 0, 512, x_grp[1])
+        group_w("s", 1, 128, 320, x_grp[1])
+        group_w("v", 1, 0, 128, x_grp[1])
+        utility(2, 0)
+        utility(3, 0)
         cast(6, "v")
+        quant_w(1, 0, 512, x_grp[1])
         cast(7, "v")
-        for i in range(1, 4):
-            taste(i, 1)
+        taste(2, 1)
+        taste(3, 1)
         turn_z(2)
         empty_z(2, "v")
         for i in range(4):

@@ -58,7 +58,7 @@ def tile_huff_retail_flows_s3_kernel(
         one = kept("one", [P, 1], F32)
         size_in = kept("size_in", [P, 8, 2], BF16)
         warm = kept("warm", [P, 1], F32)
-        ones = kept("ones", [P, 256], F32)
+        ones = kept("ones", [P, 512], BF16)
         size_cols = kept("size_cols", [P, 8], F32)
         v_sb = [kept("v_sb%d" % h, [P, 2, 2 * HALF], U8) for h in range(2)]
         v_sc = kept("v_sc", [P, 2 * J], U8)
@@ -308,16 +308,16 @@ def tile_huff_retail_flows_s3_kernel(
         def keep_warm(count):
             b = bank("warm")
             for k in range(count):
-                nc.tensor.matmul(out=b[:, 0:256], lhsT=ones[:, 0:P], rhs=ones[:], start=True, stop=True)
+                nc.tensor.matmul(out=b[:], lhsT=ones[:, 0:P], rhs=ones[:], start=True, stop=True)
             release("warm")
 
         nc.scalar.dma_start(out=a_in[:], in_=a.rearrange("(g p t) -> p g t", p=P, t=4))
-        nc.vector.memset(ones[:], 1.0)
         nc.vector.memset(v_sc[:].bitcast(I32), 0)
         nc.vector.memset(one[:], 1.0)
         nc.vector.memset(warm[:], 1.0)
         nc.vector.memset(y_sc[:].bitcast(I32), 0)
         make_identity(nc, ident[:])
+        nc.gpsimd.memset(ones[:], 1.0)
         load_x(0)
         nc.sync.dma_start(out=xs_cols[:], in_=x_scale.rearrange("o (g p t) -> p (o g) t", g=2, t=4))
         load_x(1)
@@ -341,14 +341,14 @@ def tile_huff_retail_flows_s3_kernel(
             nc.sync.dma_start(out=size_in[:, :, 0], in_=size.rearrange("(c p) -> p c", p=P))
         nc.scalar.activation(out=ln_a[:], in_=a_in[:].rearrange("p g t -> p (g t)"), func=ACT.Ln)
         nc.scalar.activation(out=warm[:], in_=warm[:], func=ACT.Exp)
-        keep_warm(3)
+        keep_warm(2)
         cast(0, "v")
         cast(1, "v")
         turn_x(0)
         turn_x(1)
+        keep_warm(2)
         cast(2, "v")
         cast(3, "v")
-        keep_warm(1)
         scale_x(0)
         turn_x(2)
         turn_x(3)
@@ -357,7 +357,7 @@ def tile_huff_retail_flows_s3_kernel(
         group_w("s", 0, 0, 128, w_all)
         scale_x(2)
         turn_z(0)
-        keep_warm(1)
+        keep_warm(2)
         empty_z(0)
         cast(4, "s")
         cast(5, "s")
@@ -365,7 +365,7 @@ def tile_huff_retail_flows_s3_kernel(
         quant_z(0)
         quant_x(0, 2)
         turn_z(1)
-        keep_warm(1)
+        keep_warm(2)
         turn_x(4)
         turn_x(5)
         empty_z(1)

@@ -129,6 +129,29 @@ def tile_huff_retail_flows_s3_kernel(
             else:
                 nc.scalar.copy(out=dst, in_=src)
 
+        def first_tile(c):
+            if c == 0:
+                x_bf[0] = rotating("x_bf", [P, K], BF16, 4)
+                x_grp[0] = kept("x_grp0", [P, 2 * K], BF16)
+            half = x_bf[0][:, 512 * c : 512 * (c + 1)]
+            nc.vector.tensor_scalar(
+                out=half.rearrange("p (u m e) -> p m u e", u=2, e=2),
+                in0=x_raw[0][:, 512 * c : 512 * (c + 1)].bitcast(FP8).rearrange("p (m u e) -> p m u e", u=2, e=2),
+                scalar1=one[:], scalar2=None, op0=ALU.mult,
+            )
+            x_bank[0, c] = bank(("x", 0, c))
+            for u in range(2):
+                nc.tensor.transpose(x_bank[0, c][:, u * P : (u + 1) * P], half.bitcast(F32)[:, u * P : (u + 1) * P], ident[:])
+
+        def first_scale(c):
+            nc.vector.tensor_tensor(
+                out=x_grp[0][:, 512 * c : 512 * (c + 1)].rearrange("p (h u e) -> p h u e", u=2, e=2),
+                in0=x_bank[0, c][:, 0:256].bitcast(BF16).rearrange("p (u h e) -> p h u e", u=2, e=2),
+                in1=xs_cols[:, c, :].rearrange("p (u e) -> p u e", u=2).unsqueeze(1).to_broadcast([P, P, 2, 2]),
+                op=ALU.mult,
+            )
+            release(("x", 0, c))
+
         def split_z(n):
             z_split[n] = rotating("z_split", [P, K], BF16, 2)
             nc.scalar.copy(
@@ -311,20 +334,21 @@ def tile_huff_retail_flows_s3_kernel(
                 nc.tensor.matmul(out=b[:], lhsT=ones[:, 0:P], rhs=ones[:], start=True, stop=True)
             release("warm")
 
-        nc.scalar.dma_start(out=a_in[:], in_=a.rearrange("(g p t) -> p g t", p=P, t=4))
+        nc.vector.memset(ones[:], 1.0)
         nc.vector.memset(v_sc[:].bitcast(I32), 0)
         nc.vector.memset(one[:], 1.0)
         nc.vector.memset(warm[:], 1.0)
         nc.vector.memset(y_sc[:].bitcast(I32), 0)
         make_identity(nc, ident[:])
-        nc.gpsimd.memset(ones[:], 1.0)
-        load_x(0)
+        load_x(0, 0, 1)
         nc.sync.dma_start(out=xs_cols[:], in_=x_scale.rearrange("o (g p t) -> p (o g) t", g=2, t=4))
+        load_x(0, 1, 2)
         load_x(1)
-        load_w(0)
         load_z(0)
+        load_w(0)
         load_x(2)
         load_z(1)
+        nc.sync.dma_start(out=a_in[:], in_=a.rearrange("(g p t) -> p g t", p=P, t=4))
         load_scales(v_sc, v_scales, 2)
         load_v(0)
         load_v(1)
@@ -339,36 +363,37 @@ def tile_huff_retail_flows_s3_kernel(
         nc.sync.dma_start(out=y_sb[:], in_=y_words.rearrange("g p n -> p g n"))
         with nc.allow_non_contiguous_dma(reason="one factor a partition for each tile of 128 stores"):
             nc.sync.dma_start(out=size_in[:, :, 0], in_=size.rearrange("(c p) -> p c", p=P))
-        nc.scalar.activation(out=ln_a[:], in_=a_in[:].rearrange("p g t -> p (g t)"), func=ACT.Ln)
-        nc.scalar.activation(out=warm[:], in_=warm[:], func=ACT.Exp)
-        keep_warm(2)
-        cast(0, "v")
-        cast(1, "v")
-        turn_x(0)
+        nc.scalar.activation(out=warm[:], in_=warm[:], func=ACT.Ln)
+        keep_warm(4)
+        first_tile(0)
+        first_tile(1)
+        cast(1, "s")
+        cast(2, "s")
+        cast(3, "s")
         turn_x(1)
-        keep_warm(2)
-        cast(2, "v")
-        cast(3, "v")
-        scale_x(0)
-        turn_x(2)
-        turn_x(3)
+        first_scale(0)
+        first_scale(1)
         scale_x(1)
-        group_w("g", 0, 128, 512, w_all)
-        group_w("s", 0, 0, 128, w_all)
-        scale_x(2)
+        turn_x(2)
         turn_z(0)
         keep_warm(2)
+        turn_x(3)
+        group_w("g", 0, 128, 512, w_all)
+        group_w("s", 0, 0, 128, w_all)
         empty_z(0)
+        scale_x(2)
         cast(4, "s")
         cast(5, "s")
+        turn_z(1)
+        turn_x(4)
+        keep_warm(2)
+        turn_x(5)
+        empty_z(1)
+        nc.scalar.activation(out=ln_a[:], in_=a_in[:].rearrange("p g t -> p (g t)"), func=ACT.Ln)
+        nc.scalar.activation(out=warm[:], in_=warm[:], func=ACT.Exp)
         quant_w(0, 0, 512, w_all)
         quant_z(0)
         quant_x(0, 2)
-        turn_z(1)
-        keep_warm(2)
-        turn_x(4)
-        turn_x(5)
-        empty_z(1)
         scale_x(3)
         travel(0, 0, True)
         travel(1, 0, True)
@@ -382,24 +407,23 @@ def tile_huff_retail_flows_s3_kernel(
         taste(1, 1)
         scale_x(4)
         scale_x(5)
-        group_w("g", 1, 320, 512, x_grp[1])
-        group_w("s", 1, 128, 320, x_grp[1])
-        group_w("v", 1, 0, 128, x_grp[1])
+        group_w("g", 1, 128, 512, x_grp[1])
+        group_w("s", 1, 0, 128, x_grp[1])
+        cast(6, "s")
         utility(2, 0)
         utility(3, 0)
-        cast(6, "v")
+        cast(7, "s")
         quant_w(1, 0, 512, x_grp[1])
-        cast(7, "v")
         taste(2, 1)
         taste(3, 1)
         turn_z(2)
+        turn_x(6)
         empty_z(2, "v")
         for i in range(4):
             travel(i, 1)
             attract(i, 1)
-        quant_x(4, 2)
         quant_z(2)
-        turn_x(6)
+        quant_x(4, 2)
         turn_x(7)
         turn_z(3)
         for n in range(2, 7):

@@ -119,13 +119,9 @@ def tile_huff_retail_flows_s3_kernel(
             dst = x_bf[i][:, 512 * c0 : 512 * c1]
             src = x_raw[i // 2][:, (i % 2) * K + 512 * c0 : (i % 2) * K + 512 * c1].bitcast(FP8)
             for c in range(c0, c1):
-                x_apart[i, c] = (c0, c1) if engine == "v" else None
+                x_apart[i, c] = None
             if engine == "v":
-                nc.vector.tensor_scalar(
-                    out=dst.rearrange("p (u m e) -> p m u e", u=2, e=2),
-                    in0=src.rearrange("p (m u e) -> p m u e", u=2, e=2),
-                    scalar1=one[:], scalar2=None, op0=ALU.mult,
-                )
+                nc.vector.tensor_copy(out=dst, in_=src)
             else:
                 nc.scalar.copy(out=dst, in_=src)
 
@@ -439,7 +435,6 @@ def tile_huff_retail_flows_s3_kernel(
             quant_x(2 * n + 2, 2)
             if n < 6:
                 cast(2 * n + 5, "s", 1, 2)
-                split_z(n + 2)
             utility(2 * n, 0)
             utility(2 * n, 1)
             group_p(g, h, "s", 352, 384 if n < 6 else HALF)

@@ -22,6 +22,8 @@ G = H // 512
 NT = 4 * G
 PAIRS = NT // 2
 HALF = J // 2
+XB = 4
+ZB = 2
 
 
 def tile_huff_retail_flows_s3_kernel(
@@ -65,7 +67,7 @@ def tile_huff_retail_flows_s3_kernel(
         y_sb = kept("y_sb", [P, G, 2 * C], U8)
         y_sc = kept("y_sc", [P, G * C], U8)
         w_raw = [kept("w_raw%d" % h, [P, 4, HALF], BF16) for h in range(2)]
-        w_all = kept("w_all", [P, 4 * HALF], BF16)
+        w_grp = {}
         w_q = [kept("w_q%d" % h, [P, HALF], U32) for h in range(2)]
         w_s = [kept("w_s%d" % h, [P, HALF], U8) for h in range(2)]
         z_raw = [kept("z_raw%d" % n, [P, 2 * D], BF16) for n in range(PAIRS)]
@@ -74,10 +76,11 @@ def tile_huff_retail_flows_s3_kernel(
         x_raw = [kept("x_raw%d" % n, [P, 2 * K], U8) for n in range(PAIRS)]
         x_q = [kept("x_q%d" % n, [P, 4 * P], U32) for n in range(PAIRS)]
         x_s = [kept("x_s%d" % n, [P, 4 * P], U8) for n in range(PAIRS)]
+        x_grp = [kept("x_grp%d" % n, [P, 2 * K], BF16) for n in range(PAIRS)]
         p_q = [[kept("p_q%d_%d" % (g, h), [P, HALF], U32) for h in range(2)] for g in range(G)]
         p_s = [[kept("p_s%d_%d" % (g, h), [P, HALF], U8) for h in range(2)] for g in range(G)]
-        x_bf, x_apart, x_bank, x_grp = {}, {}, {}, {}
-        z_split, z_bank, z_grp = {}, {}, {}
+        x_plain, x_apart, x_bank = {}, {}, {}
+        z_apart, z_bank, z_grp = {}, {}, {}
         u_bank, p_raw, p_grp, f_bank = {}, {}, {}, {}
 
         def load_w(h):
@@ -107,89 +110,87 @@ def tile_huff_retail_flows_s3_kernel(
                     in_=src.bitcast(I32).rearrange("g (q r) n -> q r g n", r=4)[q],
                 )
 
+        def load_a():
+            nc.sync.dma_start(out=a_in[:], in_=a.rearrange("(g p t) -> p g t", p=P, t=4))
+
+        def load_xs():
+            nc.sync.dma_start(out=xs_cols[:], in_=x_scale.rearrange("o (g p t) -> p (o g) t", g=2, t=4))
+
         def copy(engine, dst, src):
             if engine == "s":
                 nc.scalar.copy(out=dst, in_=src)
             else:
                 nc.vector.tensor_copy(out=dst, in_=src)
 
-        def cast(i, engine, c0=0, c1=2):
-            if c0 == 0:
-                x_bf[i] = rotating("x_bf", [P, K], BF16, 4)
-            dst = x_bf[i][:, 512 * c0 : 512 * c1]
-            src = x_raw[i // 2][:, (i % 2) * K + 512 * c0 : (i % 2) * K + 512 * c1].bitcast(FP8)
-            for c in range(c0, c1):
-                x_apart[i, c] = None
-            if engine == "v":
-                nc.vector.tensor_copy(out=dst, in_=src)
-            else:
-                nc.scalar.copy(out=dst, in_=src)
+        def x_codes(i, c0, c1):
+            return x_raw[i // 2][:, (i % 2) * K + 512 * c0 : (i % 2) * K + 512 * c1].bitcast(FP8)
 
-        def first_tile(c):
-            if c == 0:
-                x_bf[0] = rotating("x_bf", [P, K], BF16, 4)
-                x_grp[0] = kept("x_grp0", [P, 2 * K], BF16)
-            half = x_bf[0][:, 512 * c : 512 * (c + 1)]
+        def apart_room(i):
+            if i not in x_apart:
+                x_apart[i] = rotating("x_apart", [P, 2, 2 * 256], BF16, XB)
+            return x_apart[i]
+
+        def cast_apart(i, c0=0, c1=2):
             nc.vector.tensor_scalar(
-                out=half.rearrange("p (u m e) -> p m u e", u=2, e=2),
-                in0=x_raw[0][:, 512 * c : 512 * (c + 1)].bitcast(FP8).rearrange("p (m u e) -> p m u e", u=2, e=2),
+                out=apart_room(i)[:, :, 256 * c0 : 256 * c1].rearrange("p u (m e) -> p m u e", e=2),
+                in0=x_codes(i, c0, c1).rearrange("p (m u e) -> p m u e", u=2, e=2),
                 scalar1=one[:], scalar2=None, op0=ALU.mult,
             )
-            x_bank[0, c] = bank(("x", 0, c))
-            for u in range(2):
-                nc.tensor.transpose(x_bank[0, c][:, u * P : (u + 1) * P], half.bitcast(F32)[:, u * P : (u + 1) * P], ident[:])
 
-        def first_scale(c):
-            nc.vector.tensor_tensor(
-                out=x_grp[0][:, 512 * c : 512 * (c + 1)].rearrange("p (h u e) -> p h u e", u=2, e=2),
-                in0=x_bank[0, c][:, 0:256].bitcast(BF16).rearrange("p (u h e) -> p h u e", u=2, e=2),
-                in1=xs_cols[:, c, :].rearrange("p (u e) -> p u e", u=2).unsqueeze(1).to_broadcast([P, P, 2, 2]),
-                op=ALU.mult,
-            )
-            release(("x", 0, c))
+        def cast_plain(i, c0=0, c1=2):
+            if i not in x_plain:
+                x_plain[i] = rotating("x_plain", [P, K], BF16, 3)
+            nc.scalar.copy(out=x_plain[i][:, 512 * c0 : 512 * c1], in_=x_codes(i, c0, c1))
 
-        def split_z(n):
-            z_split[n] = rotating("z_split", [P, K], BF16, 2)
-            nc.scalar.copy(
-                out=z_split[n][:].bitcast(F32).rearrange("p (u m) -> p m u", u=2),
-                in_=z_raw[n][:].bitcast(F32).rearrange("p (m u) -> p m u", u=2),
+        def split_x(i, engine="v", c0=0, c1=2):
+            copy(
+                engine,
+                apart_room(i)[:, :, 256 * c0 : 256 * c1].bitcast(F32),
+                x_plain[i][:, 512 * c0 : 512 * c1].bitcast(F32).rearrange("p (m u) -> p u m", u=2),
             )
 
-        def turn(key, src, apart):
-            b = bank(key)
-            words = src.bitcast(F32)
-            for c in range(2):
+        def split_z(n, engine):
+            z_apart[n] = rotating("z_apart", [P, 2, 2 * 256], BF16, ZB)
+            copy(engine, z_apart[n][:].bitcast(F32), z_raw[n][:].bitcast(F32).rearrange("p (m u) -> p u m", u=2))
+
+        def turn(b, apart, plain, c0, c1):
+            for c in range(c0, c1):
                 for u in range(2):
-                    if apart[c] is None:
-                        cols = words[:, 256 * c + u : 256 * (c + 1) : 2]
+                    if apart is None:
+                        cols = plain[:].bitcast(F32)[:, 256 * c + u : 256 * (c + 1) : 2]
                     else:
-                        c0, c1 = apart[c]
-                        first = 256 * c0 + P * ((c1 - c0) * u + c - c0)
-                        cols = words[:, first : first + P]
+                        cols = apart[:].bitcast(F32)[:, u, P * c : P * (c + 1)]
                     m = 2 * u + c
                     nc.tensor.transpose(b[:, m * P : (m + 1) * P], cols, ident[:])
-            return b
 
         def turn_x(i):
-            x_bank[i] = turn(("x", i), x_bf[i][:], [x_apart[i, 0], x_apart[i, 1]])
+            x_bank[i] = bank(("x", i))
+            turn(x_bank[i], x_apart.get(i), x_plain.get(i), 0, 2)
 
         def turn_z(n):
-            if n in z_split:
-                z_bank[n] = turn(("z", n), z_split[n][:], [(0, 2), (0, 2)])
-            else:
-                z_bank[n] = turn(("z", n), z_raw[n][:], [None, None])
+            z_bank[n] = bank(("z", n))
+            turn(z_bank[n], z_apart.get(n), z_raw[n], 0, 2)
 
-        def scale_x(i):
+        def turn_x_pass(i, c):
+            x_bank[i, c] = bank(("x", i, c))
+            turn(x_bank[i, c], x_apart.get(i), x_plain.get(i), c, c + 1)
+
+        def scale_from(b, i, c0, c1):
             n, j = divmod(i, 2)
-            if n not in x_grp:
-                x_grp[n] = kept("x_grp%d" % n, [P, 2 * K], BF16)
             nc.vector.tensor_tensor(
-                out=x_grp[n][:, j * K : (j + 1) * K].rearrange("p (c h u e) -> p c h u e", c=2, u=2, e=2),
-                in0=x_bank[i][:].bitcast(BF16).rearrange("p (u c h e) -> p c h u e", c=2, u=2, e=2),
-                in1=xs_cols[:].rearrange("p c (u e) -> p c u e", u=2).unsqueeze(2).to_broadcast([P, 2, P, 2, 2]),
+                out=x_grp[n][:, j * K + 512 * c0 : j * K + 512 * c1].rearrange("p (c h u e) -> p c h u e", h=P, u=2, e=2),
+                in0=b[:].bitcast(BF16).rearrange("p (u c h e) -> p c h u e", c=2, u=2, e=2)[:, c0:c1],
+                in1=xs_cols[:, c0:c1, :].rearrange("p c (u e) -> p c u e", u=2).unsqueeze(2).to_broadcast([P, c1 - c0, P, 2, 2]),
                 op=ALU.mult,
             )
+
+        def scale_x(i):
+            scale_from(x_bank[i], i, 0, 2)
             release(("x", i))
+
+        def scale_x_pass(i, c):
+            scale_from(x_bank[i, c], i, c, c + 1)
+            release(("x", i, c))
 
         def empty_z(n, engine="s"):
             z_grp[n] = rotating("z_grp", [P, K], BF16, 3)
@@ -207,6 +208,19 @@ def tile_huff_retail_flows_s3_kernel(
                 out=x_q[n][:, cols].bitcast(FP8X4), scales=x_s[n][:, cols], in_=x_grp[n][:, j * K : (j + tiles) * K]
             )
 
+        def quant_x_pass(i, c):
+            n, j = divmod(i, 2)
+            cols = slice(256 * j + P * c, 256 * j + P * (c + 1))
+            nc.vector.quantize_mx(
+                out=x_q[n][:, cols].bitcast(FP8X4), scales=x_s[n][:, cols],
+                in_=x_grp[n][:, j * K + 512 * c : j * K + 512 * (c + 1)],
+            )
+
+        def scale_half(i, c):
+            scale_from(x_bank[i], i, c, c + 1)
+            if c == 1:
+                release(("x", i))
+
         def quant_z(n):
             nc.vector.quantize_mx(out=z_q[n][:].bitcast(FP8X4), scales=z_s[n][:], in_=z_grp[n][:])
 
@@ -218,18 +232,20 @@ def tile_huff_retail_flows_s3_kernel(
             else:
                 copy(engine, dst.rearrange("p (c i) t -> p c t i", i=4), src.rearrange("p t (c i) -> p c t i", i=4))
 
-        def group_w(engine, h, c0, c1, room):
-            group4(engine, room[:].rearrange("p (n t) -> p n t", t=4)[:, c0:c1, :], w_raw[h][:, :, c0:c1])
+        def group_w(engine, h, c0, c1, room=None):
+            if room is not None:
+                w_grp[h] = room
+            group4(engine, w_grp[h][:].rearrange("p (n t) -> p n t", t=4)[:, c0:c1, :], w_raw[h][:, :, c0:c1])
 
-        def quant_w(h, c0, c1, room):
+        def quant_w(h, c0=0, c1=HALF):
             nc.vector.quantize_mx(
-                out=w_q[h][:, c0:c1].bitcast(FP8X4), scales=w_s[h][:, c0:c1], in_=room[:, 4 * c0 : 4 * c1]
+                out=w_q[h][:, c0:c1].bitcast(FP8X4), scales=w_s[h][:, c0:c1], in_=w_grp[h][:, 4 * c0 : 4 * c1]
             )
 
-        def taste(i, h, first=True):
-            if first:
-                u_bank[i, h] = bank(("u", i, h))
-            for kg in range(2):
+        def taste(i, h, first=True, passes=(0, 1)):
+            for kg in passes:
+                if first and kg == 0:
+                    u_bank[i, h] = bank(("u", i, h))
                 cols = slice((2 * (i % 2) + kg) * P, (2 * (i % 2) + kg + 1) * P)
                 nc.tensor.matmul_mx(
                     out=u_bank[i, h][:],
@@ -252,7 +268,7 @@ def tile_huff_retail_flows_s3_kernel(
 
         def attract(i, h):
             g, t = divmod(i, 4)
-            if t == 0:
+            if (g, h) not in p_raw:
                 p_raw[g, h] = rotating("p_raw", [P, 4, HALF], BF16, 8)
             nc.scalar.activation(
                 out=p_raw[g, h][:, t, :], in_=u_bank[i, h][:], func=ACT.Exp, bias=ln_a[:, i : i + 1], scale=1.0
@@ -264,65 +280,50 @@ def tile_huff_retail_flows_s3_kernel(
             travel(i, h)
             attract(i, h)
 
-        def group_p(g, h, engine, c0=0, c1=HALF, after=None):
+        def group_p(g, h, engine, c0=0, c1=HALF, room=None):
             if (g, h) not in p_grp:
-                if after is None:
-                    p_grp[g, h] = rotating("p_grp", [P, 4 * HALF], BF16, 3)
-                else:
-                    p_grp[g, h] = x_grp[after]
+                p_grp[g, h] = rotating("p_grp", [P, 4 * HALF], BF16, 3) if room is None else room
             group4(engine, p_grp[g, h][:].rearrange("p (n t) -> p n t", t=4)[:, c0:c1, :], p_raw[g, h][:, :, c0:c1])
 
         def quant_p(g, h):
             nc.vector.quantize_mx(out=p_q[g][h][:].bitcast(FP8X4), scales=p_s[g][h][:], in_=p_grp[g, h][:])
 
-        def flow_passes(jt, groups):
+        def flow_pass(b, jt, g, c0, c1):
             h, c = divmod(jt, 4)
             cols = slice(c * P, (c + 1) * P)
+            nc.tensor.matmul_mx(
+                out=b,
+                lhsT=p_q[g][h][:, cols].bitcast(FP8X4), lhsT_scale=p_s[g][h][:, cols],
+                rhs=y_sb[:, g, 2 * c0 : 2 * c1].bitcast(FP4X4), rhs_scale=y_sc[:, C * g + c0 : C * g + c1],
+                start=(g == 0), stop=(g == G - 1),
+            )
+
+        def flow_passes(jt, groups):
             for g in groups:
                 if g == 0:
                     f_bank[jt] = bank(("f", jt))
-                nc.tensor.matmul_mx(
-                    out=f_bank[jt][:],
-                    lhsT=p_q[g][h][:, cols].bitcast(FP8X4), lhsT_scale=p_s[g][h][:, cols],
-                    rhs=y_sb[:, g, :].bitcast(FP4X4), rhs_scale=y_sc[:, C * g : C * (g + 1)],
-                    start=(g == 0), stop=(g == G - 1),
-                )
+                flow_pass(f_bank[jt][:], jt, g, 0, C)
 
-        def finish(jt, engine):
+        def store(engine, src, jt, c0, c1):
             o = rotating("o_sb", [P, C], F32, 6)
             factor = size_cols[:, jt : jt + 1]
             if engine == "s":
-                nc.scalar.activation(out=o[:], in_=f_bank[jt][:], func=ACT.Copy, scale=factor)
+                nc.scalar.activation(out=o[:, c0:c1], in_=src, func=ACT.Copy, scale=factor)
             else:
-                nc.vector.tensor_scalar(out=o[:], in0=f_bank[jt][:], scalar1=factor, scalar2=None, op0=ALU.mult)
-            release(("f", jt))
-            nc.sync.dma_start(out=out[jt * P : (jt + 1) * P, :], in_=o[:])
+                nc.vector.tensor_scalar(out=o[:, c0:c1], in0=src, scalar1=factor, scalar2=None, op0=ALU.mult)
+            nc.sync.dma_start(out=out[jt * P : (jt + 1) * P, c0:c1], in_=o[:, c0:c1])
 
-        def last_flows(jt, parts):
-            h, c = divmod(jt, 4)
-            cols = slice(c * P, (c + 1) * P)
-            o = rotating("o_sb", [P, C], F32, 6)
-            width = C // parts
-            for part in range(parts):
+        def finish(jt, engine):
+            store(engine, f_bank[jt][:], jt, 0, C)
+            release(("f", jt))
+
+        def last_flows(jt):
+            for part in range(2):
                 b = bank(("f", jt, part))
-                for n0 in range(0, width, P):
-                    c0 = part * width + n0
-                    for g in range(G):
-                        nc.tensor.matmul_mx(
-                            out=b[:, n0 : n0 + P],
-                            lhsT=p_q[g][h][:, cols].bitcast(FP8X4), lhsT_scale=p_s[g][h][:, cols],
-                            rhs=y_sb[:, g, 2 * c0 : 2 * (c0 + P)].bitcast(FP4X4),
-                            rhs_scale=y_sc[:, C * g + c0 : C * g + c0 + P],
-                            start=(g == 0), stop=(g == G - 1),
-                        )
-                span = slice(part * width, (part + 1) * width)
-                if part % 2 == 0:
-                    nc.scalar.activation(out=o[:, span], in_=b[:, 0:width], func=ACT.Copy, scale=size_cols[:, jt : jt + 1])
-                else:
-                    nc.vector.tensor_scalar(
-                        out=o[:, span], in0=b[:, 0:width], scalar1=size_cols[:, jt : jt + 1], scalar2=None, op0=ALU.mult
-                    )
-                nc.sync.dma_start(out=out[jt * P : (jt + 1) * P, span], in_=o[:, span])
+                c0, c1 = 256 * part, 256 * (part + 1)
+                for g in range(G):
+                    flow_pass(b[:, 0:256], jt, g, c0, c1)
+                store("sv"[part], b[:, 0:256], jt, c0, c1)
 
         def keep_warm(count):
             b = bank("warm")
@@ -330,111 +331,125 @@ def tile_huff_retail_flows_s3_kernel(
                 nc.tensor.matmul(out=b[:], lhsT=ones[:, 0:P], rhs=ones[:], start=True, stop=True)
             release("warm")
 
+        nc.vector.memset(warm[:], 1.0)
         nc.vector.memset(ones[:], 1.0)
         nc.vector.memset(v_sc[:].bitcast(I32), 0)
-        nc.vector.memset(one[:], 1.0)
-        nc.vector.memset(warm[:], 1.0)
-        nc.vector.memset(y_sc[:].bitcast(I32), 0)
         make_identity(nc, ident[:])
+        nc.vector.memset(one[:], 1.0)
         load_x(0, 0, 1)
-        nc.sync.dma_start(out=xs_cols[:], in_=x_scale.rearrange("o (g p t) -> p (o g) t", g=2, t=4))
+        load_xs()
         load_x(0, 1, 2)
         load_x(1)
-        load_z(0)
-        load_w(0)
-        load_x(2)
-        load_z(1)
-        nc.sync.dma_start(out=a_in[:], in_=a.rearrange("(g p t) -> p g t", p=P, t=4))
         load_scales(v_sc, v_scales, 2)
         load_v(0)
+        load_a()
         load_v(1)
+        load_w(0)
+        load_z(0)
+        load_z(1)
+        load_x(2)
         load_w(1)
-        load_x(3)
         load_z(2)
-        load_z(3)
-        for n in range(4, PAIRS):
+        for n in range(3, PAIRS):
             load_x(n)
             load_z(n)
+        nc.vector.memset(y_sc[:].bitcast(I32), 0)
         load_scales(y_sc, y_scales, G)
         nc.sync.dma_start(out=y_sb[:], in_=y_words.rearrange("g p n -> p g n"))
         with nc.allow_non_contiguous_dma(reason="one factor a partition for each tile of 128 stores"):
             nc.sync.dma_start(out=size_in[:, :, 0], in_=size.rearrange("(c p) -> p c", p=P))
         nc.scalar.activation(out=warm[:], in_=warm[:], func=ACT.Ln)
-        keep_warm(4)
-        first_tile(0)
-        first_tile(1)
-        cast(1, "s")
-        cast(2, "s")
-        cast(3, "s")
-        turn_x(1)
-        first_scale(0)
-        first_scale(1)
-        scale_x(1)
-        turn_x(2)
-        turn_z(0)
-        keep_warm(2)
-        turn_x(3)
-        group_w("g", 0, 128, 512, w_all)
-        group_w("s", 0, 0, 128, w_all)
-        empty_z(0)
-        scale_x(2)
-        cast(4, "s")
-        cast(5, "s")
-        turn_z(1)
-        turn_x(4)
-        keep_warm(2)
-        turn_x(5)
-        empty_z(1)
+        keep_warm(3)
+        for c in range(2):
+            cast_apart(0, c, c + 1)
+            turn_x_pass(0, c)
+        cast_apart(1)
+        cast_plain(2)
+        cast_plain(3)
         nc.scalar.activation(out=ln_a[:], in_=a_in[:].rearrange("p g t -> p (g t)"), func=ACT.Ln)
         nc.scalar.activation(out=warm[:], in_=warm[:], func=ACT.Exp)
-        quant_w(0, 0, 512, w_all)
-        quant_z(0)
-        quant_x(0, 2)
-        scale_x(3)
-        travel(0, 0, True)
-        travel(1, 0, True)
-        quant_z(1)
-        quant_x(2, 2)
-        taste(0, 0, False)
-        attract(0, 0)
-        taste(1, 0, False)
-        attract(1, 0)
-        taste(0, 1)
-        taste(1, 1)
-        scale_x(4)
-        scale_x(5)
-        group_w("g", 1, 128, 512, x_grp[1])
-        group_w("s", 1, 0, 128, x_grp[1])
-        cast(6, "s")
-        utility(2, 0)
-        utility(3, 0)
-        cast(7, "s")
-        quant_w(1, 0, 512, x_grp[1])
+        keep_warm(1)
+        turn_x(1)
+        keep_warm(1)
+        scale_x_pass(0, 0)
+        scale_x_pass(0, 1)
+        turn_x(2)
+        turn_x(3)
+        quant_x_pass(0, 0)
+        scale_half(1, 0)
+        quant_x_pass(0, 1)
+        scale_half(1, 1)
+        quant_x_pass(1, 0)
+        scale_half(2, 0)
+        quant_x_pass(1, 1)
+        for i in range(2):
+            for c in range(2):
+                taste(i, 0, passes=[c])
+                taste(i, 1, passes=[c])
+        scale_half(2, 1)
+        group_w("s", 0, 0, 320, x_grp[0])
+        quant_x_pass(2, 0)
+        scale_half(3, 0)
+        quant_x_pass(2, 1)
+        scale_half(3, 1)
+        group_w("v", 0, 320, 512)
+        turn_z(0)
+        turn_z(1)
+        empty_z(0)
+        taste(2, 0)
         taste(2, 1)
-        taste(3, 1)
+        cast_plain(4)
+        empty_z(1)
+        cast_plain(5)
+        quant_z(0)
+        quant_w(0)
+        quant_x(3)
+        quant_z(1)
+        turn_x(4)
+        travel(0, 0)
+        group_w("s", 1, 0, 112, x_grp[1])
+        attract(0, 0)
+        travel(1, 0)
+        travel(2, 0)
+        group_w("g", 1, 112, 512)
+        scale_x(4)
+        turn_x(5)
         turn_z(2)
-        turn_x(6)
-        empty_z(2, "v")
+        attract(1, 0)
+        attract(2, 0)
+        scale_half(5, 0)
+        taste(3, 0)
+        travel(3, 0)
+        empty_z(2)
+        quant_w(1)
+        scale_half(5, 1)
+        cast_plain(7)
+        attract(3, 0)
+        taste(3, 1)
         for i in range(4):
             travel(i, 1)
             attract(i, 1)
+        cast_apart(6)
+        split_z(3, "v")
         quant_z(2)
         quant_x(4, 2)
-        turn_x(7)
+        turn_x(6)
         turn_z(3)
+        turn_x(7)
         for n in range(2, 7):
             g, h = divmod(n - 2, 2)
             empty_z(n + 1)
             scale_x(2 * n + 2)
             scale_x(2 * n + 3)
-            group_p(g, h, "g", 0, 352, after=n)
+            group_p(g, h, "g", 0, 352, x_grp[n])
             if n < 6:
-                cast(2 * n + 4, "v")
-                cast(2 * n + 5, "v", 0, 1)
+                cast_plain(2 * n + 5)
+                cast_apart(2 * n + 4)
+                split_x(2 * n + 5)
             quant_z(n + 1)
             quant_x(2 * n + 2, 2)
             if n < 6:
-                cast(2 * n + 5, "s", 1, 2)
+                split_z(n + 2, "s")
             utility(2 * n, 0)
             utility(2 * n, 1)
             group_p(g, h, "s", 352, 384 if n < 6 else HALF)
@@ -475,4 +490,4 @@ def tile_huff_retail_flows_s3_kernel(
                     finish(jt, "s" if jt == 4 else "v")
         flow_passes(6, range(G))
         finish(6, "s")
-        last_flows(7, 2)
+        last_flows(7)

@@ -340,17 +340,19 @@ def tile_huff_retail_flows_s3_kernel(
         load_xs()
         load_x(0, 1, 2)
         load_x(1)
-        load_scales(v_sc, v_scales, 2)
-        load_v(0)
-        load_a()
-        load_v(1)
         load_w(0)
         load_z(0)
-        load_z(1)
         load_x(2)
+        load_z(1)
+        load_a()
+        load_scales(v_sc, v_scales, 2)
+        load_v(0)
+        load_v(1)
         load_w(1)
+        load_x(3)
         load_z(2)
-        for n in range(3, PAIRS):
+        load_z(3)
+        for n in range(4, PAIRS):
             load_x(n)
             load_z(n)
         nc.vector.memset(y_sc[:].bitcast(I32), 0)
@@ -366,102 +368,98 @@ def tile_huff_retail_flows_s3_kernel(
         cast_apart(1)
         cast_plain(2)
         cast_plain(3)
-        nc.scalar.activation(out=ln_a[:], in_=a_in[:].rearrange("p g t -> p (g t)"), func=ACT.Ln)
-        nc.scalar.activation(out=warm[:], in_=warm[:], func=ACT.Exp)
         keep_warm(1)
         turn_x(1)
-        keep_warm(1)
         scale_x_pass(0, 0)
         scale_x_pass(0, 1)
+        scale_x(1)
         turn_x(2)
         turn_x(3)
-        quant_x_pass(0, 0)
-        scale_half(1, 0)
-        quant_x_pass(0, 1)
-        scale_half(1, 1)
-        quant_x_pass(1, 0)
-        scale_half(2, 0)
-        quant_x_pass(1, 1)
-        for i in range(2):
-            for c in range(2):
-                taste(i, 0, passes=[c])
-                taste(i, 1, passes=[c])
-        scale_half(2, 1)
-        group_w("s", 0, 0, 320, x_grp[0])
-        quant_x_pass(2, 0)
-        scale_half(3, 0)
-        quant_x_pass(2, 1)
-        scale_half(3, 1)
-        group_w("v", 0, 320, 512)
+        keep_warm(1)
         turn_z(0)
-        turn_z(1)
-        empty_z(0)
-        taste(2, 0)
-        taste(2, 1)
+        w_room = kept("w_room", [P, 4 * HALF], BF16)
+        keep_warm(2)
+        group_w("g", 0, 160, 512, w_room)
+        group_w("s", 0, 0, 160)
+        scale_x(2)
         cast_plain(4)
-        empty_z(1)
         cast_plain(5)
-        quant_z(0)
-        quant_w(0)
-        quant_x(3)
-        quant_z(1)
+        empty_z(0)
+        turn_z(1)
         turn_x(4)
-        travel(0, 0)
-        group_w("s", 1, 0, 112, x_grp[1])
-        attract(0, 0)
-        travel(1, 0)
-        travel(2, 0)
-        group_w("g", 1, 112, 512)
-        scale_x(4)
         turn_x(5)
-        turn_z(2)
+        empty_z(1)
+        nc.scalar.activation(out=ln_a[:], in_=a_in[:].rearrange("p g t -> p (g t)"), func=ACT.Ln)
+        nc.scalar.activation(out=warm[:], in_=warm[:], func=ACT.Exp)
+        quant_w(0)
+        quant_z(0)
+        quant_x(0, 2)
+        scale_x(3)
+        travel(0, 0, True)
+        travel(1, 0, True)
+        quant_z(1)
+        quant_x(2, 2)
+        taste(0, 0, False)
+        attract(0, 0)
+        taste(1, 0, False)
         attract(1, 0)
-        attract(2, 0)
-        scale_half(5, 0)
-        taste(3, 0)
-        travel(3, 0)
-        empty_z(2)
+        taste(0, 1)
+        taste(1, 1)
+        scale_x(4)
+        scale_x(5)
+        group_w("g", 1, 128, 512, x_grp[1])
+        group_w("s", 1, 0, 128)
+        utility(2, 0)
+        split_z(2, "s")
+        utility(3, 0)
+        cast_apart(6)
         quant_w(1)
-        scale_half(5, 1)
         cast_plain(7)
-        attract(3, 0)
+        split_z(3, "s")
+        taste(2, 1)
         taste(3, 1)
+        turn_z(2)
+        turn_x(6)
+        empty_z(2, "v")
+        split_x(7)
         for i in range(4):
             travel(i, 1)
             attract(i, 1)
-        cast_apart(6)
-        split_z(3, "v")
-        quant_z(2)
         quant_x(4, 2)
-        turn_x(6)
-        turn_z(3)
+        quant_z(2)
         turn_x(7)
+        turn_z(3)
         for n in range(2, 7):
             g, h = divmod(n - 2, 2)
             empty_z(n + 1)
             scale_x(2 * n + 2)
             scale_x(2 * n + 3)
-            group_p(g, h, "g", 0, 352, x_grp[n])
+            group_p(g, h, "g", 0, 384, x_grp[n])
             if n < 6:
                 cast_plain(2 * n + 5)
                 cast_apart(2 * n + 4)
                 split_x(2 * n + 5)
-            quant_z(n + 1)
+            if n == 6:
+                quant_z(n + 1)
             quant_x(2 * n + 2, 2)
             if n < 6:
-                split_z(n + 2, "s")
+                quant_z(n + 1)
+            if n == 6:
+                group_p(0, 0, "s", 384, HALF)
             utility(2 * n, 0)
-            utility(2 * n, 1)
-            group_p(g, h, "s", 352, 384 if n < 6 else HALF)
+            if n < 6:
+                split_z(n + 2, "s")
             utility(2 * n + 1, 0)
+            if n == 6:
+                group_p(g, h, "s", 384, HALF)
+            utility(2 * n, 1)
             utility(2 * n + 1, 1)
             if n < 6:
                 turn_x(2 * n + 4)
                 turn_x(2 * n + 5)
                 turn_z(n + 2)
         nc.vector.tensor_copy(out=size_cols[:], in_=size_in[:, :, 0])
-        for g in range(2):
-            group_p(g, 0, "v", 384, HALF)
+        group_p(1, 0, "v", 384, HALF)
         for g in range(3):
             quant_p(g, 0)
         for g in range(2):

@@ -276,8 +276,12 @@ def tile_huff_retail_flows_s3_kernel(
             release(("u", i, h))
 
         def utility(i, h):
-            taste(i, h)
-            travel(i, h)
+            if i % 2 == 0:
+                taste(i, h)
+                travel(i, h)
+            else:
+                travel(i, h, True)
+                taste(i, h, False)
             attract(i, h)
 
         def group_p(g, h, engine, c0=0, c1=HALF, room=None):
@@ -305,25 +309,24 @@ def tile_huff_retail_flows_s3_kernel(
                 flow_pass(f_bank[jt][:], jt, g, 0, C)
 
         def store(engine, src, jt, c0, c1):
-            o = rotating("o_sb", [P, C], F32, 6)
+            o = kept("o_sb%d_%d" % (jt, c0), [P, c1 - c0], F32)
             factor = size_cols[:, jt : jt + 1]
             if engine == "s":
-                nc.scalar.activation(out=o[:, c0:c1], in_=src, func=ACT.Copy, scale=factor)
+                nc.scalar.activation(out=o[:], in_=src, func=ACT.Copy, scale=factor)
             else:
-                nc.vector.tensor_scalar(out=o[:, c0:c1], in0=src, scalar1=factor, scalar2=None, op0=ALU.mult)
-            nc.sync.dma_start(out=out[jt * P : (jt + 1) * P, c0:c1], in_=o[:, c0:c1])
+                nc.vector.tensor_scalar(out=o[:], in0=src, scalar1=factor, scalar2=None, op0=ALU.mult)
+            nc.sync.dma_start(out=out[jt * P : (jt + 1) * P, c0:c1], in_=o[:])
 
         def finish(jt, engine):
             store(engine, f_bank[jt][:], jt, 0, C)
             release(("f", jt))
 
-        def last_flows(jt):
-            for part in range(2):
-                b = bank(("f", jt, part))
-                c0, c1 = 256 * part, 256 * (part + 1)
-                for g in range(G):
-                    flow_pass(b[:, 0:256], jt, g, c0, c1)
-                store("sv"[part], b[:, 0:256], jt, c0, c1)
+        def flow_piece(jt, c0, c1, engine):
+            b = bank(("f", jt, c0))
+            for g in range(G):
+                flow_pass(b[:, 0 : c1 - c0], jt, g, c0, c1)
+            store(engine, b[:, 0 : c1 - c0], jt, c0, c1)
+            release(("f", jt, c0))
 
         def keep_warm(count):
             b = bank("warm")
@@ -488,4 +491,5 @@ def tile_huff_retail_flows_s3_kernel(
                     finish(jt, "s" if jt == 4 else "v")
         flow_passes(6, range(G))
         finish(6, "s")
-        last_flows(7)
+        flow_piece(7, 0, 256, "s")
+        flow_piece(7, 256, 512, "v")

@@ -24,6 +24,8 @@ PAIRS = NT // 2
 HALF = J // 2
 XB = 4
 ZB = 2
+G_FIRST = 384
+G_SHARE = 400
 
 
 def tile_huff_retail_flows_s3_kernel(
@@ -76,7 +78,8 @@ def tile_huff_retail_flows_s3_kernel(
         x_raw = [kept("x_raw%d" % n, [P, 2 * K], U8) for n in range(PAIRS)]
         x_q = [kept("x_q%d" % n, [P, 4 * P], U32) for n in range(PAIRS)]
         x_s = [kept("x_s%d" % n, [P, 4 * P], U8) for n in range(PAIRS)]
-        x_grp = [kept("x_grp%d" % n, [P, 2 * K], BF16) for n in range(PAIRS)]
+        x_grp = {}
+        room = {n: kept("room%d" % n, [P, 4 * HALF], BF16) for n in range(1, 7)}
         p_q = [[kept("p_q%d_%d" % (g, h), [P, HALF], U32) for h in range(2)] for g in range(G)]
         p_s = [[kept("p_s%d_%d" % (g, h), [P, HALF], U8) for h in range(2)] for g in range(G)]
         x_plain, x_apart, x_bank = {}, {}, {}
@@ -177,6 +180,8 @@ def tile_huff_retail_flows_s3_kernel(
 
         def scale_from(b, i, c0, c1):
             n, j = divmod(i, 2)
+            if n not in x_grp:
+                x_grp[n] = rotating("x_grp", [P, 2 * K], BF16, 3)
             nc.vector.tensor_tensor(
                 out=x_grp[n][:, j * K + 512 * c0 : j * K + 512 * c1].rearrange("p (c h u e) -> p c h u e", h=P, u=2, e=2),
                 in0=b[:].bitcast(BF16).rearrange("p (u c h e) -> p c h u e", c=2, u=2, e=2)[:, c0:c1],
@@ -193,10 +198,10 @@ def tile_huff_retail_flows_s3_kernel(
             release(("x", i, c))
 
         def empty_z(n, engine="s"):
-            z_grp[n] = rotating("z_grp", [P, K], BF16, 3)
+            z_grp[n] = room[n][:, 0:K] if n in room else rotating("z_grp", [P, K], BF16, 2)[:]
             copy(
                 engine,
-                z_grp[n][:].bitcast(F32).rearrange("p (m u) -> p m u", u=2),
+                z_grp[n].bitcast(F32).rearrange("p (m u) -> p m u", u=2),
                 z_bank[n][:].rearrange("p (u m) -> p m u", u=2),
             )
             release(("z", n))
@@ -222,7 +227,7 @@ def tile_huff_retail_flows_s3_kernel(
                 release(("x", i))
 
         def quant_z(n):
-            nc.vector.quantize_mx(out=z_q[n][:].bitcast(FP8X4), scales=z_s[n][:], in_=z_grp[n][:])
+            nc.vector.quantize_mx(out=z_q[n][:].bitcast(FP8X4), scales=z_s[n][:], in_=z_grp[n])
 
         def group4(engine, dst, src):
             if engine == "g":
@@ -284,6 +289,19 @@ def tile_huff_retail_flows_s3_kernel(
                 taste(i, h, False)
             attract(i, h)
 
+        def utilities(n):
+            tiles = (2 * n, 2 * n + 1)
+            for i in tiles:
+                travel(i, 0, True)
+            for i in tiles:
+                taste(i, 0, False)
+                attract(i, 0)
+            for i in tiles:
+                taste(i, 1)
+            for i in tiles:
+                travel(i, 1)
+                attract(i, 1)
+
         def group_p(g, h, engine, c0=0, c1=HALF, room=None):
             if (g, h) not in p_grp:
                 p_grp[g, h] = rotating("p_grp", [P, 4 * HALF], BF16, 3) if room is None else room
@@ -327,6 +345,9 @@ def tile_huff_retail_flows_s3_kernel(
                 flow_pass(b[:, 0 : c1 - c0], jt, g, c0, c1)
             store(engine, b[:, 0 : c1 - c0], jt, c0, c1)
             release(("f", jt, c0))
+
+        def share(g, h):
+            return G_FIRST if (g, h) == (0, 0) else G_SHARE
 
         def keep_warm(count):
             b = bank("warm")
@@ -410,73 +431,75 @@ def tile_huff_retail_flows_s3_kernel(
         taste(1, 1)
         scale_x(4)
         scale_x(5)
-        group_w("g", 1, 128, 512, x_grp[1])
-        group_w("s", 1, 0, 128)
-        utility(2, 0)
+        group_w("g", 1, 0, 416, room[1])
+        group_w("s", 1, 416, 512)
+        cast_plain(7)
         split_z(2, "s")
+        utility(2, 0)
         utility(3, 0)
         cast_apart(6)
+        split_z(3, "v")
+        split_x(7)
         quant_w(1)
-        cast_plain(7)
-        split_z(3, "s")
         taste(2, 1)
         taste(3, 1)
         turn_z(2)
         turn_x(6)
-        empty_z(2, "v")
-        split_x(7)
+        turn_z(3)
+        turn_x(7)
+        empty_z(2)
         for i in range(4):
             travel(i, 1)
-            attract(i, 1)
-        quant_x(4, 2)
         quant_z(2)
-        turn_x(7)
-        turn_z(3)
+        quant_x(4, 2)
         for n in range(2, 7):
             g, h = divmod(n - 2, 2)
             empty_z(n + 1)
+            if n == 2:
+                cast_plain(9)
+                attract(0, 1)
+                attract(1, 1)
+                split_z(4, "s")
+                attract(2, 1)
+                attract(3, 1)
             scale_x(2 * n + 2)
             scale_x(2 * n + 3)
-            group_p(g, h, "g", 0, 384, x_grp[n])
-            if n < 6:
+            group_p(g, h, "g", 0, share(g, h), room[n])
+            if 2 < n < 6:
                 cast_plain(2 * n + 5)
+            if n < 6:
                 cast_apart(2 * n + 4)
                 split_x(2 * n + 5)
-            if n == 6:
-                quant_z(n + 1)
-            quant_x(2 * n + 2, 2)
-            if n < 6:
-                quant_z(n + 1)
-            if n == 6:
-                group_p(0, 0, "s", 384, HALF)
-            utility(2 * n, 0)
-            if n < 6:
+            if 2 < n < 6:
                 split_z(n + 2, "s")
-            utility(2 * n + 1, 0)
+            quant_z(n + 1)
+            quant_x(2 * n + 2, 2)
             if n == 6:
-                group_p(g, h, "s", 384, HALF)
-            utility(2 * n, 1)
-            utility(2 * n + 1, 1)
+                group_p(0, 0, "s", share(0, 0), HALF)
+                group_p(2, 0, "s", share(2, 0), HALF)
+            utilities(n)
             if n < 6:
                 turn_x(2 * n + 4)
                 turn_x(2 * n + 5)
                 turn_z(n + 2)
         nc.vector.tensor_copy(out=size_cols[:], in_=size_in[:, :, 0])
-        group_p(1, 0, "v", 384, HALF)
+        group_p(1, 0, "v", share(1, 0), HALF)
         for g in range(3):
             quant_p(g, 0)
         for g in range(2):
-            group_p(g, 1, "v", 384, HALF)
-        utility(14, 0)
-        utility(15, 0)
-        utility(14, 1)
-        utility(15, 1)
+            group_p(g, 1, "v", share(g, 1), HALF)
+        for h in range(2):
+            for i in (14, 15):
+                travel(i, h, True)
+            for i in (14, 15):
+                taste(i, h, False)
+                attract(i, h)
         group_p(2, 1, "s")
-        group_p(3, 0, "v")
         quant_p(0, 1)
+        group_p(3, 0, "v")
+        quant_p(1, 1)
         quant_p(3, 0)
         group_p(3, 1, "v")
-        quant_p(1, 1)
         quant_p(2, 1)
         quant_p(3, 1)
         for g in range(G):

from contextlib import ExitStack

import concourse.mybir as mybir
from concourse.masks import make_identity

H, J, D, K, C = 2048, 1024, 512, 1024, 512
FLOPS = 2 * H * J * (D + K) + 2 * J * C * H

F32 = mybir.dt.float32
BF16 = mybir.dt.bfloat16
U32 = mybir.dt.uint32
I32 = mybir.dt.int32
U8 = mybir.dt.uint8
FP8 = mybir.dt.float8_e4m3fn
FP8X4 = mybir.dt.float8_e4m3fn_x4
FP4X4 = mybir.dt.float4_e2m1fn_x4
ACT = mybir.ActivationFunctionType
ALU = mybir.AluOpType

P = 128
G = H // 512
NT = 4 * G
PAIRS = NT // 2
HALF = J // 2
XB = 4
ZB = 2
G_FIRST = 384
G_SHARE = 400


def tile_huff_retail_flows_s3_kernel(
    tc, z, w, x_bytes, x_scale, v_words, v_scales, a, size, y_words, y_scales, out
):
    nc = tc.nc
    with ExitStack() as ctx:
        keep = ctx.enter_context(tc.tile_pool(name="keep", bufs=1))
        work = ctx.enter_context(tc.tile_pool(name="work", bufs=2))
        psum = ctx.enter_context(tc.psum_pool(name="psum", bufs=1))
        ctx.enter_context(tc.manual_schedule())

        def kept(name, shape, dtype):
            return keep.tile(shape, dtype, name=name, tag=name, align_bytes=64)

        def rotating(name, shape, dtype, bufs):
            return work.tile(shape, dtype, name=name, tag=name, bufs=bufs, align_bytes=64)

        free_banks = ["bank%d" % k for k in range(8)]
        bank_name = {}

        def bank(key):
            name = free_banks.pop(0)
            bank_name[key] = name
            return psum.tile([P, 512], F32, name=name, tag=name, bufs=1)

        def release(key):
            free_banks.append(bank_name[key])

        ident = kept("ident", [P, P], F32)
        a_in = kept("a_in", [P, G, 4], BF16)
        ln_a = kept("ln_a", [P, NT], F32)
        xs_cols = kept("xs_cols", [P, 2, 4], F32)
        one = kept("one", [P, 1], F32)
        size_in = kept("size_in", [P, 8, 2], BF16)
        warm = kept("warm", [P, 1], F32)
        ones = kept("ones", [P, 512], BF16)
        size_cols = kept("size_cols", [P, 8], F32)
        v_sb = [kept("v_sb%d" % h, [P, 2, 2 * HALF], U8) for h in range(2)]
        v_sc = kept("v_sc", [P, 2 * J], U8)
        y_sb = kept("y_sb", [P, G, 2 * C], U8)
        y_sc = kept("y_sc", [P, G * C], U8)
        w_raw = [kept("w_raw%d" % h, [P, 4, HALF], BF16) for h in range(2)]
        w_grp = {}
        w_q = [kept("w_q%d" % h, [P, HALF], U32) for h in range(2)]
        w_s = [kept("w_s%d" % h, [P, HALF], U8) for h in range(2)]
        z_raw = [kept("z_raw%d" % n, [P, 2 * D], BF16) for n in range(PAIRS)]
        z_q = [kept("z_q%d" % n, [P, 256], U32) for n in range(PAIRS)]
        z_s = [kept("z_s%d" % n, [P, 256], U8) for n in range(PAIRS)]
        x_raw = [kept("x_raw%d" % n, [P, 2 * K], U8) for n in range(PAIRS)]
        x_q = [kept("x_q%d" % n, [P, 4 * P], U32) for n in range(PAIRS)]
        x_s = [kept("x_s%d" % n, [P, 4 * P], U8) for n in range(PAIRS)]
        x_grp = {}
        room = {n: kept("room%d" % n, [P, 4 * HALF], BF16) for n in range(1, 7)}
        p_q = [[kept("p_q%d_%d" % (g, h), [P, HALF], U32) for h in range(2)] for g in range(G)]
        p_s = [[kept("p_s%d_%d" % (g, h), [P, HALF], U8) for h in range(2)] for g in range(G)]
        x_plain, x_apart, x_bank = {}, {}, {}
        z_apart, z_bank, z_grp = {}, {}, {}
        u_bank, p_raw, p_grp, f_bank = {}, {}, {}, {}

        def load_w(h):
            nc.sync.dma_start(out=w_raw[h][:], in_=w.rearrange("(p t) j -> p t j", t=4)[:, :, h * HALF : (h + 1) * HALF])

        def load_v(h):
            nc.sync.dma_start(
                out=v_sb[h][:], in_=v_words.rearrange("g p n -> p g n")[:, :, 2 * HALF * h : 2 * HALF * (h + 1)]
            )

        def load_z(n):
            g, half = divmod(n, 2)
            src = z[512 * g : 512 * (g + 1), :].rearrange("(p t) k -> p (t k)", t=4)
            nc.sync.dma_start(out=z_raw[n][:], in_=src[:, 2 * half * D : 2 * (half + 1) * D])

        def load_x(n, j0=0, j1=2):
            g, half = divmod(n, 2)
            src = x_bytes[512 * g : 512 * (g + 1), :].rearrange("(p t) k -> p (t k)", t=4)
            nc.sync.dma_start(
                out=x_raw[n][:, j0 * K : j1 * K], in_=src[:, (2 * half + j0) * K : (2 * half + j1) * K]
            )

        def load_scales(tile, src, groups):
            for q in range(4):
                nc.sync.dma_start(
                    out=tile[32 * q : 32 * q + 4, :].bitcast(I32).rearrange("r (g n) -> r g n", g=groups),
                    in_=src.bitcast(I32).rearrange("g (q r) n -> q r g n", r=4)[q],
                )

        def load_a():
            nc.sync.dma_start(out=a_in[:], in_=a.rearrange("(g p t) -> p g t", p=P, t=4))

        def load_xs():
            nc.sync.dma_start(out=xs_cols[:], in_=x_scale.rearrange("o (g p t) -> p (o g) t", g=2, t=4))

        def copy(engine, dst, src):
            if engine == "s":
                nc.scalar.copy(out=dst, in_=src)
            else:
                nc.vector.tensor_copy(out=dst, in_=src)

        def x_codes(i, c0, c1):
            return x_raw[i // 2][:, (i % 2) * K + 512 * c0 : (i % 2) * K + 512 * c1].bitcast(FP8)

        def apart_room(i):
            if i not in x_apart:
                x_apart[i] = rotating("x_apart", [P, 2, 2 * 256], BF16, XB)
            return x_apart[i]

        def cast_apart(i, c0=0, c1=2):
            nc.vector.tensor_scalar(
                out=apart_room(i)[:, :, 256 * c0 : 256 * c1].rearrange("p u (m e) -> p m u e", e=2),
                in0=x_codes(i, c0, c1).rearrange("p (m u e) -> p m u e", u=2, e=2),
                scalar1=one[:], scalar2=None, op0=ALU.mult,
            )

        def cast_plain(i, c0=0, c1=2):
            if i not in x_plain:
                x_plain[i] = rotating("x_plain", [P, K], BF16, 3)
            nc.scalar.copy(out=x_plain[i][:, 512 * c0 : 512 * c1], in_=x_codes(i, c0, c1))

        def split_x(i, engine="v", c0=0, c1=2):
            copy(
                engine,
                apart_room(i)[:, :, 256 * c0 : 256 * c1].bitcast(F32),
                x_plain[i][:, 512 * c0 : 512 * c1].bitcast(F32).rearrange("p (m u) -> p u m", u=2),
            )

        def split_z(n, engine):
            z_apart[n] = rotating("z_apart", [P, 2, 2 * 256], BF16, ZB)
            copy(engine, z_apart[n][:].bitcast(F32), z_raw[n][:].bitcast(F32).rearrange("p (m u) -> p u m", u=2))

        def turn(b, apart, plain, c0, c1):
            for c in range(c0, c1):
                for u in range(2):
                    if apart is None:
                        cols = plain[:].bitcast(F32)[:, 256 * c + u : 256 * (c + 1) : 2]
                    else:
                        cols = apart[:].bitcast(F32)[:, u, P * c : P * (c + 1)]
                    m = 2 * u + c
                    nc.tensor.transpose(b[:, m * P : (m + 1) * P], cols, ident[:])

        def turn_x(i):
            x_bank[i] = bank(("x", i))
            turn(x_bank[i], x_apart.get(i), x_plain.get(i), 0, 2)

        def turn_z(n):
            z_bank[n] = bank(("z", n))
            turn(z_bank[n], z_apart.get(n), z_raw[n], 0, 2)

        def turn_x_pass(i, c):
            x_bank[i, c] = bank(("x", i, c))
            turn(x_bank[i, c], x_apart.get(i), x_plain.get(i), c, c + 1)

        def scale_from(b, i, c0, c1):
            n, j = divmod(i, 2)
            if n not in x_grp:
                x_grp[n] = rotating("x_grp", [P, 2 * K], BF16, 3)
            nc.vector.tensor_tensor(
                out=x_grp[n][:, j * K + 512 * c0 : j * K + 512 * c1].rearrange("p (c h u e) -> p c h u e", h=P, u=2, e=2),
                in0=b[:].bitcast(BF16).rearrange("p (u c h e) -> p c h u e", c=2, u=2, e=2)[:, c0:c1],
                in1=xs_cols[:, c0:c1, :].rearrange("p c (u e) -> p c u e", u=2).unsqueeze(2).to_broadcast([P, c1 - c0, P, 2, 2]),
                op=ALU.mult,
            )

        def scale_x(i):
            scale_from(x_bank[i], i, 0, 2)
            release(("x", i))

        def scale_x_pass(i, c):
            scale_from(x_bank[i, c], i, c, c + 1)
            release(("x", i, c))

        def empty_z(n, engine="s"):
            z_grp[n] = room[n][:, 0:K] if n in room else rotating("z_grp", [P, K], BF16, 2)[:]
            copy(
                engine,
                z_grp[n].bitcast(F32).rearrange("p (m u) -> p m u", u=2),
                z_bank[n][:].rearrange("p (u m) -> p m u", u=2),
            )
            release(("z", n))

        def quant_x(i, tiles=1):
            n, j = divmod(i, 2)
            cols = slice(256 * j, 256 * (j + tiles))
            nc.vector.quantize_mx(
                out=x_q[n][:, cols].bitcast(FP8X4), scales=x_s[n][:, cols], in_=x_grp[n][:, j * K : (j + tiles) * K]
            )

        def quant_x_pass(i, c):
            n, j = divmod(i, 2)
            cols = slice(256 * j + P * c, 256 * j + P * (c + 1))
            nc.vector.quantize_mx(
                out=x_q[n][:, cols].bitcast(FP8X4), scales=x_s[n][:, cols],
                in_=x_grp[n][:, j * K + 512 * c : j * K + 512 * (c + 1)],
            )

        def scale_half(i, c):
            scale_from(x_bank[i], i, c, c + 1)
            if c == 1:
                release(("x", i))

        def quant_z(n):
            nc.vector.quantize_mx(out=z_q[n][:].bitcast(FP8X4), scales=z_s[n][:], in_=z_grp[n])

        def group4(engine, dst, src):
            if engine == "g":
                nc.gpsimd.tensor_scalar(
                    out=dst, in0=src.rearrange("p t n -> p n t"), scalar1=1.0, scalar2=0.0, op0=ALU.mult, op1=ALU.add
                )
            else:
                copy(engine, dst.rearrange("p (c i) t -> p c t i", i=4), src.rearrange("p t (c i) -> p c t i", i=4))

        def group_w(engine, h, c0, c1, room=None):
            if room is not None:
                w_grp[h] = room
            group4(engine, w_grp[h][:].rearrange("p (n t) -> p n t", t=4)[:, c0:c1, :], w_raw[h][:, :, c0:c1])

        def quant_w(h, c0=0, c1=HALF):
            nc.vector.quantize_mx(
                out=w_q[h][:, c0:c1].bitcast(FP8X4), scales=w_s[h][:, c0:c1], in_=w_grp[h][:, 4 * c0 : 4 * c1]
            )

        def taste(i, h, first=True, passes=(0, 1)):
            for kg in passes:
                if first and kg == 0:
                    u_bank[i, h] = bank(("u", i, h))
                cols = slice((2 * (i % 2) + kg) * P, (2 * (i % 2) + kg + 1) * P)
                nc.tensor.matmul_mx(
                    out=u_bank[i, h][:],
                    lhsT=x_q[i // 2][:, cols].bitcast(FP8X4), lhsT_scale=x_s[i // 2][:, cols],
                    rhs=v_sb[h][:, kg, :].bitcast(FP4X4),
                    rhs_scale=v_sc[:, J * kg + HALF * h : J * kg + HALF * (h + 1)],
                    start=(first and kg == 0), stop=(not first and kg == 1),
                )

        def travel(i, h, first=False):
            if first:
                u_bank[i, h] = bank(("u", i, h))
            cols = slice((i % 2) * P, (i % 2 + 1) * P)
            nc.tensor.matmul_mx(
                out=u_bank[i, h][:],
                lhsT=z_q[i // 2][:, cols].bitcast(FP8X4), lhsT_scale=z_s[i // 2][:, cols],
                rhs=w_q[h][:].bitcast(FP8X4), rhs_scale=w_s[h][:],
                start=first, stop=not first,
            )

        def attract(i, h):
            g, t = divmod(i, 4)
            if (g, h) not in p_raw:
                p_raw[g, h] = rotating("p_raw", [P, 4, HALF], BF16, 8)
            nc.scalar.activation(
                out=p_raw[g, h][:, t, :], in_=u_bank[i, h][:], func=ACT.Exp, bias=ln_a[:, i : i + 1], scale=1.0
            )
            release(("u", i, h))

        def utility(i, h):
            if i % 2 == 0:
                taste(i, h)
                travel(i, h)
            else:
                travel(i, h, True)
                taste(i, h, False)
            attract(i, h)

        def utilities(n):
            tiles = (2 * n, 2 * n + 1)
            for i in tiles:
                travel(i, 0, True)
            for i in tiles:
                taste(i, 0, False)
                attract(i, 0)
            for i in tiles:
                taste(i, 1)
            for i in tiles:
                travel(i, 1)
                attract(i, 1)

        def group_p(g, h, engine, c0=0, c1=HALF, room=None):
            if (g, h) not in p_grp:
                p_grp[g, h] = rotating("p_grp", [P, 4 * HALF], BF16, 3) if room is None else room
            group4(engine, p_grp[g, h][:].rearrange("p (n t) -> p n t", t=4)[:, c0:c1, :], p_raw[g, h][:, :, c0:c1])

        def quant_p(g, h):
            nc.vector.quantize_mx(out=p_q[g][h][:].bitcast(FP8X4), scales=p_s[g][h][:], in_=p_grp[g, h][:])

        def flow_pass(b, jt, g, c0, c1):
            h, c = divmod(jt, 4)
            cols = slice(c * P, (c + 1) * P)
            nc.tensor.matmul_mx(
                out=b,
                lhsT=p_q[g][h][:, cols].bitcast(FP8X4), lhsT_scale=p_s[g][h][:, cols],
                rhs=y_sb[:, g, 2 * c0 : 2 * c1].bitcast(FP4X4), rhs_scale=y_sc[:, C * g + c0 : C * g + c1],
                start=(g == 0), stop=(g == G - 1),
            )

        def flow_passes(jt, groups):
            for g in groups:
                if g == 0:
                    f_bank[jt] = bank(("f", jt))
                flow_pass(f_bank[jt][:], jt, g, 0, C)

        def store(engine, src, jt, c0, c1):
            o = kept("o_sb%d_%d" % (jt, c0), [P, c1 - c0], F32)
            factor = size_cols[:, jt : jt + 1]
            if engine == "s":
                nc.scalar.activation(out=o[:], in_=src, func=ACT.Copy, scale=factor)
            else:
                nc.vector.tensor_scalar(out=o[:], in0=src, scalar1=factor, scalar2=None, op0=ALU.mult)
            nc.sync.dma_start(out=out[jt * P : (jt + 1) * P, c0:c1], in_=o[:])

        def finish(jt, engine):
            store(engine, f_bank[jt][:], jt, 0, C)
            release(("f", jt))

        def flow_piece(jt, c0, c1, engine):
            b = bank(("f", jt, c0))
            for g in range(G):
                flow_pass(b[:, 0 : c1 - c0], jt, g, c0, c1)
            store(engine, b[:, 0 : c1 - c0], jt, c0, c1)
            release(("f", jt, c0))

        def share(g, h):
            return G_FIRST if (g, h) == (0, 0) else G_SHARE

        def keep_warm(count):
            b = bank("warm")
            for k in range(count):
                nc.tensor.matmul(out=b[:], lhsT=ones[:, 0:P], rhs=ones[:], start=True, stop=True)
            release("warm")

        nc.vector.memset(warm[:], 1.0)
        nc.vector.memset(ones[:], 1.0)
        nc.vector.memset(v_sc[:].bitcast(I32), 0)
        make_identity(nc, ident[:])
        nc.vector.memset(one[:], 1.0)
        load_x(0, 0, 1)
        load_xs()
        load_x(0, 1, 2)
        load_x(1)
        load_w(0)
        load_z(0)
        load_x(2)
        load_z(1)
        load_a()
        load_scales(v_sc, v_scales, 2)
        load_v(0)
        load_v(1)
        load_w(1)
        load_x(3)
        load_z(2)
        load_z(3)
        for n in range(4, PAIRS):
            load_x(n)
            load_z(n)
        nc.vector.memset(y_sc[:].bitcast(I32), 0)
        load_scales(y_sc, y_scales, G)
        nc.sync.dma_start(out=y_sb[:], in_=y_words.rearrange("g p n -> p g n"))
        with nc.allow_non_contiguous_dma(reason="one factor a partition for each tile of 128 stores"):
            nc.sync.dma_start(out=size_in[:, :, 0], in_=size.rearrange("(c p) -> p c", p=P))
        nc.scalar.activation(out=warm[:], in_=warm[:], func=ACT.Ln)
        keep_warm(3)
        for c in range(2):
            cast_apart(0, c, c + 1)
            turn_x_pass(0, c)
        cast_apart(1)
        cast_plain(2)
        cast_plain(3)
        keep_warm(1)
        turn_x(1)
        scale_x_pass(0, 0)
        scale_x_pass(0, 1)
        scale_x(1)
        turn_x(2)
        turn_x(3)
        keep_warm(1)
        turn_z(0)
        w_room = kept("w_room", [P, 4 * HALF], BF16)
        keep_warm(2)
        group_w("g", 0, 160, 512, w_room)
        group_w("s", 0, 0, 160)
        scale_x(2)
        cast_plain(4)
        cast_plain(5)
        empty_z(0)
        turn_z(1)
        turn_x(4)
        turn_x(5)
        empty_z(1)
        nc.scalar.activation(out=ln_a[:], in_=a_in[:].rearrange("p g t -> p (g t)"), func=ACT.Ln)
        nc.scalar.activation(out=warm[:], in_=warm[:], func=ACT.Exp)
        quant_w(0)
        quant_z(0)
        quant_x(0, 2)
        scale_x(3)
        travel(0, 0, True)
        travel(1, 0, True)
        quant_z(1)
        quant_x(2, 2)
        taste(0, 0, False)
        attract(0, 0)
        taste(1, 0, False)
        attract(1, 0)
        taste(0, 1)
        taste(1, 1)
        scale_x(4)
        scale_x(5)
        group_w("g", 1, 0, 416, room[1])
        group_w("s", 1, 416, 512)
        cast_plain(7)
        split_z(2, "s")
        utility(2, 0)
        utility(3, 0)
        cast_apart(6)
        split_z(3, "v")
        split_x(7)
        quant_w(1)
        taste(2, 1)
        taste(3, 1)
        turn_z(2)
        turn_x(6)
        turn_z(3)
        turn_x(7)
        empty_z(2)
        for i in range(4):
            travel(i, 1)
        quant_z(2)
        quant_x(4, 2)
        for n in range(2, 7):
            g, h = divmod(n - 2, 2)
            empty_z(n + 1)
            if n == 2:
                cast_plain(9)
                attract(0, 1)
                attract(1, 1)
                split_z(4, "s")
                attract(2, 1)
                attract(3, 1)
            scale_x(2 * n + 2)
            scale_x(2 * n + 3)
            group_p(g, h, "g", 0, share(g, h), room[n])
            if 2 < n < 6:
                cast_plain(2 * n + 5)
            if n < 6:
                cast_apart(2 * n + 4)
                split_x(2 * n + 5)
            if 2 < n < 6:
                split_z(n + 2, "s")
            quant_z(n + 1)
            quant_x(2 * n + 2, 2)
            if n == 6:
                group_p(0, 0, "s", share(0, 0), HALF)
                group_p(2, 0, "s", share(2, 0), HALF)
            utilities(n)
            if n < 6:
                turn_x(2 * n + 4)
                turn_x(2 * n + 5)
                turn_z(n + 2)
        nc.vector.tensor_copy(out=size_cols[:], in_=size_in[:, :, 0])
        group_p(1, 0, "v", share(1, 0), HALF)
        for g in range(3):
            quant_p(g, 0)
        for g in range(2):
            group_p(g, 1, "v", share(g, 1), HALF)
        for h in range(2):
            for i in (14, 15):
                travel(i, h, True)
            for i in (14, 15):
                taste(i, h, False)
                attract(i, h)
        group_p(2, 1, "s")
        quant_p(0, 1)
        group_p(3, 0, "v")
        quant_p(1, 1)
        quant_p(3, 0)
        group_p(3, 1, "v")
        quant_p(2, 1)
        quant_p(3, 1)
        for g in range(G):
            for jt in range(4):
                flow_passes(jt, [g])
                if g == G - 1:
                    finish(jt, "s")
        for g in range(G):
            for jt in (4, 5):
                flow_passes(jt, [g])
                if g == G - 1:
                    finish(jt, "s" if jt == 4 else "v")
        flow_passes(6, range(G))
        finish(6, "s")
        flow_piece(7, 0, 256, "s")
        flow_piece(7, 256, 512, "v")
